import numpy as np, ml_dtypes
CORES = [24,25,26,27,28,29,30,31]
N = 8
BF = ml_dtypes.bfloat16
W, L, RO, SH = 4096, 192, 10, (1, 3)
KK = np.arange(16, dtype=np.int32).reshape(1, 1, 16, 1)
REC = np.array([0.3, 0.0, 1.0, 0.5, 1.0, 0.3, 1.0, 1.0]).reshape(1, 8, 1, 1)
def spans(rng, kind):
    p = np.argsort(rng.random((N, 8, 16, L)), axis=2).astype(np.float64); x = rng.random((N, 8, 16, L)); t = rng.random((N, 8, 16, L))
    s = np.exp2(-rng.integers(0, 6, (N, 8, 1, L)).astype(np.float64))
    c = np.where((kind == 1) | (kind == 3), p, x)
    dur = np.where(kind == 1, 0.5, np.where(kind == 2, 1.0 + t, np.where(kind == 3, 31.0 - 2.0 * p, t * s)))
    pos = np.argsort(np.argsort(np.concatenate([c, c + dur], axis=2), axis=2, kind="stable"), axis=2)
    return pos[:, :, :16], pos[:, :, 16:]
def kinds(rng):
    return rng.choice(np.array([0, 0, 0, 0, 1, 2, 3]), (N, 8, 1, L))
def parts(rng):
    xt = np.floor(rng.random((N, 8, 16, W)) * rng.choice(np.array([12, 24, 40, 64]), (N, 8, 1, W))).astype(np.int64)
    vt = rng.integers(0, 64, (N, 8, 16, W))
    z0 = np.floor(rng.random((N, 8, 16, L)) * rng.choice(np.array([16, 32, 64]), (N, 8, 1, L))).astype(np.int64)
    nm = rng.integers(0, 4096, (N, 8, 16, L)); wt = rng.integers(0, 4096, (N, 8, 16))
    th = rng.integers(150, 330, (N, 8, 1)) + rng.integers(-60, 61, (N, 8, 16))
    th[np.arange(N), rng.integers(0, 8, N)] = rng.integers(0, 30, (N, 16))
    return xt, vt, z0, nm, wt, th
def aim(c):
    return (c - 37 * KK) & 4095
def few(a):
    return np.ascontiguousarray(np.reshape(a, (N, 128, -1))).astype(np.float32).astype(BF)
def big(a):
    return np.ascontiguousarray(np.reshape(a, (N, 128, -1))).astype(np.int32)
def pack(xt, vt, z0, nm, ca, rt, wt, th):
    return {"xt": few(xt), "vt": few(vt), "z0": few(z0), "nm": big(nm), "ca": few(ca), "rt": few(rt), "wt": big(wt), "th": big(th)}
def setup_inputs(rng):
    xt, vt, z0, nm, wt, th = parts(rng); ca, rt = spans(rng, kinds(rng))
    return pack(xt, vt, z0, nm, ca, rt, wt, th)
def uneven(rng, bits, *shape):
    return np.minimum(np.floor(np.exp2(bits * rng.random(shape))), 2 ** bits).astype(np.int64) - 1
def sized(rng, n):
    a = np.minimum(np.floor(np.exp2(6.0 * rng.random((N, 8, 1, n))) * rng.random((N, 8, 16, n))), 63).astype(np.int64)
    return np.where(rng.random((N, 8, 1, n)) < 0.5, a, 63 - a)
def setup_inputs_spread(rng):
    ca, rt = spans(rng, kinds(rng))
    return pack(sized(rng, W), sized(rng, W), sized(rng, L), uneven(rng, 12, N, 8, 16, L), ca, rt, uneven(rng, 12, N, 8, 16), np.minimum(uneven(rng, 10, N, 8, 16), 1007))
def tips(rng, n):
    return np.where(rng.random((N, 8, 1, n)) < REC, 63 * rng.integers(0, 2, (N, 8, 1, n)), 63 * rng.integers(0, 2, (N, 8, 16, n)))
def setup_inputs_ends(rng):
    xt, vt, z0 = tips(rng, W), tips(rng, W), tips(rng, L)
    nm = 4095 * rng.integers(0, 2, (N, 8, 16, L)); wt = 4095 * rng.integers(0, 2, (N, 8, 16)); th = 1007 * rng.integers(0, 2, (N, 8, 16))
    th[:, :, 0] = 0; th[:, :, 15] = 1007
    us = np.arange(W); hit = np.flatnonzero((((us * us) >> 5) + 37 * us + 613) & (W - 1) == W - 1)
    one = 65 if len(hit) == 0 else (-65 * int(hit[rng.integers(0, len(hit))])) & 4095
    wt[:, 0] = 4095; wt[:, 6:] = 0; wt[:, 7, 15] = 65; wt[:, 6, 15] = one
    last = np.array([0, 1, 6, L - 2, L - 1])
    z0[:, 0][..., last] = 63; z0[:, 7][..., last] = 63; nm[:, 7][..., last] = 4095
    ca, rt = spans(rng, rng.choice(np.array([1, 2, 3]), (N, 8, 1, L)))
    return pack(xt, vt, z0, nm, ca, rt, wt, th)
def setup_inputs_corners(rng):
    xt, vt, z0, nm, wt, th = parts(rng); H = W // 2
    hi = rng.integers(0, 64, (N, 4, 16, H)) * (rng.random((N, 4, 1, H)) < 0.5); hi[:, :, :8] = 63; hi[:, :, 8] = 0
    lo = np.where(rng.random((N, 4, 1, H)) < 0.5, 63, rng.integers(0, 64, (N, 4, 16, H))); lo[:, :, :9] = 0
    xt[:, :4, :, :H] = hi; xt[:, :4, :, H:] = lo; z0[:, :4] = rng.integers(1, 63, (N, 4, 16, L)); wt[:, :4] = 0; th[:, :4] = 0
    kind = kinds(rng); kind[:, :4] = rng.choice(np.array([1, 2, 2, 3]), (N, 4, 1, L)); kind[:, 4] = 1; kind[:, 5] = 2; kind[:, 6] = 3
    ca, rt = spans(rng, kind)
    many = rng.choice(np.array([0, 1, RO // 2, RO - 2, RO - 1, 16]), (N, 8, 1, L)); many[:, 1] = rng.integers(0, 2, (N, 1, L)); many[:, 2] = RO // 2; many[:, 3] = 16
    many[:, 0, :, L - 1] = RO - 2
    order = np.argsort(np.argsort(ca, axis=2), axis=2)
    c = np.where(order < many, rng.integers(0, H - 32, (N, 8, 16, L)), rng.integers(H, W - 32, (N, 8, 16, L)))
    nm[:, :4] = aim(c)[:, :4]
    wt[:, 4] = 4095 * rng.integers(0, 2, (N, 16)); th[:, 4] = 0; th[:, 7] = np.where(rng.random((N, 16)) < 0.25, 1007, 0)
    return pack(xt, vt, z0, nm, ca, rt, wt, th)
def setup_inputs_crowd(rng):
    xt, vt, z0, nm, wt, th = parts(rng); Q = W // 4
    xt[..., :Q] = rng.integers(40, 64, (N, 8, 16, Q)); xt[..., Q:2 * Q] = rng.integers(24, 33, (N, 8, 16, Q)); xt[..., 2 * Q:] = 0
    z0 = rng.integers(1, 8, (N, 8, 16, L)); wt[:, 0::2] = 0; wt[:, 1::2] = W // 2
    xt[:, 1::2] = (xt[:, 1::2] >> 1) << 1; z0[:, 1::2] = np.maximum((z0[:, 1::2] >> 1) << 1, 2)
    vt[..., 613] = 0; th = rng.integers(0, 300, (N, 8, 16))
    ca, rt = spans(rng, kinds(rng)); first = ca == np.min(ca, axis=2, keepdims=True)
    low = rng.integers(2 * Q, W - 32, (N, 8, 16, L)); mid = rng.integers(Q, 2 * Q - 32, (N, 8, 16, L))
    c = np.where(first, rng.integers(0, Q - 32, (N, 8, 16, L)), np.where(rng.random((N, 8, 1, L)) < 0.5, mid, low))
    out = np.zeros((N, 8, 1, L), bool); out[1, 7, 0, L - 1] = True
    for q in range(2, N - 1):
        for g in range(1, 8, 2): out[q, g, 0, rng.integers(0, L)] = True
    nm = aim(np.where(out, low, c))
    e = N - 1; cols = np.arange(W)
    xt[e] = rng.integers(0, 64, (8, 16, W)); xt[e, :, 8:] = xt[e, :, 8:] >> 2; vt[e, :, 8:] = vt[e, :, 8:] >> 2
    z0[e, :, :8] = 0; z0[e, :, 8:] = rng.integers(50, 64, (8, 8, L)); th[e] = rng.integers(0, 100, (8, 16))
    wt[e, 0::2] = rng.integers(0, 4096, (4, 16)); nm[e, 0::2] = rng.integers(0, 4096, (4, 16, L))
    wt[e, 1::2] = 0; wt[e, 1::2, 0] = 1; wt[e, 1::2, 1] = 64
    xt[e, 1::2, 0] = cols & 63; xt[e, 1::2, 1] = cols >> 6; xt[e, 1::2, 2] = np.where(cols < 600, 0, rng.integers(1, 64, (4, W)))
    us = np.arange(600, W); us = us[np.unique(((us * us >> 5) + 37 * us) & (W - 1), return_index=True)[1]]
    for g in range(1, 8, 2): nm[e, g] = np.where(first[e, g], aim(np.resize(rng.permutation(us), L))[0, 0], 0)
    return pack(xt, vt, z0, nm, ca, rt, wt, th)
def setup_inputs_twins(rng):
    xt, vt, z0, nm, wt, th = parts(rng); B = W // 128
    b = np.floor(rng.random((1, 8, 16, B)) * rng.choice(np.array([12, 24, 40, 64]), (1, 8, 1, B))).astype(np.int64)
    xt = np.repeat(np.repeat(b, 128, axis=3), N, axis=0)
    a = rng.integers(0, 40, (1, 8, 16, L // 2)); z0 = np.repeat(np.concatenate([a, a], axis=3), N, axis=0)
    a = rng.integers(0, 4096, (1, 8, 16, L // 2)); nm = np.repeat(np.concatenate([a, a], axis=3), N, axis=0)
    wt = np.repeat(wt[:1], N, axis=0); th = rng.integers(0, 4, (N, 8, 16)); ca, rt = spans(rng, kinds(rng))
    return pack(xt, vt, z0, nm, ca, rt, wt, th)
def check_inputs(d):
    bad = []
    for k, lo, hi in (("xt", 0, 63), ("vt", 0, 63), ("z0", 0, 63), ("nm", 0, 4095), ("ca", 0, 30), ("rt", 1, 31), ("wt", 0, 4095), ("th", 0, 1007)):
        a = np.asarray(d[k]).astype(np.float64)
        if not np.all((a >= lo) & (a <= hi)): bad.append("range of " + k)
        elif not np.all(a == np.floor(a)): bad.append("whole numbers in " + k)
    c = np.asarray(d["ca"]).astype(np.float64).reshape(N, 8, 16, L); r = np.asarray(d["rt"]).astype(np.float64).reshape(N, 8, 16, L)
    if not np.all(c < r): bad.append("ca under rt")
    e = np.sort(np.concatenate([c, r], axis=2), axis=2)
    if not np.all(e[:, :, 1:] > e[:, :, :-1]): bad.append("positions of a lane distinct")
    return bad
def ints(a):
    return np.asarray(a).astype(np.float32).astype(np.int32)
def pick(t, ix):
    return np.stack([np.stack([np.take(t[q, g], ix[q, g], axis=1) for g in range(8)]) for q in range(N)])
def mark(x, w):
    return np.sum(x * w, axis=2, dtype=np.int32) & (W - 1)
def place(u, d):
    return ((u * u >> 5) + 37 * u + 613 * d) & (W - 1)
def reference(xt, vt, z0, nm, ca, rt, wt, th):
    X = ints(xt).reshape(N, 8, 16, W); V = ints(vt).reshape(N, 8, 16, W); z = ints(z0).reshape(N, 8, 16, L)
    n = nm.astype(np.int32).reshape(N, 8, 16, L); c = ints(ca).reshape(N, 8, 16, L); r = ints(rt).reshape(N, 8, 16, L)
    w = wt.astype(np.int32).reshape(N, 8, 16, 1); t = th.astype(np.int32).reshape(N, 8, 16, 1)
    lev = np.zeros((N, 8, 16, L), np.int32); dep = np.zeros((N, 8, L), np.int32); ptr = np.full((N, 8, L), -1, np.int32)
    stk = np.zeros((N, 8, 16, RO, L), np.int32); A = np.zeros((N, 1, 1, 1), np.int32); height = np.arange(RO).reshape(1, 1, 1, RO, 1)
    for step in range(RO):
        kap = np.min(np.where(lev > 0, 32, r), axis=2, keepdims=True)
        can = (lev == 0) & (c > ptr[:, :, None]) & (c < kap)
        uz = mark(z, w); zz = z[:, :, :, None]
        y = pick(X, ((n * uz[:, :, None] >> 5) + n + 37 * KK + A) & (W - 1))
        zk = np.abs(zz - y); rows = np.sum(y >= zz, axis=2, dtype=np.int32)
        v = pick(V, place(mark(zk, w[..., None]), dep[:, :, None] + 1))
        far = np.sum(np.abs(v - zk), axis=2, dtype=np.int32)
        key = np.where(can & (rows >= 8) & (far > t), c, 32)
        k = np.argmin(key, axis=2); push = np.min(key, axis=2) < 32; pop = ~push & (dep > 0)
        at = place(uz, dep); wins = {}
        for q in range(N):
            for g in range(8):
                i = np.flatnonzero(pop[q, g]); p, f = np.unique(at[q, g, i], return_index=True)
                wins[q, g] = (p, z[q, g][:, i[f]])
        for d in (0,) + SH:
            for q in range(N):
                for g in range(8):
                    V[(q + d) % N, g][:, wins[q, g][0]] = wins[q, g][1]
        old = np.take_along_axis(stk, np.maximum(dep - 1, 0)[:, :, None, None, :], axis=3)[:, :, :, 0]
        new = np.take_along_axis(zk, k[:, :, None, None, :], axis=3)[:, :, :, 0]
        stk = np.where(push[:, :, None, None, :] & (dep[:, :, None, None, :] == height), zz, stk)
        P, O, D = push[:, :, None], pop[:, :, None], dep[:, :, None]
        top = O & (lev == D)
        ptr = np.where(pop, np.sum(np.where(top, c, 0), axis=2, dtype=np.int32), -1)
        lev = np.where(P & (KK == k[:, :, None]), D + 1, np.where(top, 0, lev))
        z = np.where(P, new, np.where(O, old, 63 - z))
        dep = dep + push.astype(np.int32) - pop.astype(np.int32)
        A = (np.sum(pop, axis=(1, 2)) & 31).reshape(N, 1, 1, 1)
    return {"yv": V.reshape(N, 128, W).astype(np.float32).astype(BF), "yz": z.reshape(N, 128, L).astype(np.float32).astype(BF),
            "yl": lev.reshape(N, 128, L).astype(np.float32).astype(BF), "yp": ptr.astype(np.float32)}

@@ -1,0 +1,763 @@
+from concourse.bass import DstId, RemoteDMATransfer
+from concourse.mybir import AluOpType as A, AxisListType, ActivationFunctionType as F
+
+L, W, RO = 192, 4096, 10
+CFG = {
+    "XG": ["AA", "A", "A"],
+    "XP": "RRS",
+    "VG": ["A", "A", "D"],
+    "sq": True, "brow": False, "rtp": True, "tiny": True, "zg": False, "pvp": False, "dupa": False, "pbm": False, "xs": [(0, 64), (64, 192)],
+}
+FP16W = True
+f32, bf, i32, u16 = "float32", "bfloat16", "int32", "uint16"
+
+
+def _sb(n, d):
+    return ("sbuf", [128] + (list(n) if isinstance(n, tuple) else [n]), d)
+
+
+SCRATCH = {
+    "X": _sb(2 * W + 32, bf), "V": _sb(W + L, bf), "ZW": _sb(32 * L, bf),
+    "Y": _sb(3072, bf), "S": _sb(3072, bf), "E": _sb(3072, bf), "AE": _sb(3072, bf),
+    "nmi": _sb((6, 2, 16), i32), "cai": _sb((6, 2, 16), bf), "rti": _sb((6, 2, 16), bf), "wti": _sb(1, i32), "thi": _sb(1, i32),
+    "src4": _sb((4, 6, 2, 16), f32), "tr": _sb(4 * L, f32),
+    "nB": _sb(L, f32), "ca1": _sb(L, f32), "rtB": _sb(L, f32), "thB": _sb(L, f32), "KS": _sb(L, f32),
+    "k37": _sb(L, f32), "kk": _sb(L, f32), "t192": _sb(L, f32), "i192": _sb(L, i32), "j192": _sb(L, i32),
+    "one": _sb(160, f32), "IW": _sb(160, f32), "IW0": _sb(160, f32), "IW1": _sb(160, f32),
+    "Ib": _sb(128, bf), "nIb": _sb(128, bf), "pIb": _sb(128, bf), "NI": _sb(128, bf), "thh": _sb(L, "float16"), "Ph": _sb(L, "float16"), "I8k": _sb(128, f32),
+    "BO": _sb(128, f32), "BOb": _sb(128, bf), "B8": _sb(8, f32), "B8a": _sb(8, f32),
+    "G": _sb(144, bf), "Gn": _sb(144, bf), "GB2": _sb(144, bf), "GBn": _sb(144, bf), "G8k": _sb(144, bf),
+    "Wh": _sb(144, "float16" if FP16W else bf), "Wl": _sb(144, bf), "LT": _sb((16, 128), bf), "RT": _sb((16, 128), bf),
+    "DM": _sb(L, f32), "pi": _sb(1, i32), "pj": _sb(1, i32), "PM": _sb(1, f32), "hf": _sb(2, f32), "wf": _sb(4, f32), "wi": _sb(2, i32),
+    "thf": _sb(1, f32), "C63": _sb(1, f32), "ltm": _sb(16, f32),
+    "c16": _sb(12, f32), "c1": _sb(12, f32), "LL": _sb(12, f32), "DUM": _sb(12, f32), "KQ": _sb(12, i32), "QF": _sb(12, f32), "t12": _sb(12, f32),
+    "QL": _sb(12, u16), "DL": _sb(6, u16), "EL": _sb(12, u16), "PERM": _sb(12, u16), "INV": _sb(12, u16),
+    "U": _sb(16 * (RO + 1), i32), "xi": _sb(L, u16), "nu": _sb(L, i32), "sh": _sb(L, i32), "t3": _sb(L, f32),
+    "ui": _sb(L, i32), "uk": _sb(L, i32), "v": _sb(208, f32), "sq": _sb(208, f32), "tp": _sb(208, i32), "h": _sb(208, i32), "vi": _sb(208, u16),
+    "K1": _sb(L, f32), "key": _sb(L, f32), "brow": _sb(L, bf), "bad1": _sb(L, bf), "bad2": _sb(L, bf),
+    "PV": _sb(L, f32), "PVh": _sb(96, f32), "R": _sb(96, f32), "m96": _sb(96, f32), "m48": _sb(48, f32), "m24": _sb(24, f32), "fin": _sb(12, i32),
+    "RL": _sb(L, f32), "n96": _sb(96, f32), "n48": _sb(48, f32), "n24": _sb(24, f32), "Km": _sb(16, f32),
+    "sel": _sb(L, f32), "dsel": _sb(L, f32), "D": _sb(24, f32), "e": _sb(12, f32), "thr": _sb(12, f32),
+    "sm": _sb(16 * 24, f32), "si": _sb(16 * 6, i32), "popb": _sb(16, f32), "xa": _sb(2, f32), "zo": _sb(12, u16),
+    "P8": _sb(16, f32), "Pm": _sb(L, f32), "Pb": _sb(L, "float16"), "EQ": _sb((12, 208), bf), "dupb": _sb(L, bf),
+    "so": _sb(16 * RO, u16), "rz": _sb(2 * RO * L, bf), "ro": _sb(2 * RO * 16, u16),
+    "ol": _sb((6, 2, 16), bf), "op": _sb(L, f32),
+    "dA": ("psum", [128, 1024], f32), "dB": ("psum", [128, 1024], f32),
+    "uA": ("psum", [128, 512], f32), "uB": ("psum", [128, 512], f32), "uC": ("psum", [128, 512], f32), "mP": ("psum", [128, 512], f32),
+}
+NDMA = 16
+SEMAPHORES = ["dve", "act", "pe", "pool", "sent"] + ["d%d" % i for i in range(NDMA)] + ["r%d_%d" % (s, j) for s in range(1, RO) for j in range(2)]
+
+CY, PC, GA, SC, HOP = 1.04, 0.52, 1.56, 3.8, 100.0
+
+
+def build(T, topo, core, rank):
+    ops, lastw, readers, bank, step = [], {}, {}, {}, [-1]
+
+    def kind(ts_):
+        x = ts_[0] if ts_ else ""
+        if x[:2] in ("dA", "dB") and len(x) == 3:
+            return "d"
+        y = x.rstrip("0123456789")
+        return y if y in ("U", "z", "so") else x
+
+    def add(eng, fn, cost, r=(), w=(), px=(), lat=0.0, ext=(), soft=(), dma=False):
+        i = len(ops)
+        deps = set()
+        for t in r:
+            if t in lastw:
+                deps.add(lastw[t])
+        for t in w:
+            if t in lastw:
+                deps.add(lastw[t])
+            deps.update(readers.get(t, ()))
+        for t in r:
+            readers.setdefault(t, []).append(i)
+        for t in w:
+            lastw[t] = i
+            readers[t] = []
+        for b in px:
+            who, cur, prev = bank.get(b, (None, [], []))
+            if who != eng:
+                prev, cur = cur, []
+            deps.update(prev)
+            bank[b] = (eng, cur + [i], prev)
+        deps.discard(i)
+        ops.append(dict(eng=eng, fn=fn, cost=cost, deps=deps, lat=lat, ext=list(ext), soft=list(soft), dma=dma, step=step[0],
+                        cls=eng[0] + kind(w[:1]) + "." + kind(r[-1:])))
+        return i
+
+    def n_of(ap):
+        n = 1
+        for x in ap.shape[1:]:
+            n *= x
+        return n
+
+    def vcost(n, c):
+        return max(64, n * c) * CY
+
+    def ts(out, in0, s1, s2, o0, o1, r, w, c=1.0, px=()):
+        if s2 is None:
+            fn = lambda g: g.vector.tensor_scalar(out, in0, s1, None, o0)
+        else:
+            fn = lambda g: g.vector.tensor_scalar(out, in0, s1, s2, o0, o1)
+        return add("dve", fn, vcost(n_of(out), c), r, w, px)
+
+    def tt(out, a, b, o, r, w, px=()):
+        return add("dve", lambda g: g.vector.tensor_tensor(out, a, b, o), vcost(n_of(out), 1.0 if px else 2.0), r, w, px)
+
+    def cp(out, a, r, w, c=1.0, px=()):
+        return add("dve", lambda g: g.vector.tensor_copy(out, a), vcost(n_of(out), c), r, w, px)
+
+    def gt(out, win, off, b, o, r, w):
+        if b is None:
+            fn = lambda g: g.vector.tensor_copy(out, win.indirect(off))
+        else:
+            fn = lambda g: g.vector.tensor_tensor(out, win.indirect(off), b, o)
+        return add("dve", fn, (50 / 0.83 + n_of(out) * GA) * CY, r, w)
+
+    def ag(out, win, off, r, w):
+        return add("act", lambda g: g.scalar.activation(out, win.indirect(off), F.Copy), (65 / 0.83 + n_of(out) * GA) * CY, r, w)
+
+    def ms(ap, val, w):
+        return add("dve", lambda g: g.vector.memset(ap, val), vcost(n_of(ap), 0.5), (), w)
+
+    def ac(out, a, func, r, w, bias=0.0, scale=1.0, px=()):
+        return add("act", lambda g: g.scalar.activation(out, a, func, bias=bias, scale=scale), max(64, n_of(out)) * CY + 40, r, w, px)
+
+    def mm(lst, r, w, px):
+        def fn(g):
+            for (o, a, b, st, sp, sl) in lst:
+                x = g.tensor.matmul(o, a, b, st, sp)
+            return x
+        return add("pe", fn, sum(max(64, n_of(x[2])) * (4 if x[5] else 1) for x in lst) * PC, r, w, px)
+
+    def grp(items):
+        return [(o, a, b, i == 0, i == len(items) - 1, sl) for i, (o, a, b, sl) in enumerate(items)]
+
+    def dma(q, out, a, nbytes, r, w):
+        fn = (lambda g: g.sync.dma_start(out, a)) if q == "sp" else (lambda g: g.scalar.dma_start(out, a))
+        return add(q, fn, 60.0, r, w, lat=2000.0 + nbytes / 200.0, dma=True)
+
+    def io(out, pat, base, cm, w, fl=True):
+        if fl:
+            fn = lambda g: g.iota(out, pat, base, cm, allow_small_or_imprecise_dtypes=True)
+        else:
+            fn = lambda g: g.iota(out, pat, base, cm)
+        return add("pool", fn, 130 + 2 * n_of(out) * CY, (), w)
+
+    def af(out, a, pat, op, base, cm, r, w):
+        return add("pool", lambda g: g.affine_select(out, a, pat, op, 0.0, base, cm), 170 + 2 * n_of(out) * CY, r, w)
+
+    def sl(m):
+        return slice(15 - m, 143 - m)
+
+    def zs(k):
+        return T.ZW[:, k * L:(k + 1) * L]
+
+    def sm(i):
+        return T.sm[:, 16 * i:16 * i + 12]
+
+    def si(i):
+        return T.si[:, 16 * i:16 * i + 12]
+
+    UB = [(T.uA, "uA"), (T.uB, "uB"), (T.uC, "uC")]
+    DB = [(T.dA, ("dA0", "dA1")), (T.dB, ("dB0", "dB1"))]
+    n37 = T.uC[:, 320:512]
+    M23, M28 = 1.5 * 2.0 ** 23, 1.5 * 2.0 ** 28
+    BIG = 2.0 ** 24
+
+    dma("sp", T.X[:, 0:W], T.xt[:], 1 << 20, (), ["X0"])
+    dma("act", T.nmi[:], T.nm[:], 98304, (), ["nmi"])
+    dma("act", zs(21), T.z0[:], 49152, (), ["z0"])
+    dma("act", T.wti[:], T.wt[:], 512, (), ["wti"])
+    dma("act", T.cai[:], T.ca[:], 49152, (), ["cai"])
+    dma("act", T.rti[:], T.rt[:], 49152, (), ["rti"])
+    dma("act", T.thi[:], T.th[:], 512, (), ["thi"])
+    dma("sp", T.V[:, 0:W], T.vt[:], 2 << 20, (), ["V"])
+    dma("sp", T.X[:, W:2 * W], T.xt[:], 3 << 20, (), ["X1"])
+    dma("sp", T.X[:, 2 * W:2 * W + 32], T.xt[:, 0:32], 3 << 20, (), ["X2"])
+
+    io(T.pi[:], [[0, 1]], 0, 1, ["pi"], fl=False)
+    ms(T.one[:], 1.0, ["one"])
+    af(T.IW[:], T.one[:], [[-1, 160]], A.is_equal, 16, 1, ["one"], ["IW"])
+    af(T.B8a[:], T.one[:, 0:8], [[-16, 8]], A.is_ge, 0, 1, ["one"], ["B8a"])
+    af(T.B8[:], T.B8a[:], [[16, 8]], A.is_ge, 15, -1, ["B8a"], ["B8"])
+    io(T.c1[:], [[1, 12]], 0, 0, ["c1"])
+    io(T.c16[:], [[16, 12]], 0, 0, ["c16"])
+    io(T.k37[:], [[37, 16], [0, 12]], 0, 0, ["k37"])
+    io(T.kk[:], [[4096, 16], [0, 12]], 0, 0, ["kk"])
+    io(T.DM[:], [[0, 12], [1, 16]], 0, 0, ["DM"])
+    io(T.ltm[:], [[1, 16]], 0, 0, ["ltm"])
+    ts(T.pj[:], T.pi[:], 15, None, A.bitwise_and, None, ["pi"], ["pj"])
+    cp(T.PM[:], T.pj[:], ["pj"], ["PM"])
+    ts(T.pj[:], T.pi[:], 4, 1, A.arith_shift_right, A.bitwise_and, ["pi"], ["pj"])
+    cp(T.hf[:, 1:2], T.pj[:], ["pj"], ["hf1"])
+    ts(T.hf[:, 0:1], T.hf[:, 1:2], -1.0, 1.0, A.mult, A.add, ["hf1"], ["hf0"])
+    ts(T.IW0[:], T.IW[:], T.hf[:, 0:1], None, A.mult, None, ["IW", "hf0"], ["IW0"])
+    ts(T.IW1[:], T.IW[:], T.hf[:, 1:2], None, A.mult, None, ["IW", "hf1"], ["IW1"])
+    ms(T.G[:], 0.0, ["G"])
+    cp(T.G[:, 15:143:16], T.B8[:], ["B8"], ["G"])
+    if FP16W:
+        ts(T.wf[:, 0:1], T.wti[:], 2048.0, -4096.0, A.is_ge, A.mult, ["wti"], ["wf0"])
+        tt(T.wf[:, 1:2], T.wf[:, 0:1], T.wti[:], A.add, ["wf0", "wti"], ["wf1"])
+        ts(T.Wh[:], T.G[:], T.wf[:, 1:2], None, A.mult, None, ["G", "wf1"], ["Wh"], 0.5)
+        WS = [T.Wh]
+    else:
+        ts(T.wi[:, 0:1], T.wti[:], 4032, None, A.bitwise_and, None, ["wti"], ["wi0"])
+        ts(T.wi[:, 1:2], T.wti[:], 63, None, A.bitwise_and, None, ["wti"], ["wi1"])
+        cp(T.wf[:, 0:2], T.wi[:], ["wi0", "wi1"], ["wf0"])
+        ts(T.Wh[:], T.G[:], T.wf[:, 0:1], None, A.mult, None, ["G", "wf0"], ["Wh"], 0.5)
+        ts(T.Wl[:], T.G[:], T.wf[:, 1:2], None, A.mult, None, ["G", "wf0"], ["Wl"], 0.5)
+        WS = [T.Wh, T.Wl]
+    z0 = zs(21)
+    mm(grp([(T.uA[:, 0:12], Wm[:, sl(m)], T.ZW[:, 21 * L + m:22 * L:16], False) for m in range(16) for Wm in WS]), ["Wh", "Wl", "z0"], ["uAu"], ["uA"])
+    cp(si(0), T.uA[:, 0:12], ["uAu"], ["si0"], px=["uA"])
+    ts(T.U[:, 0:12], si(0), 4095, None, A.bitwise_and, None, ["si0"], ["U0"])
+    ts(T.LL[:], T.c16[:], T.PM[:], None, A.add, None, ["c16", "PM"], ["LL"])
+    ts(T.KQ[:], T.LL[:], -5.5, 1.0 / 12, A.add, A.mult, ["LL"], ["KQ"])
+    ts(T.t12[:], T.KQ[:], -12.0, None, A.mult, None, ["KQ"], ["t12"])
+    tt(T.QF[:], T.t12[:], T.LL[:], A.add, ["t12", "LL"], ["QF"])
+    cp(T.QL[:], T.QF[:], ["QF"], ["QL"])
+    ts(T.t12[:], T.QF[:], 16.0, None, A.mult, None, ["QF"], ["t12"])
+    tt(T.t12[:], T.t12[:], T.KQ[:], A.add, ["t12", "KQ"], ["t12"])
+    cp(T.PERM[:], T.t12[:], ["t12"], ["PERM"])
+    IWS = [T.IW0, T.IW1]
+
+    def swap3(dst3, src4):
+        out = []
+        for rho in range(2):
+            out += grp([(dst3(rho), IWS[rho][:, 16 - 16 * (ga - rho):144 - 16 * (ga - rho)], src4(ga), True) for ga in range(2)])
+        return out
+
+    srcs = [(T.nmi, "nmi", T.nB, "nB"), (T.cai, "cai", T.ca1, "ca1"), (T.rti, "rti", T.rtB, "rtB"), (None, "thf", T.thB, "thB")]
+    cp(T.thf[:], T.thi[:], ["thi"], ["thf"])
+    for a, (s, sn, d, dn) in enumerate(srcs):
+        s4 = T.src4[:, a]
+        if a == 0:
+            cp(s4, s[:], [sn], ["s4%d" % a])
+        elif a == 1:
+            ac(s4, s[:], F.Identity, [sn, "one"], ["s4%d" % a], bias=T.one[:, 0:1])
+        elif a == 2:
+            ac(s4, s[:], F.Copy, [sn], ["s4%d" % a])
+        else:
+            ac(s4, T.cai[:], F.Identity, [sn, "cai"], ["s4%d" % a], bias=T.thf[:], scale=0.0)
+        P, bk = DB[a // 2]
+        c0 = 512 * (a % 2)
+        b1 = [bk[a % 2]]
+        lst = swap3(lambda rho: P[:, c0 + 96 * rho:c0 + 96 * rho + 96], lambda ga: T.src4[:, a, :, ga, :])
+        mm(lst, ["IW0", "IW1", "s4%d" % a], ["p4%d" % a], b1)
+        for rho in range(2):
+            ac(T.src4[:, a, :, rho, :], P[:, c0 + 96 * rho:c0 + 96 * rho + 96], F.Copy, ["p4%d" % a], ["s4%d" % a], px=b1)
+        add("dve", lambda g, a=a: g.vector.transpose(T.tr[:, a * L:(a + 1) * L], T.src4[:, a]), vcost(L, 1), ["s4%d" % a], ["tr%d" % a])
+        gt(d[:], T.tr[:, a * L:(a + 1) * L], T.PERM[:], None, None, ["tr%d" % a, "PERM"], [dn])
+        if a == 0:
+            tt(T.i192[:], T.nB[:], T.k37[:], A.add, ["nB", "k37"], ["i192"])
+            ts(T.j192[:], T.i192[:], 4095, None, A.bitwise_and, None, ["i192"], ["j192"])
+    ts(n37, T.j192[:], 15.5, None, A.add, None, ["j192"], ["n37"], px=["uC"])
+    cp(T.Ib[:], T.IW[:, 16:144], ["IW"], ["Ib"])
+    ts(T.nIb[:], T.IW[:, 16:144], -1.0, None, A.mult, None, ["IW"], ["nIb"])
+    ts(T.Gn[:], T.G[:], -1.0, None, A.mult, None, ["G"], ["Gn"], 0.5)
+    ts(T.DL[:, 0:1], T.PM[:], 11.0, 12.0, A.min, A.add, ["PM"], ["DL0"])
+    cp(T.DL[:, 1:5], T.QF[:, 0:4], ["QF"], ["DL1"])
+    ms(T.v[:, 12:16], 0.0, ["vpad"])
+    ts(T.t192[:], T.ca1[:], -131072.0, 128.0 * 131072, A.mult, A.add, ["ca1"], ["t192"])
+    tt(T.KS[:], T.t192[:], T.kk[:], A.add, ["t192", "kk"], ["KS"])
+    for t in range(3):
+        cp(UB[t][0][:, 128:192], T.KS[:, 64 * t:64 * t + 64], ["KS"], ["KS%d" % t], px=[UB[t][1]])
+    if CFG["rtp"] and not CFG["pvp"]:
+        cp(T.uB[:, 320:512], T.rtB[:], ["rtB"], ["rtP"], px=["uB"])
+    ac(T.pIb[:], T.IW[:, 16:144], F.Copy, ["IW"], ["pIb"], scale=-1024.0 * BIG)
+    ac(T.NI[:], T.IW[:, 16:144], F.Copy, ["IW"], ["NI"], scale=-BIG)
+    ac(T.I8k[:], T.IW[:, 16:144], F.Copy, ["IW"], ["I8k"], scale=-8192.0)
+    ac(T.GB2[:], T.G[:], F.Copy, ["G"], ["GB2"], scale=2 * BIG)
+    ac(T.GBn[:], T.G[:], F.Copy, ["G"], ["GBn"], scale=-BIG)
+    ac(T.G8k[:], T.G[:], F.Copy, ["G"], ["G8k"], scale=8192.0)
+    af(T.BO[:], T.one[:, 0:128], [[-16, 8], [0, 16]], A.is_ge, 0, 1, ["one"], ["BO"])
+    af(T.BO[:], T.BO[:], [[16, 8], [0, 16]], A.is_ge, 15, -1, ["BO"], ["BO"])
+    ac(T.BOb[:], T.BO[:], F.Copy, ["BO"], ["BOb"])
+    ms(T.ZW[:, 16 * L:20 * L], 0.0, ["zpad"])
+    ms(T.V[:, W:W + L], 0.0, ["Vpad"])
+    cp(T.PV[:], T.ca1[:], ["ca1"], ["PV"])
+    cp(T.thh[:], T.thB[:], ["thB"], ["thh"])
+    ms(T.e[:], 0.0, ["e"])
+    ms(sm(0), 0.0, ["ptr1"])
+    ms(T.popb[:, 12:13], -15.5 / 128, ["popc"])
+    ts(T.DM[:], T.DM[:], T.PM[:], None, A.is_equal, None, ["DM", "PM"], ["DM"])
+    ts(T.ltm[:], T.ltm[:], T.PM[:], 8192.0, A.is_gt, A.mult, ["ltm", "PM"], ["ltm"])
+    for m in range(1, 16):
+        ac(T.LT[:, m], T.G[:, sl(m)], F.Copy, ["G", "ltm"], ["LT%d" % m], scale=T.ltm[:, m:m + 1])
+    if CFG["pbm"]:
+        for m in range(16):
+            ac(T.RT[:, m], T.BO[:], F.Copy, ["BO", "DM"], ["RT%d" % m], scale=T.DM[:, m:m + 1])
+    cp(T.EL[:], T.c1[:], ["c1"], ["EL"])
+    ts(T.DUM[:], T.LL[:], W - 10240.0, None, A.add, None, ["LL"], ["DUM"])
+    ts(T.t12[:, 0:1], T.PM[:], 12.0, None, A.mult, None, ["PM"], ["t12"])
+    ts(T.INV[:], T.c1[:], T.t12[:, 0:1], None, A.add, None, ["c1", "t12"], ["INV"])
+    cp(T.wf[:, 2:3], T.wti[:], ["wti"], ["wf2"])
+    mm(grp([(T.mP[:, 400:401], T.BO[:], T.wf[:, 2:3], True)]), ["BO", "wf2"], ["cnt"], ["mP"])
+    ts(T.C63[:], T.mP[:, 400:401], 63.0, None, A.mult, None, ["cnt"], ["C63"], px=["mP"])
+
+    N = len(T.cores)
+    peers = [T.cores[(rank + d) % N] for d in (1, 3)]
+    halves = []
+    for j, p in enumerate(peers):
+        en = topo.engines(core, p)
+        h = len(en) // 2
+        halves.append(sum(1 << x for x in en[j * h:(j + 1) * h]))
+    neng = [bin(x).count("1") for x in halves]
+
+    def send(src, dst, s):
+        def fn(g):
+            trs = []
+            for j, p in enumerate(peers):
+                rid, pid, _se = topo.addr(p)
+                trs.append(RemoteDMATransfer(dst_ids=[DstId(rid=rid, pnc=pid)], dma_engine_mask=halves[j],
+                                             remote_sem=T.sem["r%d_%d" % (s, j)], src=src, dst=dst(j)))
+            g.remote_dma_fused(trs, local_sem=T.sem.sent)
+            return None
+        return fn
+
+    dn, later = [0], []
+    ptr1, npu = sm(0), sm(1)
+
+    def pieces(c0, n):
+        out = []
+        while n > 0:
+            k = min(n, L - c0 % L)
+            out.append((c0, k))
+            c0, n = c0 + k, n - k
+        return out
+
+    def units(c0, modes):
+        n = 1024 // len(modes)
+        return [(c0 + i * n, n, x) for i, x in enumerate(modes)]
+
+    def tk(name, u0, un):
+        return ["%s%d" % (name, x) for x in range(u0 // 512, (u0 + un) // 512)]
+
+    def tile(un):
+        if un == 1024:
+            dn[0] += dn[0] % 2
+        b = dn[0] % 4
+        dn[0] += un // 512
+        P, names = DB[b // 2]
+        return P, 512 * (b % 2), list(names[b % 2:b % 2 + un // 512])
+
+    def lin12(out, a, mul, c, r, w):
+        if CFG["tiny"]:
+            return ac(out, a, F.Identity, r, w, bias=c, scale=mul)
+        return ts(out, a, mul, c, A.mult, A.add, r, w)
+
+    for s in range(RO):
+        Uc, ut = T.U[:, 16 * s:16 * s + 12], "U%d" % s
+        z, zt = zs(21 + s), "z%d" % s
+        step[0] = s
+        for i, (a, b) in enumerate(CFG["xs"]):
+            nu, sh, xi = "nu%d" % i, "sh%d" % i, ["xi%d" % x for x in range(a // 32, b // 32)]
+            gt(T.nu[:, a:b], Uc, T.QL[:, a // 16:b // 16], T.nB[:, a:b], A.mult, [ut, "QL", "nB", nu], [nu])
+            ts(T.sh[:, a:b], T.nu[:, a:b], 5, 4095, A.arith_shift_right, A.bitwise_and, [nu], [sh])
+            if s == 0:
+                tt(T.nu[:, a:b], T.sh[:, a:b], T.j192[:, a:b], A.add, ["j192", sh], [nu])
+                ts(T.sh[:, a:b], T.nu[:, a:b], 4095, None, A.bitwise_and, None, [nu], [sh])
+                cp(T.xi[:, a:b], T.sh[:, a:b], [sh], xi)
+            else:
+                tt(T.t3[:, a:b], T.sh[:, a:b], T.uC[:, 320 + a:320 + b], A.add, ["n37", sh], ["t3%d" % i], px=["uC"])
+                ts(T.xi[:, a:b], T.t3[:, a:b], T.xa[:, 0:1], T.xa[:, 1:2], A.add, A.subtract, ["t3%d" % i, "xa0", "xa1"], xi)
+        Xw, xt_ = (T.X[:, 0:W], ["X0"]) if s == 0 else (T.X[:], ["X0", "X1", "X2"])
+        if later:
+            writes(*later.pop())
+        lin12(T.D[:, 0:12], T.e[:], 19616.0, 19616.0 * (s + 1) + 1336 * 32, ["e"], ["D0"])
+        lin12(T.D[:, 12:24], T.e[:], 19616.0, 19616.0 * s + 1336 * 32, ["e"], ["D1"])
+        ts(T.v[:, 0:12], Uc, 592.0, None, A.add, None, [ut], ["vown"])
+        if s > 0:
+            zsend = add("pool", send(z, lambda j, s=s: T.rz[:, (2 * s + j) * L:(2 * s + j + 1) * L], s), 1000.0, [zt], (), lat=2000.0)
+        for t in range(3):
+            c0, post = 1024 * t, CFG["XP"][t]
+            bs = slice(64 * t, 64 * t + 64)
+            if t == 1:
+                if CFG["pvp"] and s > 0:
+                    tt(T.RL[:], T.uB[:, 320:512], T.rtB[:], A.max, ["rtB", "PVp"], ["RL"], px=["uB"])
+                    tt(T.PVh[:], T.uB[:, 320:416], T.PV[:, 96:192], A.max, ["PV", "PVp"], ["PVh"], px=["uB"])
+                else:
+                    if CFG["rtp"] and not CFG["pvp"]:
+                        tt(T.RL[:], T.uB[:, 320:512], T.PV[:], A.max, ["rtP", "PV"], ["RL"], px=["uB"])
+                    else:
+                        tt(T.RL[:], T.rtB[:], T.PV[:], A.max, ["rtB", "PV"], ["RL"])
+                    if s > 0:
+                        tt(T.PVh[:], T.PV[:, 0:96], T.PV[:, 96:192], A.max, ["PV"], ["PVh"])
+            for (u0, un, mode) in units(c0, CFG["XG"][t]):
+                cs = slice(u0, u0 + un)
+                off = T.xi[:, u0 // 16:(u0 + un) // 16]
+                zk = T.ZW[:, cs]
+                if mode == "F":
+                    for (a, k) in pieces(u0, un):
+                        gt(T.Y[:, a:a + k], Xw, T.xi[:, a // 16:(a + k) // 16], T.ZW[:, (21 + s) * L + a % L:(21 + s) * L + a % L + k], A.subtract,
+                           xt_ + [zt] + tk("xi", u0, un), ["Y_%d" % a])
+                    yt = ["Y_%d" % a for (a, k) in pieces(u0, un)]
+                    src, px = T.Y[:, cs], ()
+                else:
+                    if mode == "A":
+                        ag(T.Y[:, cs], Xw, off, xt_ + tk("xi", u0, un), tk("Y", u0, un))
+                    else:
+                        gt(T.Y[:, cs], Xw, off, None, None, xt_ + tk("xi", u0, un), tk("Y", u0, un))
+                    P, p0, px = tile(un)
+                    lst = []
+                    for a0 in range(u0, u0 + un, 512):
+                        lst += grp([(P[:, p0 + a0 - u0:p0 + a0 - u0 + 512], T.Ib[:], T.Y[:, a0:a0 + 512], False)] +
+                                   [(P[:, p0 + a - u0:p0 + a - u0 + k], T.nIb[:], T.ZW[:, (21 + s) * L + a % L:(21 + s) * L + a % L + k], False) for (a, k) in pieces(a0, 512)])
+                    mm(lst, ["Ib", "nIb", zt] + tk("Y", u0, un), px, px)
+                    src, yt = P[:, p0:p0 + un], px
+                St, zkt = tk("S", u0, un), tk("zk", u0, un)
+                if post == "R":
+                    ac(T.S[:, cs], src, F.Abs, yt, St, bias=0.25, px=px)
+                    ts(zk, T.S[:, cs], M23, -M23, A.add, A.add, St, zkt, 0.5)
+                else:
+                    ac(zk, src, F.Abs, yt, zkt, px=px)
+                    if post == "S":
+                        ac(T.S[:, cs], src, F.Sign, yt, St, bias=0.5, px=px)
+                    else:
+                        ts(T.S[:, cs], src, 0.0, None, A.is_ge, None, yt, St, 1.0 if px else 0.5, px=px)
+            rows = [(T.G, T.S), (T.Gn, T.ZW)] if post == "R" else [(T.G, T.S)]
+            lim = 8.0 if post == "P" else 0.0
+            St, zkt = tk("S", c0, 1024), tk("zk", c0, 1024)
+            Pu, ub = UB[t]
+            mm(grp([(Pu[:, 0:64], Wm[:, sl(m)], T.ZW[:, c0 + m:c0 + 1024:16], False) for m in range(16) for Wm in WS]), ["Wh", "Wl"] + zkt, [ub + "u"], [ub])
+            cp(T.ui[:, bs], Pu[:, 0:64], [ub + "u"], ["ui%d" % t], px=[ub])
+            ts(T.uk[:, bs], T.ui[:, bs], 4095, None, A.bitwise_and, None, ["ui%d" % t], ["uk%d" % t])
+            ws = slice(16 + 64 * t, 80 + 64 * t)
+            ts(T.v[:, ws], T.uk[:, bs], 592.0, None, A.add, None, ["uk%d" % t], ["v%d" % t])
+            own = t == 0
+            if own:
+                ws = slice(0, 80)
+            rv = ["v%d" % t] + (["vown", "vpad"] if own else [])
+            if CFG["sq"]:
+                ac(T.sq[:, ws], T.v[:, ws], F.Square, rv, ["sq%d" % t])
+            else:
+                tt(T.sq[:, ws], T.v[:, ws], T.v[:, ws], A.mult, rv, ["sq%d" % t])
+            gt(T.tp[:, ws], T.D[:], T.DL[:, 0:5] if own else T.QL[:, 4 * t:4 * t + 4], T.sq[:, ws], A.add,
+               ["D0", "D1", "DL0", "DL1", "QL", "sq%d" % t], ["tp%d" % t])
+            ts(T.h[:, ws], T.tp[:, ws], 5, 4095, A.arith_shift_right, A.bitwise_and, ["tp%d" % t], ["h%d" % t])
+            cp(T.vi[:, ws], T.h[:, ws], ["h%d" % t], ["vi%d" % t])
+            full = grp([(Pu[:, 64:128], Gm[:, sl(m)], B[:, c0 + m:c0 + 1024:16], False) for (Gm, B) in rows for m in range(16)])
+            mm(full[:16], ["G", ub + "u"] + St, [ub + "r"], [ub])
+            if len(full) > 16:
+                mm(full[16:], ["Gn"] + zkt, [ub + "r"], [ub])
+            if CFG["brow"]:
+                ac(T.brow[:, bs], Pu[:, 64:128], F.Relu, [ub + "r"], ["brow%d" % t], bias=4.0 * lim, scale=-4.0, px=[ub])
+            else:
+                ts(T.brow[:, bs], Pu[:, 64:128], lim, None, A.is_lt, None, [ub + "r"], ["brow%d" % t], px=[ub])
+            tt(T.K1[:, bs], Pu[:, 128:192], T.uk[:, bs], A.add, ["KS%d" % t, "uk%d" % t], ["K1%d" % t], px=[ub])
+        tt(T.n96[:], T.RL[:, 0:96], T.RL[:, 96:192], A.min, ["RL"], ["n96"])
+        tt(T.n48[:], T.n96[:, 0:48], T.n96[:, 48:96], A.min, ["n96"], ["n48"])
+        tt(T.n24[:], T.n48[:, 0:24], T.n48[:, 24:48], A.min, ["n48"], ["n24"])
+        tt(T.Km[:, 0:12], T.n24[:, 0:12], T.n24[:, 12:24], A.min, ["n24"], ["Km"])
+        gt(T.bad2[:], T.Km[:, 0:12], T.QL[:], T.PV[:], A.is_lt, ["Km", "QL", "PV"], ["bad2"])
+        ts(si(1), Uc, -1.0, T.C63[:], A.mult, A.add, [ut, "C63"], ["si1"])
+        ts(si(2), si(1), 4095, None, A.bitwise_and, None, ["si1"], ["si2"])
+        ts(sm(20), si(2), 131072.0, None, A.add, None, ["si2"], ["fk"])
+        if s > 0:
+            gt(T.bad1[:], ptr1, T.QL[:], T.PV[:], A.is_ge, ["ptr1", "QL", "PV"], ["bad1"])
+            tt(T.PVh[:, 0:12], T.PVh[:, 0:12], sm(20), A.max, ["PVh", "fk"], ["PVh"])
+            ts(T.thr[:], T.e[:], float(-s), 96.0 * 131072, A.is_gt, A.mult, ["e"], ["thr"])
+            ts(T.P8[:, 0:12], T.h[:, 0:12], -2048.0, None, A.add, None, ["h0"], ["P8"])
+            if CFG["pbm"]:
+                ts(T.Ph[:, 0:12], T.h[:, 0:12], -2048.0, None, A.add, None, ["h0"], ["Pm"])
+                mm([(T.mP[:, m:192:16], T.RT[:, m], T.Ph[:, 0:12], True, True, False) for m in range(16)], ["RT%d" % m for m in range(16)] + ["Pm"], ["Pbc"], ["mP"])
+            else:
+                gt(T.Ph[:], T.P8[:, 0:12], T.EL[:], T.DM[:], A.mult, ["P8", "EL", "DM"], ["Pm"])
+                mm(grp([(T.mP[:, 0:192], T.BOb[:], T.Ph[:], False)]), ["BOb", "Pm"], ["Pbc"], ["mP"])
+            cp(T.Pb[:], T.mP[:, 0:192], ["Pbc"], ["Pb"], px=["mP"])
+        else:
+            ms(T.PVh[:], 0.0, ["PVh"])
+            cp(T.PVh[:, 0:12], sm(20), ["fk"], ["PVh"])
+        ac(zs(20), z, F.Identity, [zt], ["flip"], bias=63.0, scale=-1.0)
+        lin12(sm(2), T.e[:], 131072.0, 131072.0 * (2 + 10 * s), ["e"], ["P0a"])
+        tt(sm(3), sm(2), Uc, A.add, ["P0a", ut], ["P0"])
+        for t in range(3):
+            c0 = 1024 * t
+            bs = slice(64 * t, 64 * t + 64)
+            Vw = T.V[:, 0:W]
+            Pu, ub = UB[t]
+            o = Pu[:, 256:320]
+            pen = [(o, T.NI[:], T.thh[:, bs], False), (o, T.pIb[:], T.bad2[:, bs], False), (o, T.pIb[:], T.brow[:, bs], False)]
+            if s > 0:
+                pen += [(o, T.pIb[:], T.bad1[:, bs], False)]
+            lin = []
+            for (u0, un, mode) in units(c0, CFG["VG"][t]):
+                cs = slice(u0, u0 + un)
+                off = T.vi[:, 16 + u0 // 16:16 + (u0 + un) // 16]
+                zkt, Et, At = tk("zk", u0, un), tk("E", u0, un), tk("AE", u0, un)
+                if mode in "BD":
+                    gt(T.E[:, cs], Vw, off, T.ZW[:, cs], A.subtract, ["V", "vi%d" % t] + zkt, Et)
+                    if mode == "B":
+                        ac(T.AE[:, cs], T.E[:, cs], F.Abs, Et, At, scale=0.5)
+                    else:
+                        ts(T.AE[:, cs], T.E[:, cs], 0.0, None, A.max, None, Et, At, 0.5)
+                        p0 = 256 + (u0 - c0) // 16
+                        lin.append(([(Pu[:, p0:p0 + un // 16], T.GBn[:, sl(m)], T.E[:, u0 + m:u0 + un:16], False) for m in range(16)], Et))
+                else:
+                    ag(T.E[:, cs], Vw, off, ["V", "vi%d" % t], Et)
+                    P, p0, px = tile(un)
+                    lst = []
+                    for a0 in range(0, un, 512):
+                        lst += grp([(P[:, p0 + a0:p0 + a0 + 512], T.nIb[:], T.ZW[:, u0 + a0:u0 + a0 + 512], False),
+                                    (P[:, p0 + a0:p0 + a0 + 512], T.Ib[:], T.E[:, u0 + a0:u0 + a0 + 512], False)])
+                    mm(lst, ["Ib", "nIb"] + Et + zkt, px, px)
+                    ac(T.AE[:, cs], P[:, p0:p0 + un], F.Abs, px, At, scale=0.5, px=px)
+            full = grp(pen + [x for (l, _t) in lin for x in l] + [(o, T.GB2[:, sl(m)], T.AE[:, c0 + m:c0 + 1024:16], False) for m in range(16)])
+            mm(full[:len(pen)], ["NI", "pIb", "thh", "bad1", "bad2", "brow%d" % t, ub + "u", ub + "r"], [ub + "f"], [ub])
+            for i, (l, Et) in enumerate(lin):
+                mm(full[len(pen) + 16 * i:len(pen) + 16 * i + 16], ["GBn"] + Et, [ub + "f"], [ub])
+            mm(full[-16:], ["GB2"] + tk("AE", c0, 1024), [ub + "f"], [ub])
+            tt(T.key[:, bs], o, T.K1[:, bs], A.min, [ub + "f", "K1%d" % t], ["key%d" % t], px=[ub])
+            if t == 1:
+                tt(T.R[:], T.key[:, 0:96], T.PVh[:], A.max, ["key0", "key1", "PVh"], ["R"])
+        tt(T.m96[:], T.R[:], T.key[:, 96:192], A.max, ["R", "key1", "key2"], ["m96"])
+        tt(T.m48[:], T.m96[:, 0:48], T.m96[:, 48:96], A.max, ["m96"], ["m48"])
+        tt(T.m24[:], T.m48[:, 0:24], T.m48[:, 24:48], A.max, ["m48"], ["m24"])
+        tt(T.fin[:], T.m24[:, 0:12], T.m24[:, 12:24], A.max, ["m24"], ["fin"])
+        last = s == RO - 1
+        pop = T.popb[:, 0:12]
+        if s > 0:
+            tt(pop, T.fin[:], T.thr[:], A.is_lt, ["fin", "thr"], ["pop"])
+        else:
+            ms(pop, 0.0, ["pop"])
+        if not last:
+            ts(T.U[:, 16 * (s + 1):16 * (s + 1) + 12], T.fin[:], 4095, None, A.bitwise_and, None, ["fin"], ["U%d" % (s + 1)])
+            mm(grp([(T.mP[:, 400:413], T.one[:, 0:128], T.popb[:, 0:13], True)]), ["one", "pop", "popc"], ["cnt"], ["mP"])
+            add("dve", lambda g: g.vector.tensor_reduce(T.xa[:, 0:1], T.mP[:, 400:413], AxisListType.X, A.add), vcost(13, 1), ["cnt"], ["xa0"], ["mP"])
+            ts(T.xa[:, 1:2], T.xa[:, 0:1], M28, -M28, A.add, A.add, ["xa0"], ["xa1"])
+        if s > 0:
+            for q in range(12):
+                ts(T.EQ[:, q, 0:L - 16 * q], T.Pb[:, 16 * q:L], T.P8[:, q:q + 1], T.popb[:, q:q + 1], A.is_equal, A.mult, ["Pb", "P8", "pop"], ["EQ%d" % q], 0.5)
+            full = grp([(T.mP[:, 208 + 16 * q:384], T.BOb[:], T.EQ[:, q, 16:L - 16 * q], False) for q in range(11)])
+            for a, b in ((0, 3), (3, 7), (7, 11)):
+                mm(full[a:b], ["BOb"] + ["EQ%d" % q for q in range(a, b)], ["dup"], ["mP"])
+            if CFG["dupa"]:
+                ac(T.dupb[:, 16:L], T.mP[:, 208:384], F.Copy, ["dup"], ["dupb"], px=["mP"])
+            else:
+                cp(T.dupb[:, 16:L], T.mP[:, 208:384], ["dup"], ["dupb"], px=["mP"])
+            o = T.uA[:, 192:204]
+            full = grp([(o, T.IW[:, 16:144], T.P8[:, 0:12], True), (o, T.I8k[:], pop, True)] +
+                       [(o, T.LT[:, m], T.EQ[:, :, m], False) for m in range(1, 16)] +
+                       [(T.uA[:, 193:204], T.G8k[:, sl(m)], T.dupb[:, 16 + m:L:16], False) for m in range(16)])
+            later.append((full, o, pop, z, zt, zsend, s))
+
+        def writes(full, o, pop, z, zt, zsend, s):
+            mm(full[:2], ["IW", "I8k", "P8", "pop"], ["acc"], ["uA"])
+            mm(full[2:17], ["EQ%d" % q for q in range(12)] + ["LT%d" % m for m in range(1, 16)], ["acc"], ["uA"])
+            mm(full[17:], ["G8k", "dupb"], ["acc"], ["uA"])
+            tt(sm(4), o, T.DUM[:], A.min, ["acc", "DUM"], ["sof"], px=["uA"])
+            so = T.so[:, 16 * s:16 * s + 12]
+            ts(so, sm(4), 10240.0, None, A.add, None, ["sof"], ["so%d" % s])
+            osend = add("pool", send(so, lambda j, s=s: T.ro[:, (2 * s + j) * 16:(2 * s + j) * 16 + 12], s), 1000.0, ["so%d" % s], (), lat=2000.0)
+            sc = (50 / 0.83 + L * SC) * CY
+            add("dve", lambda g, so=so, z=z: g.vector.tensor_copy(T.V[:].indirect(so), z), sc, ["so%d" % s, zt], ["V", "Vpad"])
+            for j in range(2):
+                a = 2 * s + j
+                add("dve", lambda g, a=a: g.vector.tensor_copy(T.V[:].indirect(T.ro[:, 16 * a:16 * a + 12]), T.rz[:, a * L:(a + 1) * L]), sc, (), ["V", "Vpad"],
+                    ext=[("r%d_%d" % (s, j), 2 * neng[j])], soft=[zsend, osend])
+
+        if last:
+            step[0] = RO
+            writes(*later.pop())
+            step[0] = s
+        Ai, Bi, slt = si(3), si(4), si(5)
+        ts(Ai, T.fin[:], 17, None, A.arith_shift_right, None, ["fin"], ["Ai"])
+        ts(Bi, T.fin[:], 12, 31, A.arith_shift_right, A.bitwise_and, ["fin"], ["Bi"])
+        ts(slt, Ai, 183.0, 1.0 / 9, A.add, A.mult, ["Ai"], ["slt"])
+        ts(sm(5), Ai, -1.0, 128.0, A.mult, A.add, ["Ai"], ["rr"])
+        ts(npu, Ai, 96.0, None, A.is_lt, None, ["Ai"], ["np"])
+        tt(sm(6), sm(5), slt, A.min, ["rr", "slt"], ["gg"])
+        tt(sm(7), Bi, sm(6), A.subtract, ["Bi", "gg"], ["dd"])
+        tt(sm(8), sm(7), npu, A.mult, ["dd", "np"], ["dl"])
+        tt(sm(9), Bi, sm(8), A.subtract, ["Bi", "dl"], ["zsl"])
+        lin12(sm(10), sm(9), float(L), 0.0, ["zsl"], ["zs2"])
+        tt(sm(11), sm(10), T.LL[:], A.add, ["zs2", "LL"], ["zs3"])
+        cp(T.zo[:], sm(11), ["zs3"], ["zo"])
+        zr = ["zo", "zpad", "flip"] + tk("zk", 0, 3072) + ["z%d" % x for x in range(s + 1)]
+        if CFG["zg"]:
+            ag(zs(22 + s), T.ZW[:, 0:(22 + s) * L], T.zo[:], zr, ["z%d" % (s + 1)])
+        else:
+            gt(zs(22 + s), T.ZW[:, 0:(22 + s) * L], T.zo[:], None, None, zr, ["z%d" % (s + 1)])
+        tt(sm(12), sm(6), sm(8), A.add, ["gg", "dl"], ["cs"])
+        tt(ptr1, npu, Bi, A.mult, ["np", "Bi"], ["ptr1"])
+        if not last:
+            tt(sm(13), npu, pop, A.add, ["np", "pop"], ["de"])
+            tt(T.e[:], T.e[:], sm(13), A.subtract, ["e", "de"], ["e"])
+        lin12(sm(14), sm(5), 4095.0, 0.0, ["rr"], ["Pa"])
+        tt(sm(15), sm(14), sm(3), A.add, ["Pa", "P0"], ["Pp"])
+        tt(sm(21), T.fin[:], Bi, A.subtract, ["Bi", "fin"], ["fm"])
+        tt(sm(16), npu, sm(21), A.mult, ["np", "fm"], ["Pq"])
+        tt(sm(17), sm(15), npu, A.mult, ["Pp", "np"], ["Pr"])
+        tt(sm(19), sm(15), sm(17), A.subtract, ["Pp", "Pr"], ["Ps"])
+        tt(sm(18), sm(19), sm(16), A.subtract, ["Ps", "Pq"], ["dlt"])
+        gt(T.sel[:], sm(12), T.QL[:], T.ca1[:], A.is_equal, ["cs", "QL", "ca1"], ["sel"])
+        gt(T.dsel[:], sm(18), T.QL[:], T.sel[:], A.mult, ["dlt", "QL", "sel"], ["dsel"])
+        if CFG["pvp"]:
+            mm(grp([(T.uB[:, 320:512], T.IW[:, 16:144], T.PV[:], True), (T.uB[:, 320:512], T.IW[:, 16:144], T.dsel[:], True)]), ["IW", "PV", "dsel"], ["PVp"], ["uB"])
+            ac(T.PV[:], T.uB[:, 320:512], F.Copy, ["PVp"], ["PV"], px=["uB"])
+        else:
+            tt(T.PV[:], T.PV[:], T.dsel[:], A.add, ["PV", "dsel"], ["PV"])
+
+    step[0] = RO
+    dma("sp", T.yv[:], T.V[:, 0:W], 1 << 20, ["V"], ())
+    dma("sp", T.yz[:], zs(31), 49152, ["z%d" % RO], ())
+    cp(T.i192[:], T.PV[:], ["PV"], ["i192"])
+    ts(T.j192[:], T.i192[:], 17, None, A.arith_shift_right, None, ["i192"], ["j192"])
+    ts(T.i192[:], T.j192[:], -6.0, 1.0 / 9, A.add, A.mult, ["j192"], ["i192"])
+    ts(T.t192[:], T.i192[:], 0.0, 9.0, A.max, A.min, ["i192"], ["t192"])
+    ts(T.t192[:], T.t192[:], -9.0, -1.0, A.mult, A.add, ["t192"], ["t192"])
+    tt(T.t192[:], T.t192[:], T.j192[:], A.add, ["t192", "j192"], ["t192"])
+    ts(T.t192[:], T.t192[:], 0.0, None, A.max, None, ["t192"], ["t192"])
+    gt(T.tr[:, 0:L], T.t192[:], T.INV[:], None, None, ["t192", "INV"], ["tr0"])
+    add("dve", lambda g: g.vector.transpose(T.src4[:, 0], T.tr[:, 0:L]), vcost(L, 1), ["tr0"], ["s40"])
+    mm(swap3(lambda rho: T.dA[:, 96 * rho:96 * rho + 96], lambda ga: T.src4[:, 0, :, ga, :]), ["IW0", "IW1", "s40"], ["dA0"], ["dA0"])
+    for rho in range(2):
+        ac(T.ol[:, :, rho, :], T.dA[:, 96 * rho:96 * rho + 96], F.Copy, ["dA0"], ["ol%d" % rho], px=["dA0"])
+    dma("act", T.yl[:], T.ol[:], 49152, ["ol0", "ol1"], ())
+    gt(T.Pm[:], ptr1, T.EL[:], T.DM[:], A.mult, ["ptr1", "EL", "DM"], ["Pm"])
+    mm(grp([(T.dB[0:8, 0:L], T.B8[:], T.Pm[:], True)]), ["B8", "Pm"], ["dB0"], ["dB0"])
+    ts(T.op[0:8, :], T.dB[0:8, 0:L], -1.0, None, A.add, None, ["dB0"], ["op"], px=["dB0"])
+    dma("sp", T.yp[:], T.op[0:8, :], 6144, ["op"], ())
+    return ops, 2 * (RO - 1) * sum(neng)
+
+
+BIAS = {}
+ROUNDS = 4
+LOOK = 110.0
+PLAN = """
+dpop.thr:1410 dU.fin:1785 pcnt.popc:1226 dxa0.cnt:1868 dxa1.xa0:2026 dnu0.nu0:-376 dsh0.nu0:-15 dt30.sh0:28 dxi0.xa1:3 dEQ0.pop:2021 dEQ1.pop:2051 dEQ2.pop:1973 dEQ3.pop:2099 dEQ4.pop:2096 dEQ5.pop:2163 dEQ6.pop:2050 dEQ7.pop:1857 dEQ8.pop:2193 dEQ9.pop:1974 dEQ10.pop:2056 dEQ11.pop:2131 pdup.EQ2:2269 pdup.EQ6:2283 pdup.EQ10:1765 ddupb.dup:1566 pacc.pop:445 pacc.LT15:1670 pacc.dupb:262 dsof.DUM:60 dso.sof:345 p.so:-1858 dAi.fin:2133 dBi.fin:1785 dslt.Ai:2155 drr.Ai:2120 dnp.Ai:1425 dgg.slt:2178 ddd.gg:695 ddl.np:2202 dzsl.dl:2206 azs2.zsl:2031 dzs3.LL:2338 dzo.zs3:685 dz.z:1912 dnu1.nu1:169 dsh1.nu1:197 dt31.sh1:202 dxi2.xa1:244 aY0.xi0:639 aY1.xi1:-782 aY2.xi3:118 pd.Y0:2299 pd.Y1:549 p.z:3758 aS0.d:-78 aS1.d:1023 dzk0.S0:833 dzk1.S1:15 puAu.zk1:739 dui0.uAu:-384 duk0.ui0:816 dv0.uk0:119 asq0.vpad:1275 dtp0.sq0:582 dh0.tp0:18 dvi0.h0:914 pd.Y3:1570 aY4.xi5:1156 dV.z:422 dV.:127 aS2.d:-320 dzk2.S3:441 puBu.zk3:994 dui1.uBu:665 duk1.ui1:79 dv1.uk1:489 asq1.v1:951 dtp1.sq1:668 dh1.tp1:932 dvi1.h1:-26 pd.Y5:1563 aS4.d:-328 azk4.d:2130 puCu.zk5:936 dui2.uCu:870 duk2.ui2:-306 dv2.uk2:-798 asq2.v2:795 dtp2.sq2:949 dh2.tp2:289 dvi2.h2:593 dde.pop:2668 de.de:2906 dcs.dl:2320 dptr1.Bi:2865 aPa.rr:1281 dPp.P0:2358 dfm.fin:2314 dPq.fm:2409 dPr.np:2439 dPs.Pr:2612 ddlt.Pq:2811 dsel.ca1:2788 ddsel.sel:2915 dPV.dsel:2583 aD0.e:1605 aD1.e:215 dvown.U:516 dRL.PV:859 dPVh.PV:1006 dPVh.fk:1745 dn96.RL:889 dn48.n96:946 dn24.n48:898 dKm.n24:1056 dbad2.PV:500 dbad1.PV:1256 aE0.vi0:957 pd.zk1:1120 aE2.vi1:2503 pd.zk3:518 aAE0.d:1595 dE4.zk5:2853 aAE2.d:1174 dAE4.E5:1236 puAr.S1:1187 puAr.zk1:1685 dbrow0.uAr:1434 dK10.uk0:411 puBr.S3:2304 puBr.zk3:4469 dbrow1.uBr:2498 dK11.uk1:613 puCr.S5:2366 dbrow2.uCr:330 dK12.uk2:1370 puAf.uAr:2949 puAf.AE1:1121 dkey0.K10:-115 puBf.uBr:1036 puBf.AE3:2011 dkey1.K11:1390 dR.PVh:1709 puCf.uCr:1740 puCf.E5:3521 puCf.AE5:2637 dkey2.K12:332 dm96.key2:1334 dm48.m96:1350 dm24.m48:1855 dfin.m24:1339 dsi1.C63:908 dsi2.si1:999 dfk.si2:1290 dthr.e:1813 dP8.h0:837 dPm.DM:1946 pPbc.Pm:693 dPb.Pbc:1904 aP0a.e:1206 dP0.U:660 aflip.z:1397
+"""
+OFF = {x.split(":")[0]: 10 * int(x.split(":")[1]) for x in PLAN.split()}
+
+
+def schedule(ops):
+    n = len(ops)
+    pre = [sorted(set(o["deps"]) | set(o["soft"])) for o in ops]
+    suc = [[] for _ in range(n)]
+    for i in range(n):
+        for d in pre[i]:
+            suc[d].append(i)
+    pr = [0.0] * n
+    for i in range(n - 1, -1, -1):
+        pr[i] = ops[i]["cost"] + ops[i]["lat"] + HOP + max([pr[j] for j in suc[i]] + [0.0])
+    bias = [BIAS.get(o["cls"], 0) for o in ops]
+
+    def place(pre, suc, pr, back):
+        left = [len(p) for p in pre]
+        rdy, start = [0.0] * n, [0.0] * n
+        avail = [i for i in range(n) if left[i] == 0]
+        used = {}
+        for _ in range(n):
+            i = max(avail, key=lambda i: (pr[i], i if back else -i))
+            avail.remove(i)
+            c = ops[i]["cost"]
+            t = rdy[i] + (ops[i]["lat"] if back else 0.0)
+            u = used.setdefault(ops[i]["eng"], [])
+            k = len(u)
+            while k > 0 and u[k - 1][1] > t:
+                k -= 1
+            while k < len(u) and u[k][0] < t + c:
+                t = max(t, u[k][1])
+                k += 1
+            u.insert(k, (t, t + c))
+            start[i] = t
+            done = t + c + HOP + (0.0 if back else ops[i]["lat"])
+            for j in suc[i]:
+                rdy[j] = max(rdy[j], done)
+                left[j] -= 1
+                if left[j] == 0:
+                    avail.append(j)
+        return start
+
+    if OFF:
+        for i in range(n - 1, -1, -1):
+            o = ops[i]
+            if o["cls"] in OFF and 0 <= o["step"] < RO:
+                pr[i] = -(o["step"] * 20000.0 + OFF[o["cls"]])
+            else:
+                pr[i] = o["cost"] + o["lat"] + HOP + max([pr[j] for j in suc[i]] + [-(RO + 2) * 20000.0])
+        left = [len(p) for p in pre]
+        rdy, start, order, avail, free = [0.0] * n, [0.0] * n, [], {}, {}
+        for i in range(n):
+            if left[i] == 0:
+                avail.setdefault(ops[i]["eng"], []).append(i)
+        while len(order) < n:
+            best = None
+            for e, lst in avail.items():
+                if lst:
+                    t0 = max(free.get(e, 0.0), min(rdy[i] for i in lst))
+                    i = max((i for i in lst if rdy[i] <= t0 + LOOK), key=lambda i: (pr[i], -i))
+                    t = max(t0, rdy[i])
+                    if best is None or t < best[0]:
+                        best = (t, i, e)
+            t, i, e = best
+            avail[e].remove(i)
+            order.append(i)
+            start[i] = t
+            free[e] = t + ops[i]["cost"]
+            for j in suc[i]:
+                rdy[j] = max(rdy[j], free[e] + ops[i]["lat"] + HOP)
+                left[j] -= 1
+                if left[j] == 0:
+                    avail.setdefault(ops[j]["eng"], []).append(j)
+        return order, start
+    best = None
+    pr = [pr[i] + bias[i] for i in range(n)]
+    for _ in range(ROUNDS):
+        start = place(pre, suc, pr, False)
+        end = max(start[i] + ops[i]["cost"] + ops[i]["lat"] for i in range(n))
+        if best is None or end < best[0]:
+            best = (end, start)
+        rev = place(suc, pre, [start[i] + ops[i]["cost"] + ops[i]["lat"] for i in range(n)], True)
+        pr = [rev[i] + ops[i]["cost"] + bias[i] for i in range(n)]
+    start = best[1]
+    return sorted(range(n), key=lambda i: (start[i], i)), start
+
+
+ORDER = []
+
+
+def rank_program(g, core, T, topo):
+    rank = T.rank_of(core)
+    if rank is None:
+        return
+    ops, nsent = build(T, topo, core, rank)
+    if not ORDER:
+        ORDER.append(schedule(ops)[0])
+    queue = {"dve": g.vector, "act": g.scalar, "pe": g.tensor, "pool": g, "sp": g.sync}
+    known = {e: {} for e in queue}
+    mark, count, nd = {}, {}, 0
+    for i in ORDER[0]:
+        o = ops[i]
+        kn = known[o["eng"]]
+        need = {}
+        for d in o["deps"]:
+            if mark[d] is not None:
+                need[mark[d][0]] = max(need.get(mark[d][0], (0, None)), (mark[d][1], d))
+        for sem, (val, d) in sorted(need.items(), key=lambda x: -x[1][1]):
+            if kn.get(sem, 0) < val:
+                queue[o["eng"]].wait_ge(T.sem[sem], val)
+                for a, b in mark[d][2].items():
+                    kn[a] = max(kn.get(a, 0), b)
+        for sem, val in o["ext"]:
+            queue[o["eng"]].wait_ge(T.sem[sem], val)
+        x = o["fn"](g)
+        if x is None:
+            mark[i] = None
+            continue
+        if o["dma"]:
+            sem, inc = "d%d" % nd, 16
+            nd += 1
+        else:
+            sem, inc = o["eng"], 1
+        x.then_inc(T.sem[sem], inc)
+        count[sem] = count.get(sem, 0) + inc
+        clock = dict(kn)
+        clock[sem] = count[sem]
+        mark[i] = (sem, count[sem], clock)
+    for sem, val in sorted(count.items()):
+        g.wait_ge(T.sem[sem], val)
+    g.wait_ge(T.sem.sent, nsent)

@@ -3,10 +3,10 @@ from concourse.mybir import AluOpType as A, AxisListType, ActivationFunctionType
 
 L, W, RO = 192, 4096, 10
 CFG = {
-    "XG": ["AA", "A", "A"],
-    "XP": "RRS",
-    "VG": ["A", "A", "D"],
-    "sq": True, "brow": False, "rtp": True, "tiny": True, "zg": False, "pvp": False, "dupa": False, "pbm": False, "xs": [(0, 64), (64, 192)],
+    "XG": ["AA", "AA", "AD"],
+    "XP": "RRR",
+    "VG": ["AA", "DA", "BA"],
+    "sq": True, "brow": True, "rtp": False, "tiny": False, "zg": True, "pvp": False, "dupa": True, "pbm": True, "xs": [(0, 64), (64, 192)],
 }
 FP16W = True
 f32, bf, i32, u16 = "float32", "bfloat16", "int32", "uint16"
@@ -30,7 +30,7 @@ SCRATCH = {
     "Wh": _sb(144, "float16" if FP16W else bf), "Wl": _sb(144, bf), "LT": _sb((16, 128), bf), "RT": _sb((16, 128), bf),
     "DM": _sb(L, f32), "pi": _sb(1, i32), "pj": _sb(1, i32), "PM": _sb(1, f32), "hf": _sb(2, f32), "wf": _sb(4, f32), "wi": _sb(2, i32),
     "thf": _sb(1, f32), "C63": _sb(1, f32), "ltm": _sb(16, f32),
-    "c16": _sb(12, f32), "c1": _sb(12, f32), "LL": _sb(12, f32), "DUM": _sb(12, f32), "KQ": _sb(12, i32), "QF": _sb(12, f32), "t12": _sb(12, f32),
+    "c16": _sb(12, f32), "c1": _sb(12, f32), "LL": _sb(12, f32), "DUM": _sb(12, f32), "LLd": _sb(12, f32), "KQ": _sb(12, i32), "QF": _sb(12, f32), "t12": _sb(12, f32),
     "QL": _sb(12, u16), "DL": _sb(6, u16), "EL": _sb(12, u16), "PERM": _sb(12, u16), "INV": _sb(12, u16),
     "U": _sb(16 * (RO + 1), i32), "xi": _sb(L, u16), "nu": _sb(L, i32), "sh": _sb(L, i32), "t3": _sb(L, f32),
     "ui": _sb(L, i32), "uk": _sb(L, i32), "v": _sb(208, f32), "sq": _sb(208, f32), "tp": _sb(208, i32), "h": _sb(208, i32), "vi": _sb(208, u16),
@@ -48,7 +48,8 @@ SCRATCH = {
 NDMA = 16
 SEMAPHORES = ["dve", "act", "pe", "pool", "sent"] + ["d%d" % i for i in range(NDMA)] + ["r%d_%d" % (s, j) for s in range(1, RO) for j in range(2)]
 
-CY, PC, GA, SC, HOP = 1.04, 0.52, 1.56, 3.8, 100.0
+FIX, RL = 30.0, 2500.0
+CY, PC, GA, SC, HOP = 0.9, 0.46, 1.56, 3.8, 160.0
 
 
 def build(T, topo, core, rank):
@@ -83,6 +84,10 @@ def build(T, topo, core, rank):
             deps.update(prev)
             bank[b] = (eng, cur + [i], prev)
         deps.discard(i)
+        if eng in ("dve", "act"):
+            cost += FIX
+        if eng == "pool" and lat:
+            lat = RL
         ops.append(dict(eng=eng, fn=fn, cost=cost, deps=deps, lat=lat, ext=list(ext), soft=list(soft), dma=dma, step=step[0],
                         cls=eng[0] + kind(w[:1]) + "." + kind(r[-1:])))
         return i
@@ -291,6 +296,7 @@ def build(T, topo, core, rank):
         for m in range(16):
             ac(T.RT[:, m], T.BO[:], F.Copy, ["BO", "DM"], ["RT%d" % m], scale=T.DM[:, m:m + 1])
     cp(T.EL[:], T.c1[:], ["c1"], ["EL"])
+    ts(T.LLd[:], T.LL[:], 1.0 / L, None, A.mult, None, ["LL"], ["LLd"])
     ts(T.DUM[:], T.LL[:], W - 10240.0, None, A.add, None, ["LL"], ["DUM"])
     ts(T.t12[:, 0:1], T.PM[:], 12.0, None, A.mult, None, ["PM"], ["t12"])
     ts(T.INV[:], T.c1[:], T.t12[:, 0:1], None, A.add, None, ["c1", "t12"], ["INV"])
@@ -566,23 +572,23 @@ def build(T, topo, core, rank):
         Ai, Bi, slt = si(3), si(4), si(5)
         ts(Ai, T.fin[:], 17, None, A.arith_shift_right, None, ["fin"], ["Ai"])
         ts(Bi, T.fin[:], 12, 31, A.arith_shift_right, A.bitwise_and, ["fin"], ["Bi"])
-        ts(slt, Ai, 183.0, 1.0 / 9, A.add, A.mult, ["Ai"], ["slt"])
+        ts(slt, T.fin[:], 1.0 / (9 * 131072), (182.5 - 1.0 / 64) / 9, A.mult, A.add, ["fin"], ["slt"])
+        ts(sm(6), T.fin[:], 96.0 * 131072, 64.0, A.is_lt, A.mult, ["fin"], ["gg"])
+        tt(sm(7), Bi, sm(6), A.max, ["Bi", "gg"], ["dd"])
+        tt(sm(9), sm(7), slt, A.min, ["dd", "slt"], ["zsl"])
+        tt(sm(11), sm(9), T.LLd[:], A.add, ["zsl", "LLd"], ["zs3"])
+        ts(T.zo[:], sm(11), float(L), None, A.mult, None, ["zs3"], ["zo"])
         ts(sm(5), Ai, -1.0, 128.0, A.mult, A.add, ["Ai"], ["rr"])
-        ts(npu, Ai, 96.0, None, A.is_lt, None, ["Ai"], ["np"])
-        tt(sm(6), sm(5), slt, A.min, ["rr", "slt"], ["gg"])
-        tt(sm(7), Bi, sm(6), A.subtract, ["Bi", "gg"], ["dd"])
-        tt(sm(8), sm(7), npu, A.mult, ["dd", "np"], ["dl"])
-        tt(sm(9), Bi, sm(8), A.subtract, ["Bi", "dl"], ["zsl"])
-        lin12(sm(10), sm(9), float(L), 0.0, ["zsl"], ["zs2"])
-        tt(sm(11), sm(10), T.LL[:], A.add, ["zs2", "LL"], ["zs3"])
-        cp(T.zo[:], sm(11), ["zs3"], ["zo"])
+        ts(npu, T.fin[:], 96.0 * 131072, None, A.is_lt, None, ["fin"], ["np"])
+        ts(sm(10), T.fin[:], 96.0 * 131072, None, A.is_ge, None, ["fin"], ["pu"])
+        tt(sm(8), sm(5), sm(10), A.mult, ["rr", "pu"], ["dl"])
         zr = ["zo", "zpad", "flip"] + tk("zk", 0, 3072) + ["z%d" % x for x in range(s + 1)]
         if CFG["zg"]:
             ag(zs(22 + s), T.ZW[:, 0:(22 + s) * L], T.zo[:], zr, ["z%d" % (s + 1)])
         else:
             gt(zs(22 + s), T.ZW[:, 0:(22 + s) * L], T.zo[:], None, None, zr, ["z%d" % (s + 1)])
-        tt(sm(12), sm(6), sm(8), A.add, ["gg", "dl"], ["cs"])
         tt(ptr1, npu, Bi, A.mult, ["np", "Bi"], ["ptr1"])
+        tt(sm(12), ptr1, sm(8), A.add, ["ptr1", "dl"], ["cs"])
         if not last:
             tt(sm(13), npu, pop, A.add, ["np", "pop"], ["de"])
             tt(T.e[:], T.e[:], sm(13), A.subtract, ["e", "de"], ["e"])
@@ -590,8 +596,7 @@ def build(T, topo, core, rank):
         tt(sm(15), sm(14), sm(3), A.add, ["Pa", "P0"], ["Pp"])
         tt(sm(21), T.fin[:], Bi, A.subtract, ["Bi", "fin"], ["fm"])
         tt(sm(16), npu, sm(21), A.mult, ["np", "fm"], ["Pq"])
-        tt(sm(17), sm(15), npu, A.mult, ["Pp", "np"], ["Pr"])
-        tt(sm(19), sm(15), sm(17), A.subtract, ["Pp", "Pr"], ["Ps"])
+        tt(sm(19), sm(15), sm(10), A.mult, ["Pp", "pu"], ["Ps"])
         tt(sm(18), sm(19), sm(16), A.subtract, ["Ps", "Pq"], ["dlt"])
         gt(T.sel[:], sm(12), T.QL[:], T.ca1[:], A.is_equal, ["cs", "QL", "ca1"], ["sel"])
         gt(T.dsel[:], sm(18), T.QL[:], T.sel[:], A.mult, ["dlt", "QL", "sel"], ["dsel"])
@@ -626,9 +631,12 @@ def build(T, topo, core, rank):
 
 BIAS = {}
 ROUNDS = 4
-LOOK = 110.0
+LOOK, SLACK = 300.0, 60.0
 PLAN = """
 dpop.thr:1410 dU.fin:1785 pcnt.popc:1226 dxa0.cnt:1868 dxa1.xa0:2026 dnu0.nu0:-376 dsh0.nu0:-15 dt30.sh0:28 dxi0.xa1:3 dEQ0.pop:2021 dEQ1.pop:2051 dEQ2.pop:1973 dEQ3.pop:2099 dEQ4.pop:2096 dEQ5.pop:2163 dEQ6.pop:2050 dEQ7.pop:1857 dEQ8.pop:2193 dEQ9.pop:1974 dEQ10.pop:2056 dEQ11.pop:2131 pdup.EQ2:2269 pdup.EQ6:2283 pdup.EQ10:1765 ddupb.dup:1566 pacc.pop:445 pacc.LT15:1670 pacc.dupb:262 dsof.DUM:60 dso.sof:345 p.so:-1858 dAi.fin:2133 dBi.fin:1785 dslt.Ai:2155 drr.Ai:2120 dnp.Ai:1425 dgg.slt:2178 ddd.gg:695 ddl.np:2202 dzsl.dl:2206 azs2.zsl:2031 dzs3.LL:2338 dzo.zs3:685 dz.z:1912 dnu1.nu1:169 dsh1.nu1:197 dt31.sh1:202 dxi2.xa1:244 aY0.xi0:639 aY1.xi1:-782 aY2.xi3:118 pd.Y0:2299 pd.Y1:549 p.z:3758 aS0.d:-78 aS1.d:1023 dzk0.S0:833 dzk1.S1:15 puAu.zk1:739 dui0.uAu:-384 duk0.ui0:816 dv0.uk0:119 asq0.vpad:1275 dtp0.sq0:582 dh0.tp0:18 dvi0.h0:914 pd.Y3:1570 aY4.xi5:1156 dV.z:422 dV.:127 aS2.d:-320 dzk2.S3:441 puBu.zk3:994 dui1.uBu:665 duk1.ui1:79 dv1.uk1:489 asq1.v1:951 dtp1.sq1:668 dh1.tp1:932 dvi1.h1:-26 pd.Y5:1563 aS4.d:-328 azk4.d:2130 puCu.zk5:936 dui2.uCu:870 duk2.ui2:-306 dv2.uk2:-798 asq2.v2:795 dtp2.sq2:949 dh2.tp2:289 dvi2.h2:593 dde.pop:2668 de.de:2906 dcs.dl:2320 dptr1.Bi:2865 aPa.rr:1281 dPp.P0:2358 dfm.fin:2314 dPq.fm:2409 dPr.np:2439 dPs.Pr:2612 ddlt.Pq:2811 dsel.ca1:2788 ddsel.sel:2915 dPV.dsel:2583 aD0.e:1605 aD1.e:215 dvown.U:516 dRL.PV:859 dPVh.PV:1006 dPVh.fk:1745 dn96.RL:889 dn48.n96:946 dn24.n48:898 dKm.n24:1056 dbad2.PV:500 dbad1.PV:1256 aE0.vi0:957 pd.zk1:1120 aE2.vi1:2503 pd.zk3:518 aAE0.d:1595 dE4.zk5:2853 aAE2.d:1174 dAE4.E5:1236 puAr.S1:1187 puAr.zk1:1685 dbrow0.uAr:1434 dK10.uk0:411 puBr.S3:2304 puBr.zk3:4469 dbrow1.uBr:2498 dK11.uk1:613 puCr.S5:2366 dbrow2.uCr:330 dK12.uk2:1370 puAf.uAr:2949 puAf.AE1:1121 dkey0.K10:-115 puBf.uBr:1036 puBf.AE3:2011 dkey1.K11:1390 dR.PVh:1709 puCf.uCr:1740 puCf.E5:3521 puCf.AE5:2637 dkey2.K12:332 dm96.key2:1334 dm48.m96:1350 dm24.m48:1855 dfin.m24:1339 dsi1.C63:908 dsi2.si1:999 dfk.si2:1290 dthr.e:1813 dP8.h0:837 dPm.DM:1946 pPbc.Pm:693 dPb.Pbc:1904 aP0a.e:1206 dP0.U:660 aflip.z:1397
+"""
+PLAN = """
+dpop.thr:1900 dU.fin:1946 pcnt.popc:1912 dxa0.cnt:1944 dxa1.xa0:1968 dnu0.nu0:-100 dsh0.nu0:-247 dt30.sh0:-78 dxi0.xa1:-381 dEQ0.pop:2050 dEQ1.pop:2056 dEQ2.pop:2084 dEQ3.pop:2056 dEQ4.pop:2074 dEQ5.pop:2080 dEQ6.pop:2088 dEQ7.pop:2092 dEQ8.pop:1563 dEQ9.pop:2104 dEQ10.pop:2110 dEQ11.pop:2116 pdup.EQ2:2147 pdup.EQ6:1926 pdup.EQ10:1950 adupb.dup:2102 pacc.pop:-30 pacc.LT15:-131 pacc.dupb:157 dsof.DUM:-18 dso.sof:-111 p.so:-52 dBi.fin:2000 dslt.fin:2006 dgg.fin:2019 ddd.gg:2018 dzsl.slt:2038 dzs3.LLd:1997 dzo.zs3:2036 az.z:1947 dnu1.nu1:130 dsh1.nu1:136 dt31.sh1:200 dxi2.xa1:155 aY0.xi0:137 aY1.xi1:737 aY2.xi2:219 aY3.xi3:457 pd.Y0:122 pd.Y1:266 p.z:-30 aS0.d:188 aS1.d:-192 dzk0.S0:239 dzk1.S1:269 puAu.zk1:298 dui0.uAu:-627 duk0.ui0:310 dv0.uk0:316 asq0.vpad:331 dtp0.sq0:319 dh0.tp0:345 dvi0.h0:328 pd.Y2:322 pd.Y3:238 aY4.xi4:506 dY5.xi5:518 dV.z:399 dV.:344 aS2.d:295 aS3.d:343 dzk2.S2:415 dzk3.S3:152 puBu.zk3:378 dui1.uBu:592 duk1.ui1:483 dv1.uk1:632 asq1.v1:489 dtp1.sq1:336 dh1.tp1:490 dvi1.h1:481 pd.Y4:920 pd.Y5:619 aS4.d:598 aS5.d:536 dzk4.S4:612 dzk5.S5:618 puCu.zk5:678 dui2.uCu:654 duk2.ui2:660 dv2.uk2:694 asq2.v2:444 dtp2.sq2:712 dh2.tp2:667 dvi2.h2:824 dnp.fin:2359 dde.pop:2136 de.de:2319 dAi.fin:2500 drr.Ai:2344 dpu.fin:2512 ddl.pu:2426 dcs.dl:2511 dptr1.Bi:2429 dPa.rr:2542 dPp.P0:2411 dfm.fin:2618 dPq.fm:2560 dPs.pu:2554 ddlt.Pq:2496 dsel.ca1:2522 ddsel.sel:2713 dPV.dsel:2497 dD0.e:212 dD1.e:136 dvown.U:92 dRL.PV:616 dPVh.PV:656 dPVh.fk:562 dn96.RL:662 dn48.n96:668 dn24.n48:674 dKm.n24:701 dbad2.PV:854 dbad1.PV:703 aE0.vi0:800 aE1.vi0:726 pd.zk0:681 pd.zk1:730 aE3.vi1:781 dE2.zk2:1120 pd.zk3:820 aAE0.d:772 aAE1.d:1002 dE4.zk4:1122 aE5.vi2:874 pd.zk5:508 aAE3.d:1226 dAE2.E2:1198 aAE4.E4:1731 aAE5.d:1229 puAr.S1:1340 puAr.zk1:1234 abrow0.uAr:1016 dK10.uk0:1168 puBr.S3:907 puBr.zk3:1370 abrow1.uBr:881 dK11.uk1:1172 puCr.S5:1246 puCr.zk5:1916 abrow2.uCr:1204 dK12.uk2:1519 puAf.uAr:1198 puAf.AE1:941 dkey0.K10:1243 puBf.uBr:1277 puBf.E2:1614 puBf.AE3:1314 dkey1.K11:1268 dR.PVh:1274 puCf.uCr:1190 puCf.AE5:1064 dkey2.K12:1575 dm96.key2:1262 dm48.m96:1353 dm24.m48:1253 dfin.m24:1137 dsi1.C63:1131 dsi2.si1:1406 dfk.si2:1412 dthr.e:1403 dP8.h0:1424 dPm.h0:1424 pPbc.Pm:1510 dPb.Pbc:1741 dP0a.e:1456 dP0.U:1460 aflip.z:1257
 """
 OFF = {x.split(":")[0]: 10 * int(x.split(":")[1]) for x in PLAN.split()}
 
@@ -690,6 +698,10 @@ def schedule(ops):
                 if lst:
                     t0 = max(free.get(e, 0.0), min(rdy[i] for i in lst))
                     i = max((i for i in lst if rdy[i] <= t0 + LOOK), key=lambda i: (pr[i], -i))
+                    if rdy[i] > t0:
+                        fill = [j for j in lst if max(t0, rdy[j]) + ops[j]["cost"] <= rdy[i] + SLACK and j != i and rdy[j] < rdy[i]]
+                        if fill:
+                            i = max(fill, key=lambda j: (pr[j], -j))
                     t = max(t0, rdy[i])
                     if best is None or t < best[0]:
                         best = (t, i, e)
@@ -699,7 +711,7 @@ def schedule(ops):
             start[i] = t
             free[e] = t + ops[i]["cost"]
             for j in suc[i]:
-                rdy[j] = max(rdy[j], free[e] + ops[i]["lat"] + HOP)
+                rdy[j] = max(rdy[j], free[e] + ops[i]["lat"] + (0.0 if e == "pe" == ops[j]["eng"] else HOP))
                 left[j] -= 1
                 if left[j] == 0:
                     avail.setdefault(ops[j]["eng"], []).append(j)
@@ -735,7 +747,7 @@ def rank_program(g, core, T, topo):
         kn = known[o["eng"]]
         need = {}
         for d in o["deps"]:
-            if mark[d] is not None:
+            if mark[d] is not None and not (o["eng"] == "pe" == ops[d]["eng"]):
                 need[mark[d][0]] = max(need.get(mark[d][0], (0, None)), (mark[d][1], d))
         for sem, (val, d) in sorted(need.items(), key=lambda x: -x[1][1]):
             if kn.get(sem, 0) < val:

@@ -3,10 +3,10 @@ from concourse.mybir import AluOpType as A, AxisListType, ActivationFunctionType
 
 L, W, RO = 192, 4096, 10
 CFG = {
-    "XG": ["AA", "AA", "AD"],
-    "XP": "RRR",
-    "VG": ["AA", "DA", "BA"],
-    "sq": True, "brow": True, "rtp": False, "tiny": False, "zg": True, "pvp": False, "dupa": True, "pbm": True, "xs": [(0, 64), (64, 192)],
+    "XG": ["AA", "A", "A"],
+    "XP": "RRS",
+    "VG": ["DA", "DA", "BA"],
+    "sq": True, "brow": True, "rtp": False, "tiny": True, "zg": True, "pvp": False, "dupa": True, "pbm": True, "pre": True, "xs": [(0, 64), (64, 192)],
 }
 FP16W = True
 f32, bf, i32, u16 = "float32", "bfloat16", "int32", "uint16"
@@ -48,8 +48,8 @@ SCRATCH = {
 NDMA = 16
 SEMAPHORES = ["dve", "act", "pe", "pool", "sent"] + ["d%d" % i for i in range(NDMA)] + ["r%d_%d" % (s, j) for s in range(1, RO) for j in range(2)]
 
-FIX, RL = 30.0, 2500.0
-CY, PC, GA, SC, HOP = 0.9, 0.46, 1.56, 3.8, 160.0
+FIX, RL = 12.0, 2300.0
+CY, PC, GA, SC, HOP = 1.0, 0.5, 1.65, 4.0, 210.0
 
 
 def build(T, topo, core, rank):
@@ -517,13 +517,27 @@ def build(T, topo, core, rank):
                 mm(full[len(pen) + 16 * i:len(pen) + 16 * i + 16], ["GBn"] + Et, [ub + "f"], [ub])
             mm(full[-16:], ["GB2"] + tk("AE", c0, 1024), [ub + "f"], [ub])
             tt(T.key[:, bs], o, T.K1[:, bs], A.min, [ub + "f", "K1%d" % t], ["key%d" % t], px=[ub])
-            if t == 1:
-                tt(T.R[:], T.key[:, 0:96], T.PVh[:], A.max, ["key0", "key1", "PVh"], ["R"])
-        tt(T.m96[:], T.R[:], T.key[:, 96:192], A.max, ["R", "key1", "key2"], ["m96"])
-        tt(T.m48[:], T.m96[:, 0:48], T.m96[:, 48:96], A.max, ["m96"], ["m48"])
+            if not CFG["pre"]:
+                if t == 1:
+                    tt(T.R[:], T.key[:, 0:96], T.PVh[:], A.max, ["key0", "key1", "PVh"], ["R"])
+            elif t == 0:
+                tt(T.R[:, 0:48], T.PVh[:, 0:48], T.PVh[:, 48:96], A.max, ["PVh"], ["Ra"])
+                tt(T.R[:, 48:96], T.key[:, 0:48], T.R[:, 0:48], A.max, ["key0", "Ra"], ["Rb"])
+                tt(T.m96[:, 0:24], T.R[:, 48:72], T.R[:, 72:96], A.max, ["Rb"], ["Rc"])
+            elif t == 1:
+                tt(T.m96[:, 24:48], T.key[:, 48:72], T.key[:, 72:96], A.max, ["key0", "key1"], ["Rd"])
+                tt(T.m96[:, 48:72], T.key[:, 96:120], T.m96[:, 0:24], A.max, ["key1", "Rc"], ["Re"])
+                tt(T.key[:, 96:120], T.m96[:, 24:48], T.m96[:, 48:72], A.max, ["Rd", "Re"], ["key1"])
+        if CFG["pre"]:
+            tt(T.m48[:], T.key[:, 96:144], T.key[:, 144:192], A.max, ["key1", "key2"], ["m48"])
+        else:
+            tt(T.m96[:], T.R[:], T.key[:, 96:192], A.max, ["R", "key1", "key2"], ["m96"])
+            tt(T.m48[:], T.m96[:, 0:48], T.m96[:, 48:96], A.max, ["m96"], ["m48"])
         tt(T.m24[:], T.m48[:, 0:24], T.m48[:, 24:48], A.max, ["m48"], ["m24"])
         tt(T.fin[:], T.m24[:, 0:12], T.m24[:, 12:24], A.max, ["m24"], ["fin"])
         last = s == RO - 1
+        if last:
+            step[0] = RO
         pop = T.popb[:, 0:12]
         if s > 0:
             tt(pop, T.fin[:], T.thr[:], A.is_lt, ["fin", "thr"], ["pop"])
@@ -566,9 +580,7 @@ def build(T, topo, core, rank):
                     ext=[("r%d_%d" % (s, j), 2 * neng[j])], soft=[zsend, osend])
 
         if last:
-            step[0] = RO
             writes(*later.pop())
-            step[0] = s
         Ai, Bi, slt = si(3), si(4), si(5)
         ts(Ai, T.fin[:], 17, None, A.arith_shift_right, None, ["fin"], ["Ai"])
         ts(Bi, T.fin[:], 12, 31, A.arith_shift_right, A.bitwise_and, ["fin"], ["Bi"])
@@ -633,10 +645,8 @@ BIAS = {}
 ROUNDS = 4
 LOOK, SLACK = 300.0, 60.0
 PLAN = """
-dpop.thr:1410 dU.fin:1785 pcnt.popc:1226 dxa0.cnt:1868 dxa1.xa0:2026 dnu0.nu0:-376 dsh0.nu0:-15 dt30.sh0:28 dxi0.xa1:3 dEQ0.pop:2021 dEQ1.pop:2051 dEQ2.pop:1973 dEQ3.pop:2099 dEQ4.pop:2096 dEQ5.pop:2163 dEQ6.pop:2050 dEQ7.pop:1857 dEQ8.pop:2193 dEQ9.pop:1974 dEQ10.pop:2056 dEQ11.pop:2131 pdup.EQ2:2269 pdup.EQ6:2283 pdup.EQ10:1765 ddupb.dup:1566 pacc.pop:445 pacc.LT15:1670 pacc.dupb:262 dsof.DUM:60 dso.sof:345 p.so:-1858 dAi.fin:2133 dBi.fin:1785 dslt.Ai:2155 drr.Ai:2120 dnp.Ai:1425 dgg.slt:2178 ddd.gg:695 ddl.np:2202 dzsl.dl:2206 azs2.zsl:2031 dzs3.LL:2338 dzo.zs3:685 dz.z:1912 dnu1.nu1:169 dsh1.nu1:197 dt31.sh1:202 dxi2.xa1:244 aY0.xi0:639 aY1.xi1:-782 aY2.xi3:118 pd.Y0:2299 pd.Y1:549 p.z:3758 aS0.d:-78 aS1.d:1023 dzk0.S0:833 dzk1.S1:15 puAu.zk1:739 dui0.uAu:-384 duk0.ui0:816 dv0.uk0:119 asq0.vpad:1275 dtp0.sq0:582 dh0.tp0:18 dvi0.h0:914 pd.Y3:1570 aY4.xi5:1156 dV.z:422 dV.:127 aS2.d:-320 dzk2.S3:441 puBu.zk3:994 dui1.uBu:665 duk1.ui1:79 dv1.uk1:489 asq1.v1:951 dtp1.sq1:668 dh1.tp1:932 dvi1.h1:-26 pd.Y5:1563 aS4.d:-328 azk4.d:2130 puCu.zk5:936 dui2.uCu:870 duk2.ui2:-306 dv2.uk2:-798 asq2.v2:795 dtp2.sq2:949 dh2.tp2:289 dvi2.h2:593 dde.pop:2668 de.de:2906 dcs.dl:2320 dptr1.Bi:2865 aPa.rr:1281 dPp.P0:2358 dfm.fin:2314 dPq.fm:2409 dPr.np:2439 dPs.Pr:2612 ddlt.Pq:2811 dsel.ca1:2788 ddsel.sel:2915 dPV.dsel:2583 aD0.e:1605 aD1.e:215 dvown.U:516 dRL.PV:859 dPVh.PV:1006 dPVh.fk:1745 dn96.RL:889 dn48.n96:946 dn24.n48:898 dKm.n24:1056 dbad2.PV:500 dbad1.PV:1256 aE0.vi0:957 pd.zk1:1120 aE2.vi1:2503 pd.zk3:518 aAE0.d:1595 dE4.zk5:2853 aAE2.d:1174 dAE4.E5:1236 puAr.S1:1187 puAr.zk1:1685 dbrow0.uAr:1434 dK10.uk0:411 puBr.S3:2304 puBr.zk3:4469 dbrow1.uBr:2498 dK11.uk1:613 puCr.S5:2366 dbrow2.uCr:330 dK12.uk2:1370 puAf.uAr:2949 puAf.AE1:1121 dkey0.K10:-115 puBf.uBr:1036 puBf.AE3:2011 dkey1.K11:1390 dR.PVh:1709 puCf.uCr:1740 puCf.E5:3521 puCf.AE5:2637 dkey2.K12:332 dm96.key2:1334 dm48.m96:1350 dm24.m48:1855 dfin.m24:1339 dsi1.C63:908 dsi2.si1:999 dfk.si2:1290 dthr.e:1813 dP8.h0:837 dPm.DM:1946 pPbc.Pm:693 dPb.Pbc:1904 aP0a.e:1206 dP0.U:660 aflip.z:1397
-"""
-PLAN = """
-dpop.thr:1900 dU.fin:1946 pcnt.popc:1912 dxa0.cnt:1944 dxa1.xa0:1968 dnu0.nu0:-100 dsh0.nu0:-247 dt30.sh0:-78 dxi0.xa1:-381 dEQ0.pop:2050 dEQ1.pop:2056 dEQ2.pop:2084 dEQ3.pop:2056 dEQ4.pop:2074 dEQ5.pop:2080 dEQ6.pop:2088 dEQ7.pop:2092 dEQ8.pop:1563 dEQ9.pop:2104 dEQ10.pop:2110 dEQ11.pop:2116 pdup.EQ2:2147 pdup.EQ6:1926 pdup.EQ10:1950 adupb.dup:2102 pacc.pop:-30 pacc.LT15:-131 pacc.dupb:157 dsof.DUM:-18 dso.sof:-111 p.so:-52 dBi.fin:2000 dslt.fin:2006 dgg.fin:2019 ddd.gg:2018 dzsl.slt:2038 dzs3.LLd:1997 dzo.zs3:2036 az.z:1947 dnu1.nu1:130 dsh1.nu1:136 dt31.sh1:200 dxi2.xa1:155 aY0.xi0:137 aY1.xi1:737 aY2.xi2:219 aY3.xi3:457 pd.Y0:122 pd.Y1:266 p.z:-30 aS0.d:188 aS1.d:-192 dzk0.S0:239 dzk1.S1:269 puAu.zk1:298 dui0.uAu:-627 duk0.ui0:310 dv0.uk0:316 asq0.vpad:331 dtp0.sq0:319 dh0.tp0:345 dvi0.h0:328 pd.Y2:322 pd.Y3:238 aY4.xi4:506 dY5.xi5:518 dV.z:399 dV.:344 aS2.d:295 aS3.d:343 dzk2.S2:415 dzk3.S3:152 puBu.zk3:378 dui1.uBu:592 duk1.ui1:483 dv1.uk1:632 asq1.v1:489 dtp1.sq1:336 dh1.tp1:490 dvi1.h1:481 pd.Y4:920 pd.Y5:619 aS4.d:598 aS5.d:536 dzk4.S4:612 dzk5.S5:618 puCu.zk5:678 dui2.uCu:654 duk2.ui2:660 dv2.uk2:694 asq2.v2:444 dtp2.sq2:712 dh2.tp2:667 dvi2.h2:824 dnp.fin:2359 dde.pop:2136 de.de:2319 dAi.fin:2500 drr.Ai:2344 dpu.fin:2512 ddl.pu:2426 dcs.dl:2511 dptr1.Bi:2429 dPa.rr:2542 dPp.P0:2411 dfm.fin:2618 dPq.fm:2560 dPs.pu:2554 ddlt.Pq:2496 dsel.ca1:2522 ddsel.sel:2713 dPV.dsel:2497 dD0.e:212 dD1.e:136 dvown.U:92 dRL.PV:616 dPVh.PV:656 dPVh.fk:562 dn96.RL:662 dn48.n96:668 dn24.n48:674 dKm.n24:701 dbad2.PV:854 dbad1.PV:703 aE0.vi0:800 aE1.vi0:726 pd.zk0:681 pd.zk1:730 aE3.vi1:781 dE2.zk2:1120 pd.zk3:820 aAE0.d:772 aAE1.d:1002 dE4.zk4:1122 aE5.vi2:874 pd.zk5:508 aAE3.d:1226 dAE2.E2:1198 aAE4.E4:1731 aAE5.d:1229 puAr.S1:1340 puAr.zk1:1234 abrow0.uAr:1016 dK10.uk0:1168 puBr.S3:907 puBr.zk3:1370 abrow1.uBr:881 dK11.uk1:1172 puCr.S5:1246 puCr.zk5:1916 abrow2.uCr:1204 dK12.uk2:1519 puAf.uAr:1198 puAf.AE1:941 dkey0.K10:1243 puBf.uBr:1277 puBf.E2:1614 puBf.AE3:1314 dkey1.K11:1268 dR.PVh:1274 puCf.uCr:1190 puCf.AE5:1064 dkey2.K12:1575 dm96.key2:1262 dm48.m96:1353 dm24.m48:1253 dfin.m24:1137 dsi1.C63:1131 dsi2.si1:1406 dfk.si2:1412 dthr.e:1403 dP8.h0:1424 dPm.h0:1424 pPbc.Pm:1510 dPb.Pbc:1741 dP0a.e:1456 dP0.U:1460 aflip.z:1257
+dpop.thr:1938 dU.fin:1982 pcnt.popc:1136 dxa0.cnt:1777 dxa1.xa0:2018 dnu0.nu0:-237 dsh0.nu0:-493 dt30.sh0:-881 dxi0.xa1:-535 dEQ0.pop:1943 dEQ1.pop:2106 dEQ2.pop:2122 dEQ3.pop:2068 dEQ4.pop:2106 dEQ5.pop:2061 dEQ6.pop:2132 dEQ7.pop:2124 dEQ8.pop:1765 dEQ9.pop:2270 dEQ10.pop:2137 dEQ11.pop:1754 pdup.EQ2:2111 pdup.EQ6:2499 pdup.EQ10:1685 adupb.dup:1903 pacc.pop:-541 pacc.LT15:567 pacc.dupb:-410 dsof.DUM:-509 dso.sof:-396 p.so:-141 dBi.fin:2104 dslt.fin:2010 dgg.fin:1900 ddd.gg:1916 dzsl.slt:2072 dzs3.LLd:1968 dzo.zs3:2079 az.z:2030 dnu1.nu1:137 dsh1.nu1:331 dt31.sh1:42 dxi2.xa1:323 aY0.xi0:-987 aY1.xi1:984 aY2.xi3:258 pd.Y0:1145 pd.Y1:643 p.z:500 aS0.d:199 aS1.d:-940 dzk0.S0:280 dzk1.S1:-297 puAu.zk1:423 dui0.uAu:-193 duk0.ui0:451 dv0.uk0:-62 asq0.vpad:-123 dtp0.sq0:301 dh0.tp0:247 dvi0.h0:88 pd.Y3:1077 aY4.xi5:376 dV.z:-1689 dV.:-211 aS2.d:-754 dzk2.S3:-115 puBu.zk3:333 dui1.uBu:988 duk1.ui1:149 dv1.uk1:372 asq1.v1:273 dtp1.sq1:155 dh1.tp1:150 dvi1.h1:563 pd.Y5:1189 aS4.d:1148 azk4.d:-504 puCu.zk5:1291 dui2.uCu:701 duk2.ui2:1319 dv2.uk2:1205 asq2.v2:24 dtp2.sq2:1119 dh2.tp2:833 dvi2.h2:1012 dnp.fin:2789 dde.pop:2502 de.de:2521 dAi.fin:2559 drr.Ai:2119 dpu.fin:2554 ddl.pu:2278 dcs.dl:2337 dptr1.Bi:2138 aPa.rr:2572 dPp.P0:2521 dfm.fin:2975 dPq.fm:2527 dPs.pu:2609 ddlt.Pq:1898 dsel.ca1:2199 ddsel.sel:3757 dPV.dsel:2328 aD0.e:619 aD1.e:215 dvown.U:98 dRL.PV:678 dPVh.PV:1132 dPVh.fk:104 dn96.RL:482 dn48.n96:713 dn24.n48:930 dKm.n24:764 dbad2.PV:485 dbad1.PV:808 dE0.zk0:-1003 aE1.vi0:773 pd.zk1:1562 aE3.vi1:341 dE2.zk2:1039 pd.zk3:870 dAE0.E0:1746 aAE1.d:663 dE4.zk4:276 aE5.vi2:1518 pd.zk5:594 aAE3.d:923 dAE2.E2:1089 aAE4.E4:1921 aAE5.d:-258 puAr.S1:1460 puAr.zk1:1690 abrow0.uAr:1652 dK10.uk0:1129 puBr.S3:-383 puBr.zk3:2200 abrow1.uBr:1405 dK11.uk1:1085 puCr.S5:645 abrow2.uCr:632 dK12.uk2:1310 puAf.uAr:2419 puAf.E0:-927 puAf.AE1:1549 dkey0.K10:1221 puBf.uBr:1396 puBf.E2:1099 puBf.AE3:2729 dkey1.K11:1257 dR.PVh:981 puCf.uCr:1356 puCf.AE5:4 dkey2.K12:927 dm96.key2:1013 dm48.m96:1483 dm24.m48:2124 dfin.m24:850 dsi1.C63:1252 dsi2.si1:2289 dfk.si2:1729 dthr.e:1515 dP8.h0:2133 dPm.h0:1425 pPbc.Pm:1734 dPb.Pbc:2308 aP0a.e:1183 dP0.U:1282 aflip.z:1170
+dRa.PVh:1200 dRb.Ra:1200 dRc.Rb:1200 dRd.key1:1000 dRe.Rc:1000 dkey1.Re:1000 dm48.key2:1000
 """
 OFF = {x.split(":")[0]: 10 * int(x.split(":")[1]) for x in PLAN.split()}
 

@@ -1,15 +1,19 @@
+import math
 from concourse.bass import DstId, RemoteDMATransfer
 from concourse.mybir import AluOpType as A, AxisListType, ActivationFunctionType as F
 
 L, W, RO = 192, 4096, 10
 CFG = {
-    "XG": ["AA", "A", "A"],
-    "XP": "RRS",
-    "VG": ["DA", "DA", "BA"],
-    "sq": True, "brow": True, "rtp": False, "tiny": True, "zg": True, "pvp": False, "dupa": True, "pbm": True, "pre": True, "xs": [(0, 64), (64, 192)],
+    "pieces": [(0, "R", [(2, "A"), (2, "A"), (2, "A")], [(2, "A"), (2, "A"), (2, "B")]),
+               (12, "F", [(4, "D")], [(4, "D")]),
+               (6, "R", [(2, "A"), (2, "A"), (2, "A")], [(2, "A"), (2, "A"), (2, "B")])],
+    "xs": [(0, 64), (64, 192)],
+    "zact": "pf",
 }
-FP16W = True
-f32, bf, i32, u16 = "float32", "bfloat16", "int32", "uint16"
+f32, bf, f16, i32, u16 = "float32", "bfloat16", "float16", "int32", "uint16"
+XO = 16
+FLIP, HIST = 16, 17
+PW = 96
 
 
 def _sb(n, d):
@@ -17,50 +21,47 @@ def _sb(n, d):
 
 
 SCRATCH = {
-    "X": _sb(2 * W + 32, bf), "V": _sb(W + L, bf), "ZW": _sb(32 * L, bf),
-    "Y": _sb(3072, bf), "S": _sb(3072, bf), "E": _sb(3072, bf), "AE": _sb(3072, bf),
+    "X": _sb(XO + W + 32, bf), "V": _sb(W + L, bf), "ZW": _sb(27 * L, bf), "zp": _sb(11 * L, bf), "zm": _sb(L, bf),
+    "Y": _sb(3072, bf), "S": _sb(3072, bf), "Sh": _sb(3072, f16), "E": _sb(3072, bf), "AE": _sb(3072, bf),
     "nmi": _sb((6, 2, 16), i32), "cai": _sb((6, 2, 16), bf), "rti": _sb((6, 2, 16), bf), "wti": _sb(1, i32), "thi": _sb(1, i32),
     "src4": _sb((4, 6, 2, 16), f32), "tr": _sb(4 * L, f32),
-    "nB": _sb(L, f32), "ca1": _sb(L, f32), "rtB": _sb(L, f32), "thB": _sb(L, f32), "KS": _sb(L, f32),
+    "nB": _sb(L, f32), "ca1": _sb(L, f32), "rtB": _sb(L, f32), "thh": _sb(L, f16), "CA": _sb(L, f32),
+    "P4r": _sb(L, bf), "P4c": _sb(L, f32), "NR": _sb(L, bf), "Lf": _sb(L, bf), "Es": _sb(16, f32),
+    "y": _sb(L, bf), "sp": _sb(L, bf), "so_": _sb(L, bf), "OP": _sb(L, bf),
     "k37": _sb(L, f32), "kk": _sb(L, f32), "t192": _sb(L, f32), "i192": _sb(L, i32), "j192": _sb(L, i32),
     "one": _sb(160, f32), "IW": _sb(160, f32), "IW0": _sb(160, f32), "IW1": _sb(160, f32),
-    "Ib": _sb(128, bf), "nIb": _sb(128, bf), "pIb": _sb(128, bf), "NI": _sb(128, bf), "thh": _sb(L, "float16"), "Ph": _sb(L, "float16"), "I8k": _sb(128, f32),
-    "BO": _sb(128, f32), "BOb": _sb(128, bf), "B8": _sb(8, f32), "B8a": _sb(8, f32),
-    "G": _sb(144, bf), "Gn": _sb(144, bf), "GB2": _sb(144, bf), "GBn": _sb(144, bf), "G8k": _sb(144, bf),
-    "Wh": _sb(144, "float16" if FP16W else bf), "Wl": _sb(144, bf), "LT": _sb((16, 128), bf), "RT": _sb((16, 128), bf),
+    "Ib": _sb(128, bf), "nIb": _sb(128, bf), "pIb": _sb(128, bf), "NI": _sb(128, bf), "n16": _sb(128, bf), "Ph": _sb(16, f16), "I8k": _sb(128, bf),
+    "BO": _sb(128, f32), "BOb": _sb(128, bf), "WB": _sb(128, f16), "B8": _sb(8, f32),
+    "G": _sb(144, bf), "Gn": _sb(144, bf), "Gh": _sb(144, bf), "GB2": _sb(144, bf), "GBn": _sb(144, bf), "G8k": _sb(144, bf),
+    "Wh": _sb(144, f16), "LT": _sb((16, 128), bf), "RT": _sb((16, 128), bf),
+    "CI": _sb((2, PW), bf), "ones": _sb(128, bf), "N64": _sb(PW, bf),
     "DM": _sb(L, f32), "pi": _sb(1, i32), "pj": _sb(1, i32), "PM": _sb(1, f32), "hf": _sb(2, f32), "wf": _sb(4, f32), "wi": _sb(2, i32),
-    "thf": _sb(1, f32), "C63": _sb(1, f32), "ltm": _sb(16, f32),
+    "thf": _sb(1, f32), "CF": _sb(1, f32), "ltm": _sb(16, f32),
     "c16": _sb(12, f32), "c1": _sb(12, f32), "LL": _sb(12, f32), "DUM": _sb(12, f32), "LLd": _sb(12, f32), "KQ": _sb(12, i32), "QF": _sb(12, f32), "t12": _sb(12, f32),
     "QL": _sb(12, u16), "DL": _sb(6, u16), "EL": _sb(12, u16), "PERM": _sb(12, u16), "INV": _sb(12, u16),
-    "U": _sb(16 * (RO + 1), i32), "xi": _sb(L, u16), "nu": _sb(L, i32), "sh": _sb(L, i32), "t3": _sb(L, f32),
-    "ui": _sb(L, i32), "uk": _sb(L, i32), "v": _sb(208, f32), "sq": _sb(208, f32), "tp": _sb(208, i32), "h": _sb(208, i32), "vi": _sb(208, u16),
-    "K1": _sb(L, f32), "key": _sb(L, f32), "brow": _sb(L, bf), "bad1": _sb(L, bf), "bad2": _sb(L, bf),
-    "PV": _sb(L, f32), "PVh": _sb(96, f32), "R": _sb(96, f32), "m96": _sb(96, f32), "m48": _sb(48, f32), "m24": _sb(24, f32), "fin": _sb(12, i32),
-    "RL": _sb(L, f32), "n96": _sb(96, f32), "n48": _sb(48, f32), "n24": _sb(24, f32), "Km": _sb(16, f32),
-    "sel": _sb(L, f32), "dsel": _sb(L, f32), "D": _sb(24, f32), "e": _sb(12, f32), "thr": _sb(12, f32),
-    "sm": _sb(16 * 24, f32), "si": _sb(16 * 6, i32), "popb": _sb(16, f32), "xa": _sb(2, f32), "zo": _sb(12, u16),
-    "P8": _sb(16, f32), "Pm": _sb(L, f32), "Pb": _sb(L, "float16"), "EQ": _sb((12, 208), bf), "dupb": _sb(L, bf),
+    "U": _sb(16 * (RO + 1), i32), "xi": _sb(L, u16), "nu": _sb(L, f32), "t3": _sb(L, i32), "sh": _sb(L, i32),
+    "ru": _sb(3 * PW, f32), "uf": _sb(3 * PW, f32), "sq": _sb(3 * PW, f32), "tp": _sb(3 * PW, i32), "h": _sb(3 * PW, i32), "vi": _sb(L, u16),
+    "K1": _sb(L, f32), "key": _sb(3 * 112, f32), "brow": _sb(L, bf), "bad1": _sb(L, bf), "bad2": _sb(L, bf), "fin": _sb(12, i32),
+    "SK": _sb((2, 96), f32), "Dl": _sb(64, f32), "Dm": _sb(64, f32), "D": _sb(24, f32), "e": _sb(12, f32),
+    "sm": _sb(16 * 12, f32), "si": _sb(16 * 3, i32), "popb": _sb(16, bf), "xa": _sb(2, f32), "zo": _sb(12, u16),
+    "P8": _sb(16, f32), "Pb": _sb(L, f16), "EQ": _sb((12, 208), bf), "dupb": _sb(L, bf),
     "so": _sb(16 * RO, u16), "rz": _sb(2 * RO * L, bf), "ro": _sb(2 * RO * 16, u16),
-    "ol": _sb((6, 2, 16), bf), "op": _sb(L, f32),
+    "ol": _sb((6, 2, 16), bf),
     "dA": ("psum", [128, 1024], f32), "dB": ("psum", [128, 1024], f32),
     "uA": ("psum", [128, 512], f32), "uB": ("psum", [128, 512], f32), "uC": ("psum", [128, 512], f32), "mP": ("psum", [128, 512], f32),
 }
 NDMA = 16
 SEMAPHORES = ["dve", "act", "pe", "pool", "sent"] + ["d%d" % i for i in range(NDMA)] + ["r%d_%d" % (s, j) for s in range(1, RO) for j in range(2)]
 
-FIX, RL = 12.0, 2300.0
-CY, PC, GA, SC, HOP = 1.0, 0.5, 1.65, 4.0, 210.0
+SETS = [{"FIX": 6.0, "RL": 2000.0, "CY": 0.85, "PC": 0.43, "GA": 1.56, "SC": 3.8, "HOP": 150.0, "WT": 1.0},
+        {"FIX": 10.0, "RL": 3000.0, "CY": 1.2, "PC": 0.6, "GA": 1.9, "SC": 5.0, "HOP": 150.0, "WT": 0.6},
+        {"FIX": 6.0, "RL": 2500.0, "CY": 0.9, "PC": 0.45, "GA": 1.2, "SC": 2.5, "HOP": 220.0, "WT": 0.8}]
+PAR = dict(SETS[0], LOOK=300.0, SLACK=40.0, ROUNDS=3, R1=20000, R2=4000, HEAT=150.0)
 
 
 def build(T, topo, core, rank):
     ops, lastw, readers, bank, step = [], {}, {}, {}, [-1]
-
-    def kind(ts_):
-        x = ts_[0] if ts_ else ""
-        if x[:2] in ("dA", "dB") and len(x) == 3:
-            return "d"
-        y = x.rstrip("0123456789")
-        return y if y in ("U", "z", "so") else x
+    FIX, RL, CY, PC, GA, SC = (PAR[k] for k in ("FIX", "RL", "CY", "PC", "GA", "SC"))
 
     def add(eng, fn, cost, r=(), w=(), px=(), lat=0.0, ext=(), soft=(), dma=False):
         i = len(ops)
@@ -86,10 +87,7 @@ def build(T, topo, core, rank):
         deps.discard(i)
         if eng in ("dve", "act"):
             cost += FIX
-        if eng == "pool" and lat:
-            lat = RL
-        ops.append(dict(eng=eng, fn=fn, cost=cost, deps=deps, lat=lat, ext=list(ext), soft=list(soft), dma=dma, step=step[0],
-                        cls=eng[0] + kind(w[:1]) + "." + kind(r[-1:])))
+        ops.append(dict(eng=eng, fn=fn, cost=cost, deps=deps, lat=lat, ext=list(ext), soft=list(soft), dma=dma, step=step[0], name=(list(w) + [""])[0]))
         return i
 
     def n_of(ap):
@@ -121,14 +119,23 @@ def build(T, topo, core, rank):
             fn = lambda g: g.vector.tensor_tensor(out, win.indirect(off), b, o)
         return add("dve", fn, (50 / 0.83 + n_of(out) * GA) * CY, r, w)
 
-    def ag(out, win, off, r, w):
-        return add("act", lambda g: g.scalar.activation(out, win.indirect(off), F.Copy), (65 / 0.83 + n_of(out) * GA) * CY, r, w)
+    def ag(out, win, off, r, w, bias=None):
+        if bias is None:
+            fn = lambda g: g.scalar.activation(out, win.indirect(off), F.Copy)
+        else:
+            fn = lambda g: g.scalar.activation(out, win.indirect(off), F.Identity, bias=bias)
+        return add("act", fn, (65 / 0.83 + n_of(out) * GA) * CY, r, w)
 
     def ms(ap, val, w):
         return add("dve", lambda g: g.vector.memset(ap, val), vcost(n_of(ap), 0.5), (), w)
 
     def ac(out, a, func, r, w, bias=0.0, scale=1.0, px=()):
-        return add("act", lambda g: g.scalar.activation(out, a, func, bias=bias, scale=scale), max(64, n_of(out)) * CY + 40, r, w, px)
+        return add("act", lambda g: g.scalar.activation(out, a, func, bias=bias, scale=scale), max(64, n_of(out)) * CY, r, w, px)
+
+    def lin(on_act, out, a, mul, c, r, w):
+        if on_act:
+            return ac(out, a, F.Identity, r, w, bias=c, scale=mul)
+        return ts(out, a, mul, c, A.mult, A.add, r, w, 0.5)
 
     def mm(lst, r, w, px):
         def fn(g):
@@ -139,6 +146,9 @@ def build(T, topo, core, rank):
 
     def grp(items):
         return [(o, a, b, i == 0, i == len(items) - 1, sl) for i, (o, a, b, sl) in enumerate(items)]
+
+    def more(items, stop=False):
+        return [(x[0], x[1], x[2], False, stop and i == len(items) - 1, False) for i, x in enumerate(items)]
 
     def dma(q, out, a, nbytes, r, w):
         fn = (lambda g: g.sync.dma_start(out, a)) if q == "sp" else (lambda g: g.scalar.dma_start(out, a))
@@ -160,6 +170,9 @@ def build(T, topo, core, rank):
     def zs(k):
         return T.ZW[:, k * L:(k + 1) * L]
 
+    def zp(k):
+        return T.zp[:, k * L:(k + 1) * L]
+
     def sm(i):
         return T.sm[:, 16 * i:16 * i + 12]
 
@@ -168,30 +181,30 @@ def build(T, topo, core, rank):
 
     UB = [(T.uA, "uA"), (T.uB, "uB"), (T.uC, "uC")]
     DB = [(T.dA, ("dA0", "dA1")), (T.dB, ("dB0", "dB1"))]
-    n37 = T.uC[:, 320:512]
-    M23, M28 = 1.5 * 2.0 ** 23, 1.5 * 2.0 ** 28
-    BIG = 2.0 ** 24
+    PCS = [(b0, sum(n for n, _ in xu), xm, xu, vu) for (b0, xm, xu, vu) in CFG["pieces"]]
+    M23, M28, M35 = 1.5 * 2.0 ** 23, 1.5 * 2.0 ** 28, 1.5 * 2.0 ** 35
+    BIG, H1, S1 = 2.0 ** 24, 2.0 ** 18, 2.0 ** 13
+    W0 = 12 * PCS[0][1]
 
-    dma("sp", T.X[:, 0:W], T.xt[:], 1 << 20, (), ["X0"])
     dma("act", T.nmi[:], T.nm[:], 98304, (), ["nmi"])
-    dma("act", zs(21), T.z0[:], 49152, (), ["z0"])
-    dma("act", T.wti[:], T.wt[:], 512, (), ["wti"])
+    dma("sp", zp(0), T.z0[:], 49152, (), ["zp0"])
+    dma("sp", T.wti[:], T.wt[:], 512, (), ["wti"])
     dma("act", T.cai[:], T.ca[:], 49152, (), ["cai"])
-    dma("act", T.rti[:], T.rt[:], 49152, (), ["rti"])
+    dma("sp", T.rti[:], T.rt[:], 49152, (), ["rti"])
     dma("act", T.thi[:], T.th[:], 512, (), ["thi"])
+    dma("sp", T.X[:, XO:XO + W], T.xt[:], 1 << 20, (), ["X0"])
+    dma("act", T.X[:, XO + W:], T.xt[:, 0:32], 1 << 20, (), ["X1"])
     dma("sp", T.V[:, 0:W], T.vt[:], 2 << 20, (), ["V"])
-    dma("sp", T.X[:, W:2 * W], T.xt[:], 3 << 20, (), ["X1"])
-    dma("sp", T.X[:, 2 * W:2 * W + 32], T.xt[:, 0:32], 3 << 20, (), ["X2"])
 
     io(T.pi[:], [[0, 1]], 0, 1, ["pi"], fl=False)
     ms(T.one[:], 1.0, ["one"])
     af(T.IW[:], T.one[:], [[-1, 160]], A.is_equal, 16, 1, ["one"], ["IW"])
-    af(T.B8a[:], T.one[:, 0:8], [[-16, 8]], A.is_ge, 0, 1, ["one"], ["B8a"])
-    af(T.B8[:], T.B8a[:], [[16, 8]], A.is_ge, 15, -1, ["B8a"], ["B8"])
+    af(T.B8[:], T.one[:, 0:8], [[-16, 8]], A.is_ge, 0, 1, ["one"], ["B8"])
+    af(T.B8[:], T.B8[:], [[16, 8]], A.is_ge, 15, -1, ["B8"], ["B8"])
     io(T.c1[:], [[1, 12]], 0, 0, ["c1"])
     io(T.c16[:], [[16, 12]], 0, 0, ["c16"])
     io(T.k37[:], [[37, 16], [0, 12]], 0, 0, ["k37"])
-    io(T.kk[:], [[4096, 16], [0, 12]], 0, 0, ["kk"])
+    io(T.kk[:], [[8192, 16], [0, 12]], (63 << 18) + 2048, 0, ["kk"])
     io(T.DM[:], [[0, 12], [1, 16]], 0, 0, ["DM"])
     io(T.ltm[:], [[1, 16]], 0, 0, ["ltm"])
     ts(T.pj[:], T.pi[:], 15, None, A.bitwise_and, None, ["pi"], ["pj"])
@@ -203,22 +216,16 @@ def build(T, topo, core, rank):
     ts(T.IW1[:], T.IW[:], T.hf[:, 1:2], None, A.mult, None, ["IW", "hf1"], ["IW1"])
     ms(T.G[:], 0.0, ["G"])
     cp(T.G[:, 15:143:16], T.B8[:], ["B8"], ["G"])
-    if FP16W:
-        ts(T.wf[:, 0:1], T.wti[:], 2048.0, -4096.0, A.is_ge, A.mult, ["wti"], ["wf0"])
-        tt(T.wf[:, 1:2], T.wf[:, 0:1], T.wti[:], A.add, ["wf0", "wti"], ["wf1"])
-        ts(T.Wh[:], T.G[:], T.wf[:, 1:2], None, A.mult, None, ["G", "wf1"], ["Wh"], 0.5)
-        WS = [T.Wh]
-    else:
-        ts(T.wi[:, 0:1], T.wti[:], 4032, None, A.bitwise_and, None, ["wti"], ["wi0"])
-        ts(T.wi[:, 1:2], T.wti[:], 63, None, A.bitwise_and, None, ["wti"], ["wi1"])
-        cp(T.wf[:, 0:2], T.wi[:], ["wi0", "wi1"], ["wf0"])
-        ts(T.Wh[:], T.G[:], T.wf[:, 0:1], None, A.mult, None, ["G", "wf0"], ["Wh"], 0.5)
-        ts(T.Wl[:], T.G[:], T.wf[:, 1:2], None, A.mult, None, ["G", "wf0"], ["Wl"], 0.5)
-        WS = [T.Wh, T.Wl]
-    z0 = zs(21)
-    mm(grp([(T.uA[:, 0:12], Wm[:, sl(m)], T.ZW[:, 21 * L + m:22 * L:16], False) for m in range(16) for Wm in WS]), ["Wh", "Wl", "z0"], ["uAu"], ["uA"])
-    cp(si(0), T.uA[:, 0:12], ["uAu"], ["si0"], px=["uA"])
+    af(T.BO[:], T.one[:, 0:128], [[-16, 8], [0, 16]], A.is_ge, 0, 1, ["one"], ["BO"])
+    af(T.BO[:], T.BO[:], [[16, 8], [0, 16]], A.is_ge, 15, -1, ["BO"], ["BO"])
+    ts(T.wf[:, 0:1], T.wti[:], 2048.0, -4096.0, A.is_ge, A.mult, ["wti"], ["wf0"])
+    tt(T.wf[:, 1:2], T.wf[:, 0:1], T.wti[:], A.add, ["wf0", "wti"], ["wf1"])
+    ts(T.Wh[:], T.G[:], T.wf[:, 1:2], None, A.mult, None, ["G", "wf1"], ["Wh"], 0.5)
+    ts(T.WB[:], T.BO[:], T.wf[:, 1:2], None, A.mult, None, ["BO", "wf1"], ["WB"])
+    mm(grp([(T.uA[:, 0:12], T.Wh[:, sl(m)], T.zp[:, m:L:16], False) for m in range(16)]), ["Wh", "zp0"], ["uAg"], ["uA"])
+    cp(si(0), T.uA[:, 0:12], ["uAg"], ["si0"], px=["uA"])
     ts(T.U[:, 0:12], si(0), 4095, None, A.bitwise_and, None, ["si0"], ["U0"])
+    ts(T.zm[:], zp(0), -64.0, None, A.add, None, ["zp0"], ["zm"], 0.5)
     ts(T.LL[:], T.c16[:], T.PM[:], None, A.add, None, ["c16", "PM"], ["LL"])
     ts(T.KQ[:], T.LL[:], -5.5, 1.0 / 12, A.add, A.mult, ["LL"], ["KQ"])
     ts(T.t12[:], T.KQ[:], -12.0, None, A.mult, None, ["KQ"], ["t12"])
@@ -235,74 +242,81 @@ def build(T, topo, core, rank):
             out += grp([(dst3(rho), IWS[rho][:, 16 - 16 * (ga - rho):144 - 16 * (ga - rho)], src4(ga), True) for ga in range(2)])
         return out
 
-    srcs = [(T.nmi, "nmi", T.nB, "nB"), (T.cai, "cai", T.ca1, "ca1"), (T.rti, "rti", T.rtB, "rtB"), (None, "thf", T.thB, "thB")]
+    srcs = [(T.nmi, "nmi", T.nB, "nB"), (T.cai, "cai", T.ca1, "ca1"), (T.rti, "rti", T.rtB, "rtB"), (None, "thf", T.thh, "thh")]
     cp(T.thf[:], T.thi[:], ["thi"], ["thf"])
     for a, (s, sn, d, dn) in enumerate(srcs):
         s4 = T.src4[:, a]
         if a == 0:
             cp(s4, s[:], [sn], ["s4%d" % a])
         elif a == 1:
-            ac(s4, s[:], F.Identity, [sn, "one"], ["s4%d" % a], bias=T.one[:, 0:1])
+            ac(s4, s[:], F.Identity, [sn], ["s4%d" % a], bias=1.0)
         elif a == 2:
-            ac(s4, s[:], F.Copy, [sn], ["s4%d" % a])
+            ac(s4, s[:], F.Identity, [sn], ["s4%d" % a], bias=1.0)
         else:
             ac(s4, T.cai[:], F.Identity, [sn, "cai"], ["s4%d" % a], bias=T.thf[:], scale=0.0)
         P, bk = DB[a // 2]
         c0 = 512 * (a % 2)
         b1 = [bk[a % 2]]
         lst = swap3(lambda rho: P[:, c0 + 96 * rho:c0 + 96 * rho + 96], lambda ga: T.src4[:, a, :, ga, :])
-        mm(lst, ["IW0", "IW1", "s4%d" % a], ["p4%d" % a], b1)
+        mm(lst, ["IW0", "IW1", "s4%d" % a], b1, b1)
         for rho in range(2):
-            ac(T.src4[:, a, :, rho, :], P[:, c0 + 96 * rho:c0 + 96 * rho + 96], F.Copy, ["p4%d" % a], ["s4%d" % a], px=b1)
+            ac(T.src4[:, a, :, rho, :], P[:, c0 + 96 * rho:c0 + 96 * rho + 96], F.Copy, b1, ["s4%d" % a], px=b1)
         add("dve", lambda g, a=a: g.vector.transpose(T.tr[:, a * L:(a + 1) * L], T.src4[:, a]), vcost(L, 1), ["s4%d" % a], ["tr%d" % a])
         gt(d[:], T.tr[:, a * L:(a + 1) * L], T.PERM[:], None, None, ["tr%d" % a, "PERM"], [dn])
         if a == 0:
             tt(T.i192[:], T.nB[:], T.k37[:], A.add, ["nB", "k37"], ["i192"])
             ts(T.j192[:], T.i192[:], 4095, None, A.bitwise_and, None, ["i192"], ["j192"])
-    ts(n37, T.j192[:], 15.5, None, A.add, None, ["j192"], ["n37"], px=["uC"])
+            ts(T.uB[:, 320:512], T.j192[:], 32.0, -131072.0, A.mult, A.add, ["j192"], ["C32"], px=["uB"])
     cp(T.Ib[:], T.IW[:, 16:144], ["IW"], ["Ib"])
     ts(T.nIb[:], T.IW[:, 16:144], -1.0, None, A.mult, None, ["IW"], ["nIb"])
     ts(T.Gn[:], T.G[:], -1.0, None, A.mult, None, ["G"], ["Gn"], 0.5)
-    ts(T.DL[:, 0:1], T.PM[:], 11.0, 12.0, A.min, A.add, ["PM"], ["DL0"])
-    cp(T.DL[:, 1:5], T.QF[:, 0:4], ["QF"], ["DL1"])
-    ms(T.v[:, 12:16], 0.0, ["vpad"])
-    ts(T.t192[:], T.ca1[:], -131072.0, 128.0 * 131072, A.mult, A.add, ["ca1"], ["t192"])
-    tt(T.KS[:], T.t192[:], T.kk[:], A.add, ["t192", "kk"], ["KS"])
-    for t in range(3):
-        cp(UB[t][0][:, 128:192], T.KS[:, 64 * t:64 * t + 64], ["KS"], ["KS%d" % t], px=[UB[t][1]])
-    if CFG["rtp"] and not CFG["pvp"]:
-        cp(T.uB[:, 320:512], T.rtB[:], ["rtB"], ["rtP"], px=["uB"])
+    ts(T.Gh[:], T.G[:], 0.5, None, A.mult, None, ["G"], ["Gh"], 0.5)
+    ts(sm(0), T.LL[:], float(W0), 12.0, A.is_ge, A.mult, ["LL"], ["sm0"])
+    tt(sm(1), sm(0), T.QF[:], A.add, ["sm0", "QF"], ["sm1"])
+    cp(T.DL[:], T.sm[:, 16:22], ["sm1"], ["DL"])
+    ms(T.sq[:], 0.0, ["sq0", "sq1", "sq2", "sqo"])
+    ac(T.t192[:], T.ca1[:], F.Identity, ["ca1"], ["t192"], bias=H1, scale=-H1)
+    for t, (b0, nb, xm, xu, vu) in enumerate(PCS):
+        bs = slice(12 * b0, 12 * (b0 + nb))
+        tt(UB[t][0][:, 36 * nb:48 * nb], T.t192[:, bs], T.kk[:, bs], A.add, ["t192", "kk"], ["KS%d" % t], px=[UB[t][1]])
+    ac(T.CA[:], T.ca1[:], F.Identity, ["ca1"], ["CA"], scale=H1)
+    ac(T.P4r[:], T.rtB[:], F.Exp, ["rtB"], ["P4r"], scale=-math.log(4.0))
+    ac(T.P4c[:], T.ca1[:], F.Exp, ["ca1"], ["P4c"], scale=-math.log(4.0))
     ac(T.pIb[:], T.IW[:, 16:144], F.Copy, ["IW"], ["pIb"], scale=-1024.0 * BIG)
     ac(T.NI[:], T.IW[:, 16:144], F.Copy, ["IW"], ["NI"], scale=-BIG)
+    ac(T.n16[:], T.IW[:, 16:144], F.Copy, ["IW"], ["n16"], scale=-16.0)
     ac(T.I8k[:], T.IW[:, 16:144], F.Copy, ["IW"], ["I8k"], scale=-8192.0)
     ac(T.GB2[:], T.G[:], F.Copy, ["G"], ["GB2"], scale=2 * BIG)
     ac(T.GBn[:], T.G[:], F.Copy, ["G"], ["GBn"], scale=-BIG)
     ac(T.G8k[:], T.G[:], F.Copy, ["G"], ["G8k"], scale=8192.0)
-    af(T.BO[:], T.one[:, 0:128], [[-16, 8], [0, 16]], A.is_ge, 0, 1, ["one"], ["BO"])
-    af(T.BO[:], T.BO[:], [[16, 8], [0, 16]], A.is_ge, 15, -1, ["BO"], ["BO"])
     ac(T.BOb[:], T.BO[:], F.Copy, ["BO"], ["BOb"])
-    ms(T.ZW[:, 16 * L:20 * L], 0.0, ["zpad"])
+    ms(T.X[:, 0:XO], 0.0, ["Xpad"])
     ms(T.V[:, W:W + L], 0.0, ["Vpad"])
-    cp(T.PV[:], T.ca1[:], ["ca1"], ["PV"])
-    cp(T.thh[:], T.thB[:], ["thB"], ["thh"])
     ms(T.e[:], 0.0, ["e"])
-    ms(sm(0), 0.0, ["ptr1"])
-    ms(T.popb[:, 12:13], -15.5 / 128, ["popc"])
+    ms(T.SK[:], 0.0, ["F0", "F1", "St0", "St1"])
+    ms(T.Dl[:], 0.0, ["Dl"])
+    ms(T.Lf[:], 0.0, ["Lf"])
+    ms(T.popb[:, 12:13], -15.75 / 128, ["popc"])
+    ms(T.ones[:], 1.0, ["ones"])
+    ms(T.N64[:], -64.0, ["N64"])
+    ms(T.CI[:, 0], -2048.0, ["CI0"])
+    ms(T.CI[:, 1], -15.0 / 64, ["CI1"])
     ts(T.DM[:], T.DM[:], T.PM[:], None, A.is_equal, None, ["DM", "PM"], ["DM"])
     ts(T.ltm[:], T.ltm[:], T.PM[:], 8192.0, A.is_gt, A.mult, ["ltm", "PM"], ["ltm"])
     for m in range(1, 16):
         ac(T.LT[:, m], T.G[:, sl(m)], F.Copy, ["G", "ltm"], ["LT%d" % m], scale=T.ltm[:, m:m + 1])
-    if CFG["pbm"]:
-        for m in range(16):
-            ac(T.RT[:, m], T.BO[:], F.Copy, ["BO", "DM"], ["RT%d" % m], scale=T.DM[:, m:m + 1])
+    for m in range(16):
+        ac(T.RT[:, m], T.BO[:], F.Copy, ["BO", "DM"], ["RT%d" % m], scale=T.DM[:, m:m + 1])
     cp(T.EL[:], T.c1[:], ["c1"], ["EL"])
     ts(T.LLd[:], T.LL[:], 1.0 / L, None, A.mult, None, ["LL"], ["LLd"])
     ts(T.DUM[:], T.LL[:], W - 10240.0, None, A.add, None, ["LL"], ["DUM"])
     ts(T.t12[:, 0:1], T.PM[:], 12.0, None, A.mult, None, ["PM"], ["t12"])
     ts(T.INV[:], T.c1[:], T.t12[:, 0:1], None, A.add, None, ["c1", "t12"], ["INV"])
     cp(T.wf[:, 2:3], T.wti[:], ["wti"], ["wf2"])
-    mm(grp([(T.mP[:, 400:401], T.BO[:], T.wf[:, 2:3], True)]), ["BO", "wf2"], ["cnt"], ["mP"])
-    ts(T.C63[:], T.mP[:, 400:401], 63.0, None, A.mult, None, ["cnt"], ["C63"], px=["mP"])
+    mm(grp([(T.mP[:, 400:401], T.BO[:], T.wf[:, 2:3], True)]), ["BO", "wf2"], ["mPg"], ["mP"])
+    ts(T.wi[:, 0:1], T.mP[:, 400:401], 63.0, None, A.mult, None, ["mPg"], ["wi0"], px=["mP"])
+    ts(T.wi[:, 1:2], T.wi[:, 0:1], 4095, None, A.bitwise_and, None, ["wi0"], ["wi1"])
+    ts(T.CF[:], T.wi[:, 1:2], 32 * H1 + FLIP * S1 + 4096 + 592, None, A.add, None, ["wi1"], ["CF"])
 
     N = len(T.cores)
     peers = [T.cores[(rank + d) % N] for d in (1, 3)]
@@ -325,9 +339,8 @@ def build(T, topo, core, rank):
         return fn
 
     dn, later = [0], []
-    ptr1, npu = sm(0), sm(1)
 
-    def pieces(c0, n):
+    def cuts(c0, n):
         out = []
         while n > 0:
             k = min(n, L - c0 % L)
@@ -335,368 +348,288 @@ def build(T, topo, core, rank):
             c0, n = c0 + k, n - k
         return out
 
-    def units(c0, modes):
-        n = 1024 // len(modes)
-        return [(c0 + i * n, n, x) for i, x in enumerate(modes)]
+    def units(b0, lst):
+        out = []
+        for n, x in lst:
+            out.append((b0, n, x))
+            b0 += n
+        return out
 
-    def tk(name, u0, un):
-        return ["%s%d" % (name, x) for x in range(u0 // 512, (u0 + un) // 512)]
+    def tk(name, b0, nb):
+        return ["%s%d" % (name, x) for x in range(b0, b0 + nb)]
 
     def tile(un):
-        if un == 1024:
+        k = (un + 511) // 512
+        if k == 2:
             dn[0] += dn[0] % 2
         b = dn[0] % 4
-        dn[0] += un // 512
+        dn[0] += k
         P, names = DB[b // 2]
-        return P, 512 * (b % 2), list(names[b % 2:b % 2 + un // 512])
+        return P, 512 * (b % 2), list(names[b % 2:b % 2 + k])
 
-    def lin12(out, a, mul, c, r, w):
-        if CFG["tiny"]:
-            return ac(out, a, F.Identity, r, w, bias=c, scale=mul)
-        return ts(out, a, mul, c, A.mult, A.add, r, w)
+    def sums(o, Gm, B, c0, n):
+        return [(o, Gm[:, sl(m)], B[:, c0 + m:c0 + n:16], False) for m in range(16)]
 
+    def least_return(src, tok):
+        mm(grp([(T.mP[:, 432:480], T.Ib[:], src[:, 48 * k:48 * k + 48], False) for k in range(4)]), ["Ib", tok], ["mPg"], ["mP"])
+        ac(T.so_[:, 0:48], T.mP[:, 432:480], F.Copy, ["mPg"], ["so_"], px=["mP"])
+        mm(grp([(T.mP[:, 420:432], T.Ib[:], T.so_[:, 12 * k:12 * k + 12], False) for k in range(4)]), ["Ib", "so_"], ["mPg"], ["mP"])
+        ac(T.Es[:, 0:12], T.mP[:, 420:432], F.Copy, ["mPg"], ["Es"], px=["mP"])
+        gt(T.bad2[:], T.Es[:, 0:12], T.QL[:], T.P4c[:], A.is_gt, ["Es", "QL", "P4c"], ["bad2"])
+
+    def writes(full, o, z, zt, zsend, s):
+        mm(full[:2], ["Ib", "I8k", "Ph", "pop"], ["uCg"], ["uC"])
+        mm(full[2:17], ["EQ%d" % q for q in range(12)] + ["LT%d" % m for m in range(1, 16)] + ["uCg"], ["acc1"], ["uC"])
+        mm(full[17:], ["G8k", "dupb", "uCg", "acc1"], ["acc"], ["uC"])
+        tt(sm(4), o, T.DUM[:], A.min, ["acc", "DUM", "uCg"], ["sof"], px=["uC"])
+        so = T.so[:, 16 * s:16 * s + 12]
+        ts(so, sm(4), 10240.0, None, A.add, None, ["sof"], ["so%d" % s])
+        osend = add("pool", send(so, lambda j, s=s: T.ro[:, (2 * s + j) * 16:(2 * s + j) * 16 + 12], s), 1000.0, ["so%d" % s], (), lat=RL)
+        sc = (50 / 0.83 + L * SC) * CY
+        add("dve", lambda g: g.vector.tensor_copy(T.V[:].indirect(so), z), sc, ["so%d" % s, zt], ["V", "Vpad"])
+        for j in range(2):
+            a = 2 * s + j
+            add("dve", lambda g, a=a: g.vector.tensor_copy(T.V[:].indirect(T.ro[:, 16 * a:16 * a + 12]), T.rz[:, a * L:(a + 1) * L]), sc, (), ["V", "Vpad"],
+                ext=[("r%d_%d" % (s, j), 2 * neng[j])], soft=[zsend, osend])
+
+    least_return(T.P4r, "P4r")
     for s in range(RO):
         Uc, ut = T.U[:, 16 * s:16 * s + 12], "U%d" % s
-        z, zt = zs(21 + s), "z%d" % s
-        step[0] = s
+        zt = "zp%d" % s
+        last = s == RO - 1
+        step[0], dn[0] = s, 0
         for i, (a, b) in enumerate(CFG["xs"]):
-            nu, sh, xi = "nu%d" % i, "sh%d" % i, ["xi%d" % x for x in range(a // 32, b // 32)]
-            gt(T.nu[:, a:b], Uc, T.QL[:, a // 16:b // 16], T.nB[:, a:b], A.mult, [ut, "QL", "nB", nu], [nu])
-            ts(T.sh[:, a:b], T.nu[:, a:b], 5, 4095, A.arith_shift_right, A.bitwise_and, [nu], [sh])
+            gt(T.nu[:, a:b], Uc, T.QL[:, a // 16:b // 16], T.nB[:, a:b], A.mult, [ut, "QL", "nB"], ["nu%d" % i])
+            tt(T.t3[:, a:b], T.nu[:, a:b], T.uB[:, 320 + a:320 + b], A.add, ["C32", "nu%d" % i], ["t3%d" % i], px=["uB"])
+            ts(T.sh[:, a:b], T.t3[:, a:b], 5, 4095, A.arith_shift_right, A.bitwise_and, ["t3%d" % i], ["sh%d" % i])
             if s == 0:
-                tt(T.nu[:, a:b], T.sh[:, a:b], T.j192[:, a:b], A.add, ["j192", sh], [nu])
-                ts(T.sh[:, a:b], T.nu[:, a:b], 4095, None, A.bitwise_and, None, [nu], [sh])
-                cp(T.xi[:, a:b], T.sh[:, a:b], [sh], xi)
+                ts(T.xi[:, a:b], T.sh[:, a:b], float(XO), None, A.add, None, ["sh%d" % i], ["xi%d" % i])
             else:
-                tt(T.t3[:, a:b], T.sh[:, a:b], T.uC[:, 320 + a:320 + b], A.add, ["n37", sh], ["t3%d" % i], px=["uC"])
-                ts(T.xi[:, a:b], T.t3[:, a:b], T.xa[:, 0:1], T.xa[:, 1:2], A.add, A.subtract, ["t3%d" % i, "xa0", "xa1"], xi)
-        Xw, xt_ = (T.X[:, 0:W], ["X0"]) if s == 0 else (T.X[:], ["X0", "X1", "X2"])
+                ts(T.xi[:, a:b], T.sh[:, a:b], T.xa[:, 0:1], T.xa[:, 1:2], A.add, A.subtract, ["sh%d" % i, "xa0", "xa1"], ["xi%d" % i])
+
+        def xit(b0, nb):
+            return ["xi%d" % i for i, (a, b) in enumerate(CFG["xs"]) if a < 12 * (b0 + nb) and b > 12 * b0] + ["X0", "X1", "Xpad"]
+
         if later:
             writes(*later.pop())
-        lin12(T.D[:, 0:12], T.e[:], 19616.0, 19616.0 * (s + 1) + 1336 * 32, ["e"], ["D0"])
-        lin12(T.D[:, 12:24], T.e[:], 19616.0, 19616.0 * s + 1336 * 32, ["e"], ["D1"])
-        ts(T.v[:, 0:12], Uc, 592.0, None, A.add, None, [ut], ["vown"])
+        za = CFG["zact"]
         if s > 0:
-            zsend = add("pool", send(z, lambda j, s=s: T.rz[:, (2 * s + j) * L:(2 * s + j + 1) * L], s), 1000.0, [zt], (), lat=2000.0)
-        for t in range(3):
-            c0, post = 1024 * t, CFG["XP"][t]
-            bs = slice(64 * t, 64 * t + 64)
-            if t == 1:
-                if CFG["pvp"] and s > 0:
-                    tt(T.RL[:], T.uB[:, 320:512], T.rtB[:], A.max, ["rtB", "PVp"], ["RL"], px=["uB"])
-                    tt(T.PVh[:], T.uB[:, 320:416], T.PV[:, 96:192], A.max, ["PV", "PVp"], ["PVh"], px=["uB"])
-                else:
-                    if CFG["rtp"] and not CFG["pvp"]:
-                        tt(T.RL[:], T.uB[:, 320:512], T.PV[:], A.max, ["rtP", "PV"], ["RL"], px=["uB"])
-                    else:
-                        tt(T.RL[:], T.rtB[:], T.PV[:], A.max, ["rtB", "PV"], ["RL"])
-                    if s > 0:
-                        tt(T.PVh[:], T.PV[:, 0:96], T.PV[:, 96:192], A.max, ["PV"], ["PVh"])
-            for (u0, un, mode) in units(c0, CFG["XG"][t]):
-                cs = slice(u0, u0 + un)
-                off = T.xi[:, u0 // 16:(u0 + un) // 16]
-                zk = T.ZW[:, cs]
-                if mode == "F":
-                    for (a, k) in pieces(u0, un):
-                        gt(T.Y[:, a:a + k], Xw, T.xi[:, a // 16:(a + k) // 16], T.ZW[:, (21 + s) * L + a % L:(21 + s) * L + a % L + k], A.subtract,
-                           xt_ + [zt] + tk("xi", u0, un), ["Y_%d" % a])
-                    yt = ["Y_%d" % a for (a, k) in pieces(u0, un)]
-                    src, px = T.Y[:, cs], ()
+            lin("p" in za, zp(s), T.zm[:], 1.0, 64.0, ["zm"], [zt])
+            zsend = add("pool", send(zp(s), lambda j, s=s: T.rz[:, (2 * s + j) * L:(2 * s + j + 1) * L], s), 1000.0, [zt], (), lat=RL)
+        if not last:
+            lin("h" in za, zs(HIST + s), T.zm[:], 1.0, 128.0, ["zm"], ["z%d" % s])
+        lin("f" in za, zs(FLIP), T.zm[:], -1.0, 63.0, ["zm"], ["flip"])
+        ac(T.D[:, 0:12], T.e[:], F.Identity, ["e"], ["D0"], bias=19616.0 * (1 - 32 * s) + 1336 * 32, scale=19616.0 / H1)
+        ac(T.D[:, 12:24], T.e[:], F.Identity, ["e"], ["D1"], bias=19616.0 * (-32 * s) + 1336 * 32, scale=19616.0 / H1)
+        ac(sm(2), T.e[:], F.Identity, ["e"], ["dp1"], bias=1.0 - 32 * s, scale=1.0 / H1)
+        ts(sm(5), Uc, 592.0, None, A.add, None, [ut], ["vown"])
+        ac(T.sq[:, W0:W0 + 12], sm(5), F.Square, ["vown"], ["sqo"])
+        SK, Ft, St, Sn = T.SK[:, s % 2], "F%d" % (s % 2), "St%d" % (s % 2), "St%d" % (1 - s % 2)
+        if s > 0:
+            ac(sm(3), T.e[:], F.Identity, ["e"], ["cap"], bias=BIG * (1 + 32 * s), scale=-64.0)
+            ac(sm(6), sm(5), F.Identity, ["vown", "CF"], ["fk"], bias=T.CF[:], scale=-1.0)
+            tt(sm(7), SK[:, 12:24], sm(3), A.max, [St, "cap"], ["fb"])
+            tt(T.key[:, 0:12], sm(7), sm(6), A.min, ["fb", "fk"], ["R0"])
+        else:
+            ac(T.key[:, 0:12], sm(5), F.Identity, ["vown", "CF"], ["R0"], bias=T.CF[:], scale=-1.0)
+        if not last:
+            ac(sm(8), sm(5), F.Identity, ["vown"], ["P0"], bias=(HIST + s) * S1 - 32 * H1 - 592)
+        for t, (b0, nb, xm, xu, vu) in enumerate(PCS):
+            c0, cn, w = L * b0, L * nb, 12 * nb
+            bs = slice(12 * b0, 12 * b0 + w)
+            Pu, ub = UB[t]
+            gp = ub + "g"
+            for (u0, un, mode) in units(b0, xu):
+                cs = slice(L * u0, L * (u0 + un))
+                off = T.xi[:, 12 * u0:12 * (u0 + un)]
+                Yt, St_, zkt = tk("Y", u0, un), tk("S", u0, un), tk("zk", u0, un)
+                if xm == "F":
+                    for k in range(u0, u0 + un):
+                        gt(T.Y[:, L * k:L * k + L], T.X[:], T.xi[:, 12 * k:12 * k + 12], T.zm[:], A.subtract, xit(k, 1) + ["zm"], ["Y%d" % k])
+                    ts(T.Sh[:, cs], T.Y[:, cs], 64.0 - 1.0 / 32, 2.0, A.max, A.mult, Yt, St_, 0.5)
+                    add("dve", lambda g, cs=cs: g.vector.tensor_tensor_scan(T.ZW[:, cs], T.Sh[:, cs], T.Y[:, cs], 0.0, A.max, A.subtract),
+                        vcost(L * un, 0.5), Yt + St_, zkt)
                 else:
                     if mode == "A":
-                        ag(T.Y[:, cs], Xw, off, xt_ + tk("xi", u0, un), tk("Y", u0, un))
+                        ag(T.Y[:, cs], T.X[:], off, xit(u0, un), Yt)
                     else:
-                        gt(T.Y[:, cs], Xw, off, None, None, xt_ + tk("xi", u0, un), tk("Y", u0, un))
-                    P, p0, px = tile(un)
-                    lst = []
-                    for a0 in range(u0, u0 + un, 512):
-                        lst += grp([(P[:, p0 + a0 - u0:p0 + a0 - u0 + 512], T.Ib[:], T.Y[:, a0:a0 + 512], False)] +
-                                   [(P[:, p0 + a - u0:p0 + a - u0 + k], T.nIb[:], T.ZW[:, (21 + s) * L + a % L:(21 + s) * L + a % L + k], False) for (a, k) in pieces(a0, 512)])
-                    mm(lst, ["Ib", "nIb", zt] + tk("Y", u0, un), px, px)
-                    src, yt = P[:, p0:p0 + un], px
-                St, zkt = tk("S", u0, un), tk("zk", u0, un)
-                if post == "R":
-                    ac(T.S[:, cs], src, F.Abs, yt, St, bias=0.25, px=px)
-                    ts(zk, T.S[:, cs], M23, -M23, A.add, A.add, St, zkt, 0.5)
-                else:
-                    ac(zk, src, F.Abs, yt, zkt, px=px)
-                    if post == "S":
-                        ac(T.S[:, cs], src, F.Sign, yt, St, bias=0.5, px=px)
-                    else:
-                        ts(T.S[:, cs], src, 0.0, None, A.is_ge, None, yt, St, 1.0 if px else 0.5, px=px)
-            rows = [(T.G, T.S), (T.Gn, T.ZW)] if post == "R" else [(T.G, T.S)]
-            lim = 8.0 if post == "P" else 0.0
-            St, zkt = tk("S", c0, 1024), tk("zk", c0, 1024)
-            Pu, ub = UB[t]
-            mm(grp([(Pu[:, 0:64], Wm[:, sl(m)], T.ZW[:, c0 + m:c0 + 1024:16], False) for m in range(16) for Wm in WS]), ["Wh", "Wl"] + zkt, [ub + "u"], [ub])
-            cp(T.ui[:, bs], Pu[:, 0:64], [ub + "u"], ["ui%d" % t], px=[ub])
-            ts(T.uk[:, bs], T.ui[:, bs], 4095, None, A.bitwise_and, None, ["ui%d" % t], ["uk%d" % t])
-            ws = slice(16 + 64 * t, 80 + 64 * t)
-            ts(T.v[:, ws], T.uk[:, bs], 592.0, None, A.add, None, ["uk%d" % t], ["v%d" % t])
-            own = t == 0
-            if own:
-                ws = slice(0, 80)
-            rv = ["v%d" % t] + (["vown", "vpad"] if own else [])
-            if CFG["sq"]:
-                ac(T.sq[:, ws], T.v[:, ws], F.Square, rv, ["sq%d" % t])
+                        gt(T.Y[:, cs], T.X[:], off, None, None, xit(u0, un), Yt)
+                    P, p0, px = tile(L * un)
+                    lst, a1 = [], L * u0
+                    for a0 in range(a1, a1 + L * un, 512):
+                        n = min(512, a1 + L * un - a0)
+                        lst += grp([(P[:, p0 + a0 - a1:p0 + a0 - a1 + n], T.Ib[:], T.Y[:, a0:a0 + n], False)] +
+                                   [(P[:, p0 + a - a1:p0 + a - a1 + k], T.nIb[:], T.zm[:, a % L:a % L + k], False) for (a, k) in cuts(a0, n)])
+                    mm(lst, ["Ib", "nIb", "zm"] + Yt, px, px)
+                    ac(T.S[:, cs], P[:, p0:p0 + L * un], F.Abs, px, St_, bias=-63.75, px=px)
+                    ts(T.ZW[:, cs], T.S[:, cs], M23, 64.0 - M23, A.add, A.add, St_, zkt, 0.5)
+            St_, zkt = tk("S", b0, nb), tk("zk", b0, nb)
+            pu, pr = Pu[:, 0:w], Pu[:, w:2 * w]
+            ps = slice(PW * t, PW * t + w)
+            wide = (w + (12 if t == 0 else 0) + 15) // 16 * 16
+            pw = slice(PW * t, PW * t + wide)
+            full = grp([(pu, T.Ib[:], T.CI[:, 0, 0:w], False), (pu, T.WB[:], T.N64[:, 0:w], False)] + sums(pu, T.Wh, T.ZW, c0, cn))
+            mm(full[:2], ["Ib", "WB", "N64", "CI0"], [gp, ub + "u"], [ub])
+            mm(full[2:], ["Wh", gp] + zkt, [ub + "u"], [ub])
+            ts(T.ru[:, ps], pu, M35, -M35, A.add, A.add, [ub + "u"], ["ru%d" % t], px=[ub])
+            tt(T.uf[:, ps], pu, T.ru[:, ps], A.subtract, [ub + "u", "ru%d" % t], ["uf%d" % t], px=[ub])
+            ac(T.sq[:, ps], T.uf[:, ps], F.Square, ["uf%d" % t], ["sq%d" % t], bias=2048.0 + 592)
+            gt(T.tp[:, pw], T.D[:], T.DL[:, 0:wide // 16] if t == 0 else T.QL[:, 0:wide // 16], T.sq[:, pw], A.add,
+               ["D0", "D1", "DL", "QL", "sq%d" % t] + (["sqo"] if t == 0 else []), ["tp%d" % t])
+            ts(T.h[:, pw], T.tp[:, pw], 5, 4095, A.arith_shift_right, A.bitwise_and, ["tp%d" % t], ["h%d" % t])
+            cp(T.vi[:, bs], T.h[:, ps], ["h%d" % t], ["vi%d" % t])
+            if xm == "R":
+                full = grp(sums(pr, T.G, T.S, c0, cn) + sums(pr, T.Gn, T.ZW, c0, cn))
+                mm(full[:16], ["G", ub + "u"] + St_, [gp, ub + "r"], [ub])
+                mm(full[16:], ["Gn", gp] + zkt, [ub + "r"], [ub])
+                ac(T.brow[:, bs], pr, F.Relu, [ub + "r"], ["brow%d" % t], bias=-4096.0, scale=-4.0, px=[ub])
             else:
-                tt(T.sq[:, ws], T.v[:, ws], T.v[:, ws], A.mult, rv, ["sq%d" % t])
-            gt(T.tp[:, ws], T.D[:], T.DL[:, 0:5] if own else T.QL[:, 4 * t:4 * t + 4], T.sq[:, ws], A.add,
-               ["D0", "D1", "DL0", "DL1", "QL", "sq%d" % t], ["tp%d" % t])
-            ts(T.h[:, ws], T.tp[:, ws], 5, 4095, A.arith_shift_right, A.bitwise_and, ["tp%d" % t], ["h%d" % t])
-            cp(T.vi[:, ws], T.h[:, ws], ["h%d" % t], ["vi%d" % t])
-            full = grp([(Pu[:, 64:128], Gm[:, sl(m)], B[:, c0 + m:c0 + 1024:16], False) for (Gm, B) in rows for m in range(16)])
-            mm(full[:16], ["G", ub + "u"] + St, [ub + "r"], [ub])
-            if len(full) > 16:
-                mm(full[16:], ["Gn"] + zkt, [ub + "r"], [ub])
-            if CFG["brow"]:
-                ac(T.brow[:, bs], Pu[:, 64:128], F.Relu, [ub + "r"], ["brow%d" % t], bias=4.0 * lim, scale=-4.0, px=[ub])
-            else:
-                ts(T.brow[:, bs], Pu[:, 64:128], lim, None, A.is_lt, None, [ub + "r"], ["brow%d" % t], px=[ub])
-            tt(T.K1[:, bs], Pu[:, 128:192], T.uk[:, bs], A.add, ["KS%d" % t, "uk%d" % t], ["K1%d" % t], px=[ub])
-        tt(T.n96[:], T.RL[:, 0:96], T.RL[:, 96:192], A.min, ["RL"], ["n96"])
-        tt(T.n48[:], T.n96[:, 0:48], T.n96[:, 48:96], A.min, ["n96"], ["n48"])
-        tt(T.n24[:], T.n48[:, 0:24], T.n48[:, 24:48], A.min, ["n48"], ["n24"])
-        tt(T.Km[:, 0:12], T.n24[:, 0:12], T.n24[:, 12:24], A.min, ["n24"], ["Km"])
-        gt(T.bad2[:], T.Km[:, 0:12], T.QL[:], T.PV[:], A.is_lt, ["Km", "QL", "PV"], ["bad2"])
-        ts(si(1), Uc, -1.0, T.C63[:], A.mult, A.add, [ut, "C63"], ["si1"])
-        ts(si(2), si(1), 4095, None, A.bitwise_and, None, ["si1"], ["si2"])
-        ts(sm(20), si(2), 131072.0, None, A.add, None, ["si2"], ["fk"])
+                mm(grp([(pr, T.Ib[:], T.CI[:, 1, 0:w], False)] + sums(pr, T.Gh, T.Sh, c0, cn)), ["Ib", "CI1", "Gh", ub + "u"] + St_, [gp, ub + "r"], [ub])
+                ts(T.ru[:, ps], pr, M23, -M23, A.add, A.add, [ub + "r"], ["ru%d" % t], px=[ub])
+                tt(T.brow[:, bs], pr, T.ru[:, ps], A.is_gt, [ub + "r", "ru%d" % t], ["brow%d" % t], px=[ub])
+            tt(T.K1[:, bs], Pu[:, 3 * w:4 * w], T.uf[:, ps], A.add, ["KS%d" % t, "uf%d" % t], ["K1%d" % t], px=[ub])
         if s > 0:
-            gt(T.bad1[:], ptr1, T.QL[:], T.PV[:], A.is_ge, ["ptr1", "QL", "PV"], ["bad1"])
-            tt(T.PVh[:, 0:12], T.PVh[:, 0:12], sm(20), A.max, ["PVh", "fk"], ["PVh"])
-            ts(T.thr[:], T.e[:], float(-s), 96.0 * 131072, A.is_gt, A.mult, ["e"], ["thr"])
-            ts(T.P8[:, 0:12], T.h[:, 0:12], -2048.0, None, A.add, None, ["h0"], ["P8"])
-            if CFG["pbm"]:
-                ts(T.Ph[:, 0:12], T.h[:, 0:12], -2048.0, None, A.add, None, ["h0"], ["Pm"])
-                mm([(T.mP[:, m:192:16], T.RT[:, m], T.Ph[:, 0:12], True, True, False) for m in range(16)], ["RT%d" % m for m in range(16)] + ["Pm"], ["Pbc"], ["mP"])
-            else:
-                gt(T.Ph[:], T.P8[:, 0:12], T.EL[:], T.DM[:], A.mult, ["P8", "EL", "DM"], ["Pm"])
-                mm(grp([(T.mP[:, 0:192], T.BOb[:], T.Ph[:], False)]), ["BOb", "Pm"], ["Pbc"], ["mP"])
-            cp(T.Pb[:], T.mP[:, 0:192], ["Pbc"], ["Pb"], px=["mP"])
-        else:
-            ms(T.PVh[:], 0.0, ["PVh"])
-            cp(T.PVh[:, 0:12], sm(20), ["fk"], ["PVh"])
-        ac(zs(20), z, F.Identity, [zt], ["flip"], bias=63.0, scale=-1.0)
-        lin12(sm(2), T.e[:], 131072.0, 131072.0 * (2 + 10 * s), ["e"], ["P0a"])
-        tt(sm(3), sm(2), Uc, A.add, ["P0a", ut], ["P0"])
-        for t in range(3):
-            c0 = 1024 * t
-            bs = slice(64 * t, 64 * t + 64)
+            ho = T.h[:, W0:W0 + 12]
+            ts(T.P8[:, 0:12], ho, -2048.0, None, A.add, None, ["h0"], ["P8"])
+            ts(T.Ph[:, 0:12], ho, -2048.0, None, A.add, None, ["h0"], ["Ph"])
+            mm([(T.mP[:, m:192:16], T.RT[:, m], T.Ph[:, 0:12], True, True, False) for m in range(16)], ["RT%d" % m for m in range(16)] + ["Ph"], ["mPg"], ["mP"])
+            cp(T.Pb[:], T.mP[:, 0:192], ["mPg"], ["Pb"], px=["mP"])
+        for t, (b0, nb, xm, xu, vu) in enumerate(PCS):
+            c0, cn, w = L * b0, L * nb, 12 * nb
+            bs = slice(12 * b0, 12 * b0 + w)
             Vw = T.V[:, 0:W]
             Pu, ub = UB[t]
-            o = Pu[:, 256:320]
-            pen = [(o, T.NI[:], T.thh[:, bs], False), (o, T.pIb[:], T.bad2[:, bs], False), (o, T.pIb[:], T.brow[:, bs], False)]
+            gp = ub + "g"
+            o = Pu[:, 2 * w:3 * w]
+            mm([(o, T.NI[:], T.thh[:, bs], True, False, False)], ["NI", "thh", ub + "r"], [gp, ub + "f"], [ub])
+            pen = [(o, T.pIb[:], T.bad2[:, bs]), (o, T.pIb[:], T.brow[:, bs])]
             if s > 0:
-                pen += [(o, T.pIb[:], T.bad1[:, bs], False)]
-            lin = []
-            for (u0, un, mode) in units(c0, CFG["VG"][t]):
-                cs = slice(u0, u0 + un)
-                off = T.vi[:, 16 + u0 // 16:16 + (u0 + un) // 16]
+                pen += [(o, T.pIb[:], T.bad1[:, bs]), (o, T.pIb[:], T.Lf[:, bs])]
+            mm(more(pen), ["NI", "pIb", "thh", "bad1", "bad2", "Lf", "brow%d" % t, gp], [ub + "p"], [ub])
+            for (u0, un, mode) in units(b0, vu):
+                cs = slice(L * u0, L * (u0 + un))
+                off = T.vi[:, 12 * u0:12 * (u0 + un)]
                 zkt, Et, At = tk("zk", u0, un), tk("E", u0, un), tk("AE", u0, un)
                 if mode in "BD":
                     gt(T.E[:, cs], Vw, off, T.ZW[:, cs], A.subtract, ["V", "vi%d" % t] + zkt, Et)
                     if mode == "B":
-                        ac(T.AE[:, cs], T.E[:, cs], F.Abs, Et, At, scale=0.5)
+                        ac(T.AE[:, cs], T.E[:, cs], F.Abs, Et, At, bias=32.0, scale=0.5)
                     else:
-                        ts(T.AE[:, cs], T.E[:, cs], 0.0, None, A.max, None, Et, At, 0.5)
-                        p0 = 256 + (u0 - c0) // 16
-                        lin.append(([(Pu[:, p0:p0 + un // 16], T.GBn[:, sl(m)], T.E[:, u0 + m:u0 + un:16], False) for m in range(16)], Et))
+                        ts(T.AE[:, cs], T.E[:, cs], -64.0, 32.0, A.max, A.add, Et, At, 0.5)
+                        p0 = 2 * w + 12 * (u0 - b0)
+                        mm(more(sums(Pu[:, p0:p0 + 12 * un], T.GBn, T.E, L * u0, L * un)), ["GBn", gp] + Et, [ub + "f"], [ub])
                 else:
                     ag(T.E[:, cs], Vw, off, ["V", "vi%d" % t], Et)
-                    P, p0, px = tile(un)
-                    lst = []
-                    for a0 in range(0, un, 512):
-                        lst += grp([(P[:, p0 + a0:p0 + a0 + 512], T.nIb[:], T.ZW[:, u0 + a0:u0 + a0 + 512], False),
-                                    (P[:, p0 + a0:p0 + a0 + 512], T.Ib[:], T.E[:, u0 + a0:u0 + a0 + 512], False)])
+                    P, p0, px = tile(L * un)
+                    lst, a1 = [], L * u0
+                    for a0 in range(0, L * un, 512):
+                        n = min(512, L * un - a0)
+                        lst += grp([(P[:, p0 + a0:p0 + a0 + n], T.nIb[:], T.ZW[:, a1 + a0:a1 + a0 + n], False),
+                                    (P[:, p0 + a0:p0 + a0 + n], T.Ib[:], T.E[:, a1 + a0:a1 + a0 + n], False)])
                     mm(lst, ["Ib", "nIb"] + Et + zkt, px, px)
-                    ac(T.AE[:, cs], P[:, p0:p0 + un], F.Abs, px, At, scale=0.5, px=px)
-            full = grp(pen + [x for (l, _t) in lin for x in l] + [(o, T.GB2[:, sl(m)], T.AE[:, c0 + m:c0 + 1024:16], False) for m in range(16)])
-            mm(full[:len(pen)], ["NI", "pIb", "thh", "bad1", "bad2", "brow%d" % t, ub + "u", ub + "r"], [ub + "f"], [ub])
-            for i, (l, Et) in enumerate(lin):
-                mm(full[len(pen) + 16 * i:len(pen) + 16 * i + 16], ["GBn"] + Et, [ub + "f"], [ub])
-            mm(full[-16:], ["GB2"] + tk("AE", c0, 1024), [ub + "f"], [ub])
-            tt(T.key[:, bs], o, T.K1[:, bs], A.min, [ub + "f", "K1%d" % t], ["key%d" % t], px=[ub])
-            if not CFG["pre"]:
-                if t == 1:
-                    tt(T.R[:], T.key[:, 0:96], T.PVh[:], A.max, ["key0", "key1", "PVh"], ["R"])
-            elif t == 0:
-                tt(T.R[:, 0:48], T.PVh[:, 0:48], T.PVh[:, 48:96], A.max, ["PVh"], ["Ra"])
-                tt(T.R[:, 48:96], T.key[:, 0:48], T.R[:, 0:48], A.max, ["key0", "Ra"], ["Rb"])
-                tt(T.m96[:, 0:24], T.R[:, 48:72], T.R[:, 72:96], A.max, ["Rb"], ["Rc"])
-            elif t == 1:
-                tt(T.m96[:, 24:48], T.key[:, 48:72], T.key[:, 72:96], A.max, ["key0", "key1"], ["Rd"])
-                tt(T.m96[:, 48:72], T.key[:, 96:120], T.m96[:, 0:24], A.max, ["key1", "Rc"], ["Re"])
-                tt(T.key[:, 96:120], T.m96[:, 24:48], T.m96[:, 48:72], A.max, ["Rd", "Re"], ["key1"])
-        if CFG["pre"]:
-            tt(T.m48[:], T.key[:, 96:144], T.key[:, 144:192], A.max, ["key1", "key2"], ["m48"])
-        else:
-            tt(T.m96[:], T.R[:], T.key[:, 96:192], A.max, ["R", "key1", "key2"], ["m96"])
-            tt(T.m48[:], T.m96[:, 0:48], T.m96[:, 48:96], A.max, ["m96"], ["m48"])
-        tt(T.m24[:], T.m48[:, 0:24], T.m48[:, 24:48], A.max, ["m48"], ["m24"])
-        tt(T.fin[:], T.m24[:, 0:12], T.m24[:, 12:24], A.max, ["m24"], ["fin"])
-        last = s == RO - 1
-        if last:
-            step[0] = RO
+                    ac(T.AE[:, cs], P[:, p0:p0 + L * un], F.Abs, px, At, bias=32.0, scale=0.5, px=px)
+            mm(more(sums(o, T.GB2, T.AE, c0, cn), True), ["GB2", gp, ub + "p"] + tk("AE", b0, nb), [ub + "f"], [ub])
+            k0 = 112 * t
+            tt(T.key[:, k0 + 12:k0 + 12 + w], o, T.K1[:, bs], A.min, [ub + "f", gp, "K1%d" % t], ["key%d" % t], px=[ub])
+            n = nb + 1
+            while n > 1:
+                hh = n // 2
+                if n > 2:
+                    dst, wt_ = T.key[:, k0:k0 + 12 * hh], ["key%d" % t, "R%d" % t]
+                elif t < 2:
+                    dst, wt_ = T.key[:, k0 + 112:k0 + 124], ["R%d" % (t + 1)]
+                else:
+                    dst, wt_ = T.fin[:], ["fin"]
+                tt(dst, T.key[:, k0:k0 + 12 * hh], T.key[:, k0 + 12 * (n - hh):k0 + 12 * n], A.max, ["key%d" % t, "R%d" % t], wt_)
+                n -= hh
         pop = T.popb[:, 0:12]
-        if s > 0:
-            tt(pop, T.fin[:], T.thr[:], A.is_lt, ["fin", "thr"], ["pop"])
-        else:
-            ms(pop, 0.0, ["pop"])
+        ts(pop, T.fin[:], 32 * H1, None, A.is_lt, None, ["fin"], ["pop"])
         if not last:
             ts(T.U[:, 16 * (s + 1):16 * (s + 1) + 12], T.fin[:], 4095, None, A.bitwise_and, None, ["fin"], ["U%d" % (s + 1)])
-            mm(grp([(T.mP[:, 400:413], T.one[:, 0:128], T.popb[:, 0:13], True)]), ["one", "pop", "popc"], ["cnt"], ["mP"])
-            add("dve", lambda g: g.vector.tensor_reduce(T.xa[:, 0:1], T.mP[:, 400:413], AxisListType.X, A.add), vcost(13, 1), ["cnt"], ["xa0"], ["mP"])
-            ts(T.xa[:, 1:2], T.xa[:, 0:1], M28, -M28, A.add, A.add, ["xa0"], ["xa1"])
+            mm(grp([(T.mP[:, 400:413], T.ones[:], T.popb[:, 0:13], False)]), ["ones", "pop", "popc"], ["mPg"], ["mP"])
+            add("dve", lambda g: g.vector.tensor_reduce(T.xa[:, 0:1], T.mP[:, 400:413], AxisListType.X, A.add), vcost(13, 1), ["mPg"], ["xa0"], ["mP"])
+            ts(T.xa[:, 1:2], T.xa[:, 0:1], M28, -(M28 + 32), A.add, A.add, ["xa0"], ["xa1"])
+        ts(si(1), T.fin[:], 13, 31, A.arith_shift_right, A.bitwise_and, ["fin"], ["slt"])
+        tt(sm(9), si(1), T.LLd[:], A.add, ["slt", "LLd"], ["zs3"])
+        ts(T.zo[:], sm(9), float(L), None, A.mult, None, ["zs3"], ["zo"])
+        zr = ["zo", "flip"] + tk("zk", 0, 16) + ["z%d" % x for x in range(s)]
+        if last:
+            ag(zp(RO), T.ZW[:, 0:(HIST + s) * L], T.zo[:], zr, ["zp%d" % RO], bias=-64.0)
+        else:
+            ag(T.zm[:], T.ZW[:, 0:(HIST + s) * L], T.zo[:], zr, ["zm"], bias=-128.0)
         if s > 0:
+            ts(sm(11), T.fin[:], 32 * H1, None, A.is_lt, None, ["fin"], ["popf"])
             for q in range(12):
-                ts(T.EQ[:, q, 0:L - 16 * q], T.Pb[:, 16 * q:L], T.P8[:, q:q + 1], T.popb[:, q:q + 1], A.is_equal, A.mult, ["Pb", "P8", "pop"], ["EQ%d" % q], 0.5)
+                ts(T.EQ[:, q, 0:L - 16 * q], T.Pb[:, 16 * q:L], T.P8[:, q:q + 1], T.sm[:, 176 + q:177 + q], A.is_equal, A.mult, ["Pb", "P8", "popf"], ["EQ%d" % q], 0.5)
             full = grp([(T.mP[:, 208 + 16 * q:384], T.BOb[:], T.EQ[:, q, 16:L - 16 * q], False) for q in range(11)])
             for a, b in ((0, 3), (3, 7), (7, 11)):
-                mm(full[a:b], ["BOb"] + ["EQ%d" % q for q in range(a, b)], ["dup"], ["mP"])
-            if CFG["dupa"]:
-                ac(T.dupb[:, 16:L], T.mP[:, 208:384], F.Copy, ["dup"], ["dupb"], px=["mP"])
-            else:
-                cp(T.dupb[:, 16:L], T.mP[:, 208:384], ["dup"], ["dupb"], px=["mP"])
-            o = T.uA[:, 192:204]
-            full = grp([(o, T.IW[:, 16:144], T.P8[:, 0:12], True), (o, T.I8k[:], pop, True)] +
+                mm(full[a:b], ["BOb"] + ["EQ%d" % q for q in range(a, b)] + ["mPg"] * (a > 0), ["dup"] + ["mPg"] * (a == 0), ["mP"])
+            ac(T.dupb[:, 16:L], T.mP[:, 208:384], F.Copy, ["dup", "mPg"], ["dupb"], px=["mP"])
+            o = T.uC[:, 300:312]
+            full = grp([(o, T.Ib[:], T.Ph[:, 0:12], False), (o, T.I8k[:], pop, False)] +
                        [(o, T.LT[:, m], T.EQ[:, :, m], False) for m in range(1, 16)] +
-                       [(T.uA[:, 193:204], T.G8k[:, sl(m)], T.dupb[:, 16 + m:L:16], False) for m in range(16)])
-            later.append((full, o, pop, z, zt, zsend, s))
-
-        def writes(full, o, pop, z, zt, zsend, s):
-            mm(full[:2], ["IW", "I8k", "P8", "pop"], ["acc"], ["uA"])
-            mm(full[2:17], ["EQ%d" % q for q in range(12)] + ["LT%d" % m for m in range(1, 16)], ["acc"], ["uA"])
-            mm(full[17:], ["G8k", "dupb"], ["acc"], ["uA"])
-            tt(sm(4), o, T.DUM[:], A.min, ["acc", "DUM"], ["sof"], px=["uA"])
-            so = T.so[:, 16 * s:16 * s + 12]
-            ts(so, sm(4), 10240.0, None, A.add, None, ["sof"], ["so%d" % s])
-            osend = add("pool", send(so, lambda j, s=s: T.ro[:, (2 * s + j) * 16:(2 * s + j) * 16 + 12], s), 1000.0, ["so%d" % s], (), lat=2000.0)
-            sc = (50 / 0.83 + L * SC) * CY
-            add("dve", lambda g, so=so, z=z: g.vector.tensor_copy(T.V[:].indirect(so), z), sc, ["so%d" % s, zt], ["V", "Vpad"])
-            for j in range(2):
-                a = 2 * s + j
-                add("dve", lambda g, a=a: g.vector.tensor_copy(T.V[:].indirect(T.ro[:, 16 * a:16 * a + 12]), T.rz[:, a * L:(a + 1) * L]), sc, (), ["V", "Vpad"],
-                    ext=[("r%d_%d" % (s, j), 2 * neng[j])], soft=[zsend, osend])
-
+                       [(T.uC[:, 301:312], T.G8k[:, sl(m)], T.dupb[:, 16 + m:L:16], False) for m in range(16)])
+            later.append((full, o, zp(s), zt, zsend, s))
         if last:
             writes(*later.pop())
-        Ai, Bi, slt = si(3), si(4), si(5)
-        ts(Ai, T.fin[:], 17, None, A.arith_shift_right, None, ["fin"], ["Ai"])
-        ts(Bi, T.fin[:], 12, 31, A.arith_shift_right, A.bitwise_and, ["fin"], ["Bi"])
-        ts(slt, T.fin[:], 1.0 / (9 * 131072), (182.5 - 1.0 / 64) / 9, A.mult, A.add, ["fin"], ["slt"])
-        ts(sm(6), T.fin[:], 96.0 * 131072, 64.0, A.is_lt, A.mult, ["fin"], ["gg"])
-        tt(sm(7), Bi, sm(6), A.max, ["Bi", "gg"], ["dd"])
-        tt(sm(9), sm(7), slt, A.min, ["dd", "slt"], ["zsl"])
-        tt(sm(11), sm(9), T.LLd[:], A.add, ["zsl", "LLd"], ["zs3"])
-        ts(T.zo[:], sm(11), float(L), None, A.mult, None, ["zs3"], ["zo"])
-        ts(sm(5), Ai, -1.0, 128.0, A.mult, A.add, ["Ai"], ["rr"])
-        ts(npu, T.fin[:], 96.0 * 131072, None, A.is_lt, None, ["fin"], ["np"])
-        ts(sm(10), T.fin[:], 96.0 * 131072, None, A.is_ge, None, ["fin"], ["pu"])
-        tt(sm(8), sm(5), sm(10), A.mult, ["rr", "pu"], ["dl"])
-        zr = ["zo", "zpad", "flip"] + tk("zk", 0, 3072) + ["z%d" % x for x in range(s + 1)]
-        if CFG["zg"]:
-            ag(zs(22 + s), T.ZW[:, 0:(22 + s) * L], T.zo[:], zr, ["z%d" % (s + 1)])
-        else:
-            gt(zs(22 + s), T.ZW[:, 0:(22 + s) * L], T.zo[:], None, None, zr, ["z%d" % (s + 1)])
-        tt(ptr1, npu, Bi, A.mult, ["np", "Bi"], ["ptr1"])
-        tt(sm(12), ptr1, sm(8), A.add, ["ptr1", "dl"], ["cs"])
+        Hs = si(2)
+        ts(Hs, T.fin[:], 63 << 18, None, A.bitwise_and, None, ["fin"], ["Hs"])
+        gt(T.y[:], Hs, T.QL[:], T.CA[:], A.add, ["Hs", "QL", "CA"], ["y"])
+        ts(T.sp[:], T.y[:], 64 * H1, 16.0, A.is_equal, A.mult, ["y"], ["sp"], 0.5)
+        gt(T.OP[:], sm(2), T.QL[:], T.sp[:], A.min, ["dp1", "QL", "sp"], ["OP"])
+        lst = [(T.mP[:, 0:L], T.Ib[:], T.OP[:], False)]
+        if s > 0:
+            ts(T.so_[:], T.y[:], 32 * H1, None, A.is_equal, None, ["y"], ["so_"], 0.5)
+            lst += [(T.mP[:, 0:L], T.Ib[:], T.Lf[:], False), (T.mP[:, 0:L], T.n16[:], T.so_[:], False)]
+        mm(grp(lst), ["Ib", "n16", "OP", "Lf", "so_"], ["mPg"], ["mP"])
+        ac(T.Lf[:], T.mP[:, 0:L], F.Relu, ["mPg"], ["Lf"], px=["mP"])
         if not last:
-            tt(sm(13), npu, pop, A.add, ["np", "pop"], ["de"])
-            tt(T.e[:], T.e[:], sm(13), A.subtract, ["e", "de"], ["e"])
-        lin12(sm(14), sm(5), 4095.0, 0.0, ["rr"], ["Pa"])
-        tt(sm(15), sm(14), sm(3), A.add, ["Pa", "P0"], ["Pp"])
-        tt(sm(21), T.fin[:], Bi, A.subtract, ["Bi", "fin"], ["fm"])
-        tt(sm(16), npu, sm(21), A.mult, ["np", "fm"], ["Pq"])
-        tt(sm(19), sm(15), sm(10), A.mult, ["Pp", "pu"], ["Ps"])
-        tt(sm(18), sm(19), sm(16), A.subtract, ["Ps", "Pq"], ["dlt"])
-        gt(T.sel[:], sm(12), T.QL[:], T.ca1[:], A.is_equal, ["cs", "QL", "ca1"], ["sel"])
-        gt(T.dsel[:], sm(18), T.QL[:], T.sel[:], A.mult, ["dlt", "QL", "sel"], ["dsel"])
-        if CFG["pvp"]:
-            mm(grp([(T.uB[:, 320:512], T.IW[:, 16:144], T.PV[:], True), (T.uB[:, 320:512], T.IW[:, 16:144], T.dsel[:], True)]), ["IW", "PV", "dsel"], ["PVp"], ["uB"])
-            ac(T.PV[:], T.uB[:, 320:512], F.Copy, ["PVp"], ["PV"], px=["uB"])
-        else:
-            tt(T.PV[:], T.PV[:], T.dsel[:], A.add, ["PV", "dsel"], ["PV"])
+            ts(T.bad1[:], T.y[:], 32 * H1, None, A.is_le, None, ["y"], ["bad1"], 0.5)
+            mm(grp([(T.mP[:, 0:L], T.Ib[:], T.P4r[:], False), (T.mP[:, 0:L], T.nIb[:], T.Lf[:], False)]), ["Ib", "nIb", "P4r", "Lf"], ["mPg"], ["mP"])
+            ac(T.NR[:], T.mP[:, 0:L], F.Relu, ["mPg"], ["NR"], px=["mP"])
+            least_return(T.NR, "NR")
+            ts(sm(10), Hs, 31 * H1, 33 * H1, A.max, A.min, ["Hs"], ["de"])
+            tt(T.e[:], T.e[:], sm(10), A.add, ["e", "de"], ["e"])
+            n = 12 * min(s + 1, RO - 1 - s)
+            tt(SK[:, 0:12], Hs, sm(8), A.add, ["Hs", "P0"], [Ft])
+            tt(T.Dl[:, 0:n], SK[:, 24:24 + n], SK[:, 0:n], A.subtract, [Ft, St], ["Dl"])
+            if n == 12:
+                tt(T.Dm[:, 0:n], T.Dl[:, 0:n], pop, A.mult, ["Dl", "pop"], ["Dm"])
+            else:
+                k = (n + 15) // 16
+                gt(T.Dm[:, 0:16 * k], pop, T.QL[:, 0:k], T.Dl[:, 0:16 * k], A.mult, ["Dl", "pop", "QL"], ["Dm"])
+            tt(T.SK[:, 1 - s % 2, 12:12 + n], SK[:, 0:n], T.Dm[:, 0:n], A.add, [Ft, St, "Dm"], [Sn])
 
     step[0] = RO
     dma("sp", T.yv[:], T.V[:, 0:W], 1 << 20, ["V"], ())
-    dma("sp", T.yz[:], zs(31), 49152, ["z%d" % RO], ())
-    cp(T.i192[:], T.PV[:], ["PV"], ["i192"])
-    ts(T.j192[:], T.i192[:], 17, None, A.arith_shift_right, None, ["i192"], ["j192"])
-    ts(T.i192[:], T.j192[:], -6.0, 1.0 / 9, A.add, A.mult, ["j192"], ["i192"])
-    ts(T.t192[:], T.i192[:], 0.0, 9.0, A.max, A.min, ["i192"], ["t192"])
-    ts(T.t192[:], T.t192[:], -9.0, -1.0, A.mult, A.add, ["t192"], ["t192"])
-    tt(T.t192[:], T.t192[:], T.j192[:], A.add, ["t192", "j192"], ["t192"])
-    ts(T.t192[:], T.t192[:], 0.0, None, A.max, None, ["t192"], ["t192"])
-    gt(T.tr[:, 0:L], T.t192[:], T.INV[:], None, None, ["t192", "INV"], ["tr0"])
+    dma("sp", T.yz[:], zp(RO), 49152, ["zp%d" % RO], ())
+    gt(T.tr[:, 0:L], T.Lf[:], T.INV[:], None, None, ["Lf", "INV"], ["tr0"])
     add("dve", lambda g: g.vector.transpose(T.src4[:, 0], T.tr[:, 0:L]), vcost(L, 1), ["tr0"], ["s40"])
     mm(swap3(lambda rho: T.dA[:, 96 * rho:96 * rho + 96], lambda ga: T.src4[:, 0, :, ga, :]), ["IW0", "IW1", "s40"], ["dA0"], ["dA0"])
     for rho in range(2):
         ac(T.ol[:, :, rho, :], T.dA[:, 96 * rho:96 * rho + 96], F.Copy, ["dA0"], ["ol%d" % rho], px=["dA0"])
     dma("act", T.yl[:], T.ol[:], 49152, ["ol0", "ol1"], ())
-    gt(T.Pm[:], ptr1, T.EL[:], T.DM[:], A.mult, ["ptr1", "EL", "DM"], ["Pm"])
-    mm(grp([(T.dB[0:8, 0:L], T.B8[:], T.Pm[:], True)]), ["B8", "Pm"], ["dB0"], ["dB0"])
-    ts(T.op[0:8, :], T.dB[0:8, 0:L], -1.0, None, A.add, None, ["dB0"], ["op"], px=["dB0"])
-    dma("sp", T.yp[:], T.op[0:8, :], 6144, ["op"], ())
+    ts(sm(0), si(2), -1.0 / H1, 32.0, A.mult, A.add, ["Hs"], ["sm0"])
+    tt(sm(1), sm(0), T.popb[:, 0:12], A.mult, ["sm0", "pop"], ["sm1"])
+    gt(T.t192[:], sm(1), T.EL[:], T.DM[:], A.mult, ["sm1", "EL", "DM"], ["t192"])
+    mm(grp([(T.dB[0:8, 0:L], T.B8[:], T.t192[:], True)]), ["B8", "t192"], ["dB0"], ["dB0"])
+    ts(T.k37[0:8, :], T.dB[0:8, 0:L], -1.0, None, A.add, None, ["dB0"], ["k37"], px=["dB0"])
+    dma("sp", T.yp[:], T.k37[0:8, :], 6144, ["k37"], ())
     return ops, 2 * (RO - 1) * sum(neng)
 
 
-BIAS = {}
-ROUNDS = 4
-LOOK, SLACK = 300.0, 60.0
-PLAN = """
-dpop.thr:1938 dU.fin:1982 pcnt.popc:1136 dxa0.cnt:1777 dxa1.xa0:2018 dnu0.nu0:-237 dsh0.nu0:-493 dt30.sh0:-881 dxi0.xa1:-535 dEQ0.pop:1943 dEQ1.pop:2106 dEQ2.pop:2122 dEQ3.pop:2068 dEQ4.pop:2106 dEQ5.pop:2061 dEQ6.pop:2132 dEQ7.pop:2124 dEQ8.pop:1765 dEQ9.pop:2270 dEQ10.pop:2137 dEQ11.pop:1754 pdup.EQ2:2111 pdup.EQ6:2499 pdup.EQ10:1685 adupb.dup:1903 pacc.pop:-541 pacc.LT15:567 pacc.dupb:-410 dsof.DUM:-509 dso.sof:-396 p.so:-141 dBi.fin:2104 dslt.fin:2010 dgg.fin:1900 ddd.gg:1916 dzsl.slt:2072 dzs3.LLd:1968 dzo.zs3:2079 az.z:2030 dnu1.nu1:137 dsh1.nu1:331 dt31.sh1:42 dxi2.xa1:323 aY0.xi0:-987 aY1.xi1:984 aY2.xi3:258 pd.Y0:1145 pd.Y1:643 p.z:500 aS0.d:199 aS1.d:-940 dzk0.S0:280 dzk1.S1:-297 puAu.zk1:423 dui0.uAu:-193 duk0.ui0:451 dv0.uk0:-62 asq0.vpad:-123 dtp0.sq0:301 dh0.tp0:247 dvi0.h0:88 pd.Y3:1077 aY4.xi5:376 dV.z:-1689 dV.:-211 aS2.d:-754 dzk2.S3:-115 puBu.zk3:333 dui1.uBu:988 duk1.ui1:149 dv1.uk1:372 asq1.v1:273 dtp1.sq1:155 dh1.tp1:150 dvi1.h1:563 pd.Y5:1189 aS4.d:1148 azk4.d:-504 puCu.zk5:1291 dui2.uCu:701 duk2.ui2:1319 dv2.uk2:1205 asq2.v2:24 dtp2.sq2:1119 dh2.tp2:833 dvi2.h2:1012 dnp.fin:2789 dde.pop:2502 de.de:2521 dAi.fin:2559 drr.Ai:2119 dpu.fin:2554 ddl.pu:2278 dcs.dl:2337 dptr1.Bi:2138 aPa.rr:2572 dPp.P0:2521 dfm.fin:2975 dPq.fm:2527 dPs.pu:2609 ddlt.Pq:1898 dsel.ca1:2199 ddsel.sel:3757 dPV.dsel:2328 aD0.e:619 aD1.e:215 dvown.U:98 dRL.PV:678 dPVh.PV:1132 dPVh.fk:104 dn96.RL:482 dn48.n96:713 dn24.n48:930 dKm.n24:764 dbad2.PV:485 dbad1.PV:808 dE0.zk0:-1003 aE1.vi0:773 pd.zk1:1562 aE3.vi1:341 dE2.zk2:1039 pd.zk3:870 dAE0.E0:1746 aAE1.d:663 dE4.zk4:276 aE5.vi2:1518 pd.zk5:594 aAE3.d:923 dAE2.E2:1089 aAE4.E4:1921 aAE5.d:-258 puAr.S1:1460 puAr.zk1:1690 abrow0.uAr:1652 dK10.uk0:1129 puBr.S3:-383 puBr.zk3:2200 abrow1.uBr:1405 dK11.uk1:1085 puCr.S5:645 abrow2.uCr:632 dK12.uk2:1310 puAf.uAr:2419 puAf.E0:-927 puAf.AE1:1549 dkey0.K10:1221 puBf.uBr:1396 puBf.E2:1099 puBf.AE3:2729 dkey1.K11:1257 dR.PVh:981 puCf.uCr:1356 puCf.AE5:4 dkey2.K12:927 dm96.key2:1013 dm48.m96:1483 dm24.m48:2124 dfin.m24:850 dsi1.C63:1252 dsi2.si1:2289 dfk.si2:1729 dthr.e:1515 dP8.h0:2133 dPm.h0:1425 pPbc.Pm:1734 dPb.Pbc:2308 aP0a.e:1183 dP0.U:1282 aflip.z:1170
-dRa.PVh:1200 dRb.Ra:1200 dRc.Rb:1200 dRd.key1:1000 dRe.Rc:1000 dkey1.Re:1000 dm48.key2:1000
-"""
-OFF = {x.split(":")[0]: 10 * int(x.split(":")[1]) for x in PLAN.split()}
-
-
 def schedule(ops):
-    n = len(ops)
+    n, HOP = len(ops), PAR["HOP"]
     pre = [sorted(set(o["deps"]) | set(o["soft"])) for o in ops]
     suc = [[] for _ in range(n)]
     for i in range(n):
         for d in pre[i]:
             suc[d].append(i)
-    pr = [0.0] * n
-    for i in range(n - 1, -1, -1):
-        pr[i] = ops[i]["cost"] + ops[i]["lat"] + HOP + max([pr[j] for j in suc[i]] + [0.0])
-    bias = [BIAS.get(o["cls"], 0) for o in ops]
 
-    def place(pre, suc, pr, back):
-        left = [len(p) for p in pre]
-        rdy, start = [0.0] * n, [0.0] * n
-        avail = [i for i in range(n) if left[i] == 0]
-        used = {}
-        for _ in range(n):
-            i = max(avail, key=lambda i: (pr[i], i if back else -i))
-            avail.remove(i)
-            c = ops[i]["cost"]
-            t = rdy[i] + (ops[i]["lat"] if back else 0.0)
-            u = used.setdefault(ops[i]["eng"], [])
-            k = len(u)
-            while k > 0 and u[k - 1][1] > t:
-                k -= 1
-            while k < len(u) and u[k][0] < t + c:
-                t = max(t, u[k][1])
-                k += 1
-            u.insert(k, (t, t + c))
-            start[i] = t
-            done = t + c + HOP + (0.0 if back else ops[i]["lat"])
-            for j in suc[i]:
-                rdy[j] = max(rdy[j], done)
-                left[j] -= 1
-                if left[j] == 0:
-                    avail.append(j)
-        return start
+    def hop(i, j):
+        return ops[i]["lat"] + (0.0 if ops[i]["eng"] == "pe" == ops[j]["eng"] else HOP)
 
-    if OFF:
-        for i in range(n - 1, -1, -1):
-            o = ops[i]
-            if o["cls"] in OFF and 0 <= o["step"] < RO:
-                pr[i] = -(o["step"] * 20000.0 + OFF[o["cls"]])
-            else:
-                pr[i] = o["cost"] + o["lat"] + HOP + max([pr[j] for j in suc[i]] + [-(RO + 2) * 20000.0])
+    def run(pre, suc, pr, back):
         left = [len(p) for p in pre]
         rdy, start, order, avail, free = [0.0] * n, [0.0] * n, [], {}, {}
         for i in range(n):
@@ -707,9 +640,9 @@ def schedule(ops):
             for e, lst in avail.items():
                 if lst:
                     t0 = max(free.get(e, 0.0), min(rdy[i] for i in lst))
-                    i = max((i for i in lst if rdy[i] <= t0 + LOOK), key=lambda i: (pr[i], -i))
+                    i = max((i for i in lst if rdy[i] <= t0 + PAR["LOOK"]), key=lambda i: (pr[i], -i))
                     if rdy[i] > t0:
-                        fill = [j for j in lst if max(t0, rdy[j]) + ops[j]["cost"] <= rdy[i] + SLACK and j != i and rdy[j] < rdy[i]]
+                        fill = [j for j in lst if max(t0, rdy[j]) + ops[j]["cost"] <= rdy[i] + PAR["SLACK"] and j != i and rdy[j] < rdy[i]]
                         if fill:
                             i = max(fill, key=lambda j: (pr[j], -j))
                     t = max(t0, rdy[i])
@@ -721,22 +654,134 @@ def schedule(ops):
             start[i] = t
             free[e] = t + ops[i]["cost"]
             for j in suc[i]:
-                rdy[j] = max(rdy[j], free[e] + ops[i]["lat"] + (0.0 if e == "pe" == ops[j]["eng"] else HOP))
+                rdy[j] = max(rdy[j], free[e] + (hop(j, i) if back else hop(i, j)))
                 left[j] -= 1
                 if left[j] == 0:
                     avail.setdefault(ops[j]["eng"], []).append(j)
-        return order, start
+        return order, start, max(start[i] + ops[i]["cost"] + (0.0 if back else ops[i]["lat"]) for i in range(n))
+
+    pr = [0.0] * n
+    for i in range(n - 1, -1, -1):
+        pr[i] = ops[i]["cost"] + max([pr[j] + hop(i, j) for j in suc[i]] + [ops[i]["lat"]])
     best = None
-    pr = [pr[i] + bias[i] for i in range(n)]
-    for _ in range(ROUNDS):
-        start = place(pre, suc, pr, False)
-        end = max(start[i] + ops[i]["cost"] + ops[i]["lat"] for i in range(n))
-        if best is None or end < best[0]:
-            best = (end, start)
-        rev = place(suc, pre, [start[i] + ops[i]["cost"] + ops[i]["lat"] for i in range(n)], True)
-        pr = [rev[i] + ops[i]["cost"] + bias[i] for i in range(n)]
-    start = best[1]
-    return sorted(range(n), key=lambda i: (start[i], i)), start
+    for _ in range(PAR["ROUNDS"]):
+        for i in range(n):
+            if ops[i]["dma"] and not pre[i]:
+                pr[i] = 1e9 - i
+        order, start, end = run(pre, suc, pr, False)
+        if best is None or end < best[2]:
+            best = (order, start, end)
+        _o, rev, _e = run(suc, pre, [start[i] + ops[i]["cost"] for i in range(n)], True)
+        pr = [rev[i] + ops[i]["cost"] for i in range(n)]
+    return best
+
+
+def kinds(ops):
+    seen, out = {}, []
+    for o in ops:
+        nm = o["name"]
+        if nm.rstrip("0123456789") in ("U", "zp", "z", "so", "F", "St"):
+            nm = nm.rstrip("0123456789")
+        k = (o["step"], o["eng"], nm)
+        seen[k] = seen.get(k, 0) + 1
+        out.append((0 <= o["step"] < RO, o["step"] >= RO, o["eng"], nm, seen[k]))
+    return out
+
+
+def refine(al, place, period, lo, hi, rounds, heat, free):
+    ops, kd = al[0], kinds(al[0])
+    ids = [i for i, o in enumerate(ops) if lo <= o["step"] <= hi]
+    at = {i: k for k, i in enumerate(ids)}
+    n, whole = len(ids), lo < 0 or hi >= RO
+    cl, eng = [kd[i] for i in ids], [ops[i]["eng"] for i in ids]
+    base = [max(ops[i]["step"], 0) * period for i in ids]
+    pre = [[at[d] for d in sorted(set(ops[i]["deps"]) | set(ops[i]["soft"])) if d in at] for i in ids]
+    first = [k for k, i in enumerate(ids) if ops[i]["dma"] and not ops[i]["deps"]]
+    sets = []
+    for a, m in zip(al, SETS):
+        sets.append(([a[i]["cost"] for i in ids], [a[i]["lat"] for i in ids],
+                     [[(d, a[ids[d]]["lat"] + (0.0 if eng[k] == "pe" == eng[d] else m["HOP"])) for d in pre[k]] for k in range(n)]))
+    fins = [k for k in range(n) if ops[ids[k]]["name"] == "fin"]
+
+    def score(place):
+        key = [base[k] + place[cl[k]] for k in range(n)]
+        for k in first:
+            key[k] = -1e9 + k
+        for k in range(n):
+            for d in pre[k]:
+                if key[d] >= key[k]:
+                    key[k] = key[d] + 1e-3
+        order = sorted(range(n), key=lambda k: key[k])
+        tot, info = 0.0, []
+        for (cost, lat, pr), m in zip(sets, SETS):
+            freeat, lastop, end, why = {}, {}, [0.0] * n, [-1] * n
+            for k in order:
+                e = eng[k]
+                t, w = freeat.get(e, 0.0), lastop.get(e, -1)
+                for d, h in pr[k]:
+                    if end[d] + h > t:
+                        t, w = end[d] + h, -2 - d
+                end[k] = freeat[e] = t + cost[k]
+                why[k], lastop[e] = w, k
+            tail = max(range(n), key=lambda k: end[k] + lat[k]) if whole else fins[-1]
+            tot += m["WT"] * (end[tail] + lat[tail] if whole else (end[tail] - end[fins[0]]) / (len(fins) - 1))
+            info.append((why, tail))
+        return tot, info, key, order
+
+    seed = [12345]
+
+    def rnd():
+        seed[0] = (seed[0] * 1103515245 + 12345) % 2147483648
+        return seed[0] / 2147483648.0
+
+    def pick(x):
+        return x[int(rnd() * len(x))]
+
+    cur = best = score(place)
+    keep = place
+    for it in range(rounds):
+        why, k = pick(cur[1])
+        arcs = []
+        while why[k] != -1:
+            if why[k] >= 0:
+                arcs.append((why[k], k))
+            k = why[k] if why[k] >= 0 else -2 - why[k]
+        if arcs and rnd() < 0.7:
+            j, i = pick(arcs)
+            if rnd() < 0.5:
+                c, v = cl[i], cur[2][j] - base[i] - pick((1, 1, 100, 400)) * rnd()
+            else:
+                c, v = cl[j], cur[2][i] - base[j] + pick((1, 100, 400, 1500)) * rnd()
+        else:
+            c = pick(cl)
+            v = place[c] + pick((-1, 1)) * pick((50, 200, 800)) * rnd()
+        if not free(c):
+            continue
+        new = dict(place)
+        new[c] = v
+        sc = score(new)
+        if sc[0] <= cur[0] or rnd() < math.exp((cur[0] - sc[0]) / (heat * (1 - it / rounds) + 1)):
+            place, cur = new, sc
+            if sc[0] < best[0]:
+                best, keep = sc, new
+    return keep, [ids[k] for k in best[3]], best[0]
+
+
+def plan(al):
+    ops, kd = al[0], kinds(al[0])
+    _o, start, _e = schedule(ops)
+    f = [start[i] for i, o in enumerate(ops) if o["name"] == "fin"]
+    period, place = f[5] - f[4], {}
+    for i, o in enumerate(ops):
+        if o["step"] in (-1, 5, RO):
+            place[kd[i]] = start[i] - {-1: f[0] - period, 5: f[4], RO: f[RO - 1]}[o["step"]]
+    for i, o in enumerate(ops):
+        place.setdefault(kd[i], start[i] - f[o["step"] - 1])
+    inner = set(kd[i] for i, o in enumerate(ops) if o["step"] == 5)
+    place = refine(al, place, period, 4, 6, PAR["R1"], PAR["HEAT"], lambda c: True)[0]
+    place = refine(al, place, period, -1, 1, PAR["R2"], PAR["HEAT"], lambda c: c not in inner)[0]
+    place = refine(al, place, period, RO - 1, RO, PAR["R2"], PAR["HEAT"], lambda c: c not in inner)[0]
+    return refine(al, place, period, -1, RO, 0, 1.0, None)[1]
 
 
 ORDER = []
@@ -746,9 +791,13 @@ def rank_program(g, core, T, topo):
     rank = T.rank_of(core)
     if rank is None:
         return
-    ops, nsent = build(T, topo, core, rank)
     if not ORDER:
-        ORDER.append(schedule(ops)[0])
+        al = []
+        for m in SETS[::-1]:
+            PAR.update(m)
+            al.insert(0, build(T, topo, core, rank)[0])
+        ORDER.append(plan(al))
+    ops, nsent = build(T, topo, core, rank)
     queue = {"dve": g.vector, "act": g.scalar, "pe": g.tensor, "pool": g, "sp": g.sync}
     known = {e: {} for e in queue}
     mark, count, nd = {}, {}, 0

@@ -4,11 +4,12 @@ from concourse.mybir import AluOpType as A, AxisListType, ActivationFunctionType
 
 L, W, RO = 192, 4096, 10
 CFG = {
-    "pieces": [(0, "R", [(2, "A"), (2, "A"), (2, "A")], [(2, "A"), (2, "A"), (2, "B")]),
-               (12, "F", [(4, "D")], [(4, "D")]),
-               (6, "R", [(2, "A"), (2, "A"), (2, "A")], [(2, "A"), (2, "A"), (2, "B")])],
+    "pieces": [(0, "R", [(2, "A"), (2, "A"), (1, "A")], [(2, "A"), (1, "A"), (2, "B")]),
+               (10, "F", [(3, "D"), (3, "D")], [(6, "D")]),
+               (5, "R", [(2, "A"), (2, "A"), (1, "A")], [(2, "A"), (1, "A"), (2, "B")])],
     "xs": [(0, 64), (64, 192)],
-    "zact": "pf",
+    "xa": True, "rua": (), "sca": "AAA",
+    "zact": "phf",
 }
 f32, bf, f16, i32, u16 = "float32", "bfloat16", "float16", "int32", "uint16"
 XO = 16
@@ -21,12 +22,12 @@ def _sb(n, d):
 
 
 SCRATCH = {
-    "X": _sb(XO + W + 32, bf), "V": _sb(W + L, bf), "ZW": _sb(27 * L, bf), "zp": _sb(11 * L, bf), "zm": _sb(L, bf),
+    "X": _sb(XO + W + 32, bf), "V": _sb(W + L, f32), "Vb": _sb(W + L, bf), "ZW": _sb(27 * L, bf), "zp": _sb(4 * L, bf), "zq": _sb(RO * L, f32), "zm": _sb(L, bf),
     "Y": _sb(3072, bf), "S": _sb(3072, bf), "Sh": _sb(3072, f16), "E": _sb(3072, bf), "AE": _sb(3072, bf),
     "nmi": _sb((6, 2, 16), i32), "cai": _sb((6, 2, 16), bf), "rti": _sb((6, 2, 16), bf), "wti": _sb(1, i32), "thi": _sb(1, i32),
     "src4": _sb((4, 6, 2, 16), f32), "tr": _sb(4 * L, f32),
     "nB": _sb(L, f32), "ca1": _sb(L, f32), "rtB": _sb(L, f32), "thh": _sb(L, f16), "CA": _sb(L, f32),
-    "P4r": _sb(L, bf), "P4c": _sb(L, f32), "NR": _sb(L, bf), "Lf": _sb(L, bf), "Es": _sb(16, f32),
+    "P4r": _sb(L, bf), "P4c": _sb(L, bf), "NR": _sb(L, bf), "Lf": _sb(L, bf), "Es": _sb(16, f32),
     "y": _sb(L, bf), "sp": _sb(L, bf), "so_": _sb(L, bf), "OP": _sb(L, bf),
     "k37": _sb(L, f32), "kk": _sb(L, f32), "t192": _sb(L, f32), "i192": _sb(L, i32), "j192": _sb(L, i32),
     "one": _sb(160, f32), "IW": _sb(160, f32), "IW0": _sb(160, f32), "IW1": _sb(160, f32),
@@ -36,7 +37,7 @@ SCRATCH = {
     "Wh": _sb(144, f16), "LT": _sb((16, 128), bf), "RT": _sb((16, 128), bf),
     "CI": _sb((2, PW), bf), "ones": _sb(128, bf), "N64": _sb(PW, bf),
     "DM": _sb(L, f32), "pi": _sb(1, i32), "pj": _sb(1, i32), "PM": _sb(1, f32), "hf": _sb(2, f32), "wf": _sb(4, f32), "wi": _sb(2, i32),
-    "thf": _sb(1, f32), "CF": _sb(1, f32), "ltm": _sb(16, f32),
+    "thf": _sb(1, f32), "CF": _sb(1, f32),
     "c16": _sb(12, f32), "c1": _sb(12, f32), "LL": _sb(12, f32), "DUM": _sb(12, f32), "LLd": _sb(12, f32), "KQ": _sb(12, i32), "QF": _sb(12, f32), "t12": _sb(12, f32),
     "QL": _sb(12, u16), "DL": _sb(6, u16), "EL": _sb(12, u16), "PERM": _sb(12, u16), "INV": _sb(12, u16),
     "U": _sb(16 * (RO + 1), i32), "xi": _sb(L, u16), "nu": _sb(L, f32), "t3": _sb(L, i32), "sh": _sb(L, i32),
@@ -45,7 +46,7 @@ SCRATCH = {
     "SK": _sb((2, 96), f32), "Dl": _sb(64, f32), "Dm": _sb(64, f32), "D": _sb(24, f32), "e": _sb(12, f32),
     "sm": _sb(16 * 12, f32), "si": _sb(16 * 3, i32), "popb": _sb(16, bf), "xa": _sb(2, f32), "zo": _sb(12, u16),
     "P8": _sb(16, f32), "Pb": _sb(L, f16), "EQ": _sb((12, 208), bf), "dupb": _sb(L, bf),
-    "so": _sb(16 * RO, u16), "rz": _sb(2 * RO * L, bf), "ro": _sb(2 * RO * 16, u16),
+    "so": _sb(16 * RO, u16), "rz": _sb(2 * RO * L, f32), "ro": _sb(2 * RO * 16, u16),
     "ol": _sb((6, 2, 16), bf),
     "dA": ("psum", [128, 1024], f32), "dB": ("psum", [128, 1024], f32),
     "uA": ("psum", [128, 512], f32), "uB": ("psum", [128, 512], f32), "uC": ("psum", [128, 512], f32), "mP": ("psum", [128, 512], f32),
@@ -53,10 +54,10 @@ SCRATCH = {
 NDMA = 16
 SEMAPHORES = ["dve", "act", "pe", "pool", "sent"] + ["d%d" % i for i in range(NDMA)] + ["r%d_%d" % (s, j) for s in range(1, RO) for j in range(2)]
 
-SETS = [{"FIX": 6.0, "RL": 2000.0, "CY": 0.85, "PC": 0.43, "GA": 1.56, "SC": 3.8, "HOP": 150.0, "WT": 1.0},
-        {"FIX": 10.0, "RL": 3000.0, "CY": 1.2, "PC": 0.6, "GA": 1.9, "SC": 5.0, "HOP": 150.0, "WT": 0.6},
-        {"FIX": 6.0, "RL": 2500.0, "CY": 0.9, "PC": 0.45, "GA": 1.2, "SC": 2.5, "HOP": 220.0, "WT": 0.8}]
-PAR = dict(SETS[0], LOOK=300.0, SLACK=40.0, ROUNDS=3, R1=20000, R2=4000, HEAT=150.0)
+SETS = [{"FIX": 10.0, "RC": 700.0, "RL": 1500.0, "CY": 0.91, "PC": 0.46, "GA": 1.56, "SC": 3.8, "HOP": 150.0, "WT": 1.0},
+        {"FIX": 10.0, "RC": 1000.0, "RL": 2500.0, "CY": 1.2, "PC": 0.6, "GA": 1.9, "SC": 5.0, "HOP": 150.0, "WT": 0.6},
+        {"FIX": 10.0, "RC": 1000.0, "RL": 2000.0, "CY": 0.95, "PC": 0.48, "GA": 1.2, "SC": 2.5, "HOP": 220.0, "WT": 0.8}]
+PAR = dict(SETS[0], LOOK=300.0, SLACK=40.0, ROUNDS=3, R2=20000, HEAT=100.0, PULL=0.1)
 
 
 def build(T, topo, core, rank):
@@ -194,7 +195,7 @@ def build(T, topo, core, rank):
     dma("act", T.thi[:], T.th[:], 512, (), ["thi"])
     dma("sp", T.X[:, XO:XO + W], T.xt[:], 1 << 20, (), ["X0"])
     dma("act", T.X[:, XO + W:], T.xt[:, 0:32], 1 << 20, (), ["X1"])
-    dma("sp", T.V[:, 0:W], T.vt[:], 2 << 20, (), ["V"])
+    dma("sp", T.Vb[:, 0:W], T.vt[:], 2 << 20, (), ["Vb"])
 
     io(T.pi[:], [[0, 1]], 0, 1, ["pi"], fl=False)
     ms(T.one[:], 1.0, ["one"])
@@ -206,7 +207,6 @@ def build(T, topo, core, rank):
     io(T.k37[:], [[37, 16], [0, 12]], 0, 0, ["k37"])
     io(T.kk[:], [[8192, 16], [0, 12]], (63 << 18) + 2048, 0, ["kk"])
     io(T.DM[:], [[0, 12], [1, 16]], 0, 0, ["DM"])
-    io(T.ltm[:], [[1, 16]], 0, 0, ["ltm"])
     ts(T.pj[:], T.pi[:], 15, None, A.bitwise_and, None, ["pi"], ["pj"])
     cp(T.PM[:], T.pj[:], ["pj"], ["PM"])
     ts(T.pj[:], T.pi[:], 4, 1, A.arith_shift_right, A.bitwise_and, ["pi"], ["pj"])
@@ -243,7 +243,7 @@ def build(T, topo, core, rank):
         return out
 
     srcs = [(T.nmi, "nmi", T.nB, "nB"), (T.cai, "cai", T.ca1, "ca1"), (T.rti, "rti", T.rtB, "rtB"), (None, "thf", T.thh, "thh")]
-    cp(T.thf[:], T.thi[:], ["thi"], ["thf"])
+    ts(T.thf[:], T.thi[:], 0.5, None, A.add, None, ["thi"], ["thf"])
     for a, (s, sn, d, dn) in enumerate(srcs):
         s4 = T.src4[:, a]
         if a == 0:
@@ -280,18 +280,22 @@ def build(T, topo, core, rank):
         bs = slice(12 * b0, 12 * (b0 + nb))
         tt(UB[t][0][:, 36 * nb:48 * nb], T.t192[:, bs], T.kk[:, bs], A.add, ["t192", "kk"], ["KS%d" % t], px=[UB[t][1]])
     ac(T.CA[:], T.ca1[:], F.Identity, ["ca1"], ["CA"], scale=H1)
-    ac(T.P4r[:], T.rtB[:], F.Exp, ["rtB"], ["P4r"], scale=-math.log(4.0))
-    ac(T.P4c[:], T.ca1[:], F.Exp, ["ca1"], ["P4c"], scale=-math.log(4.0))
-    ac(T.pIb[:], T.IW[:, 16:144], F.Copy, ["IW"], ["pIb"], scale=-1024.0 * BIG)
-    ac(T.NI[:], T.IW[:, 16:144], F.Copy, ["IW"], ["NI"], scale=-BIG)
+    ac(T.P4r[:], T.rtB[:], F.Silu, ["rtB"], ["P4r"], scale=-2.5)
+    ac(T.P4c[:], T.ca1[:], F.Silu, ["ca1"], ["P4c"], scale=-2.5)
+    ac(T.pIb[:], T.IW[:, 16:144], F.Copy, ["IW"], ["pIb"], scale=-4096.0 * BIG)
+    ac(T.NI[:], T.IW[:, 16:144], F.Copy, ["IW"], ["NI"], scale=-2 * BIG)
     ac(T.n16[:], T.IW[:, 16:144], F.Copy, ["IW"], ["n16"], scale=-16.0)
     ac(T.I8k[:], T.IW[:, 16:144], F.Copy, ["IW"], ["I8k"], scale=-8192.0)
-    ac(T.GB2[:], T.G[:], F.Copy, ["G"], ["GB2"], scale=2 * BIG)
-    ac(T.GBn[:], T.G[:], F.Copy, ["G"], ["GBn"], scale=-BIG)
+    ac(T.GB2[:], T.G[:], F.Copy, ["G"], ["GB2"], scale=4 * BIG)
+    ac(T.GBn[:], T.G[:], F.Copy, ["G"], ["GBn"], scale=-2 * BIG)
     ac(T.G8k[:], T.G[:], F.Copy, ["G"], ["G8k"], scale=8192.0)
     ac(T.BOb[:], T.BO[:], F.Copy, ["BO"], ["BOb"])
     ms(T.X[:, 0:XO], 0.0, ["Xpad"])
-    ms(T.V[:, W:W + L], 0.0, ["Vpad"])
+    ms(T.V[:, W:W + L], 64.0, ["Vpad"])
+    ms(T.Vb[:, W:W + L], 0.0, ["Vbpad"])
+    VQ = ["V%d" % c for c in range(0, W, 512)]
+    for c in range(0, W, 512):
+        ac(T.V[:, c:c + 512], T.Vb[:, c:c + 512], F.Identity, ["Vb"], ["V%d" % c], bias=64.0)
     ms(T.e[:], 0.0, ["e"])
     ms(T.SK[:], 0.0, ["F0", "F1", "St0", "St1"])
     ms(T.Dl[:], 0.0, ["Dl"])
@@ -302,11 +306,12 @@ def build(T, topo, core, rank):
     ms(T.CI[:, 0], -2048.0, ["CI0"])
     ms(T.CI[:, 1], -15.0 / 64, ["CI1"])
     ts(T.DM[:], T.DM[:], T.PM[:], None, A.is_equal, None, ["DM", "PM"], ["DM"])
-    ts(T.ltm[:], T.ltm[:], T.PM[:], 8192.0, A.is_gt, A.mult, ["ltm", "PM"], ["ltm"])
-    for m in range(1, 16):
-        ac(T.LT[:, m], T.G[:, sl(m)], F.Copy, ["G", "ltm"], ["LT%d" % m], scale=T.ltm[:, m:m + 1])
-    for m in range(16):
-        ac(T.RT[:, m], T.BO[:], F.Copy, ["BO", "DM"], ["RT%d" % m], scale=T.DM[:, m:m + 1])
+    io(T.RT[:], [[0, 2048]], 1, 0, ["RT"])
+    af(T.RT[:], T.RT[:], [[-1, 16], [-16, 8], [0, 16]], A.is_equal, 0, 1, ["RT"], ["RT"])
+    io(T.LT[:], [[0, 2048]], 8192, 0, ["LT"])
+    af(T.LT[:], T.LT[:], [[-1, 16], [0, 8], [1, 16]], A.is_equal, 0, 0, ["LT"], ["LT"])
+    af(T.LT[:], T.LT[:], [[0, 16], [-16, 8], [0, 16]], A.is_ge, 0, 1, ["LT"], ["LT"])
+    af(T.LT[:], T.LT[:], [[1, 16], [16, 8], [0, 16]], A.is_gt, 0, -1, ["LT"], ["LT"])
     cp(T.EL[:], T.c1[:], ["c1"], ["EL"])
     ts(T.LLd[:], T.LL[:], 1.0 / L, None, A.mult, None, ["LL"], ["LLd"])
     ts(T.DUM[:], T.LL[:], W - 10240.0, None, A.add, None, ["LL"], ["DUM"])
@@ -371,26 +376,40 @@ def build(T, topo, core, rank):
         return [(o, Gm[:, sl(m)], B[:, c0 + m:c0 + n:16], False) for m in range(16)]
 
     def least_return(src, tok):
-        mm(grp([(T.mP[:, 432:480], T.Ib[:], src[:, 48 * k:48 * k + 48], False) for k in range(4)]), ["Ib", tok], ["mPg"], ["mP"])
+        sign = T.Ib if tok == "P4r" else T.nIb
+        mm(grp([(T.mP[:, 432:480], sign[:], src[:, 48 * k:48 * k + 48], False) for k in range(4)]), ["Ib", "nIb", tok], ["mPg"], ["mP"])
         ac(T.so_[:, 0:48], T.mP[:, 432:480], F.Copy, ["mPg"], ["so_"], px=["mP"])
         mm(grp([(T.mP[:, 420:432], T.Ib[:], T.so_[:, 12 * k:12 * k + 12], False) for k in range(4)]), ["Ib", "so_"], ["mPg"], ["mP"])
         ac(T.Es[:, 0:12], T.mP[:, 420:432], F.Copy, ["mPg"], ["Es"], px=["mP"])
-        gt(T.bad2[:], T.Es[:, 0:12], T.QL[:], T.P4c[:], A.is_gt, ["Es", "QL", "P4c"], ["bad2"])
+        gt(T.bad2[:], T.Es[:, 0:12], T.QL[:], T.P4c[:], A.is_lt, ["Es", "QL", "P4c"], ["bad2"])
+
+    def landing(s, j):
+        return zp(2 + j) if s == RO - 1 else T.rz[:, (2 * s + j) * L:(2 * s + j + 1) * L]
 
     def writes(full, o, z, zt, zsend, s):
         mm(full[:2], ["Ib", "I8k", "Ph", "pop"], ["uCg"], ["uC"])
-        mm(full[2:17], ["EQ%d" % q for q in range(12)] + ["LT%d" % m for m in range(1, 16)] + ["uCg"], ["acc1"], ["uC"])
+        mm(full[2:17], ["EQ%d" % q for q in range(12)] + ["LT", "uCg"], ["acc1"], ["uC"])
         mm(full[17:], ["G8k", "dupb", "uCg", "acc1"], ["acc"], ["uC"])
         tt(sm(4), o, T.DUM[:], A.min, ["acc", "DUM", "uCg"], ["sof"], px=["uC"])
         so = T.so[:, 16 * s:16 * s + 12]
         ts(so, sm(4), 10240.0, None, A.add, None, ["sof"], ["so%d" % s])
-        osend = add("pool", send(so, lambda j, s=s: T.ro[:, (2 * s + j) * 16:(2 * s + j) * 16 + 12], s), 1000.0, ["so%d" % s], (), lat=RL)
+        osend = add("pool", send(so, lambda j, s=s: T.ro[:, (2 * s + j) * 16:(2 * s + j) * 16 + 12], s), PAR["RC"], ["so%d" % s], (), lat=RL)
         sc = (50 / 0.83 + L * SC) * CY
-        add("dve", lambda g: g.vector.tensor_copy(T.V[:].indirect(so), z), sc, ["so%d" % s, zt], ["V", "Vpad"])
+
+        def scatter(who, off, src, r, **kw):
+            if s == RO - 1:
+                add("dve", lambda g: g.vector.tensor_copy(T.Vb[:].indirect(off), src), sc, r, ["Vb", "Vbpad"] + VQ, **kw)
+            elif who == "A":
+                add("act", lambda g: g.scalar.activation(T.V[:].indirect(off), src, F.Silu), sc + 15, r, ["V", "Vpad"] + VQ, **kw)
+            else:
+                add("dve", lambda g: g.vector.tensor_copy(T.V[:].indirect(off), src), sc, r, ["V", "Vpad"] + VQ, **kw)
+
+        if s == RO - 1:
+            for c in range(0, W, 512):
+                ac(T.Vb[:, c:c + 512], T.V[:, c:c + 512], F.Relu, ["V", "Vb"], ["V%d" % c], bias=-64.001)
+        scatter(CFG["sca"][0], so, z, ["so%d" % s, zt])
         for j in range(2):
-            a = 2 * s + j
-            add("dve", lambda g, a=a: g.vector.tensor_copy(T.V[:].indirect(T.ro[:, 16 * a:16 * a + 12]), T.rz[:, a * L:(a + 1) * L]), sc, (), ["V", "Vpad"],
-                ext=[("r%d_%d" % (s, j), 2 * neng[j])], soft=[zsend, osend])
+            scatter(CFG["sca"][1 + j], T.ro[:, 16 * (2 * s + j):16 * (2 * s + j) + 12], landing(s, j), (), ext=[("r%d_%d" % (s, j), 2 * neng[j])], soft=[zsend, osend])
 
     least_return(T.P4r, "P4r")
     for s in range(RO):
@@ -414,8 +433,9 @@ def build(T, topo, core, rank):
             writes(*later.pop())
         za = CFG["zact"]
         if s > 0:
-            lin("p" in za, zp(s), T.zm[:], 1.0, 64.0, ["zm"], [zt])
-            zsend = add("pool", send(zp(s), lambda j, s=s: T.rz[:, (2 * s + j) * L:(2 * s + j + 1) * L], s), 1000.0, [zt], (), lat=RL)
+            zq = zp(0) if last else T.zq[:, s * L:(s + 1) * L]
+            ac(zq, T.zm[:], F.Identity, ["zm"], [zt] + ["zp0"] * last, bias=64.0 if last else 128.0)
+            zsend = add("pool", send(zq, lambda j, s=s: landing(s, j), s), PAR["RC"], [zt], (), lat=RL)
         if not last:
             lin("h" in za, zs(HIST + s), T.zm[:], 1.0, 128.0, ["zm"], ["z%d" % s])
         lin("f" in za, zs(FLIP), T.zm[:], -1.0, 63.0, ["zm"], ["flip"])
@@ -471,7 +491,11 @@ def build(T, topo, core, rank):
             full = grp([(pu, T.Ib[:], T.CI[:, 0, 0:w], False), (pu, T.WB[:], T.N64[:, 0:w], False)] + sums(pu, T.Wh, T.ZW, c0, cn))
             mm(full[:2], ["Ib", "WB", "N64", "CI0"], [gp, ub + "u"], [ub])
             mm(full[2:], ["Wh", gp] + zkt, [ub + "u"], [ub])
-            ts(T.ru[:, ps], pu, M35, -M35, A.add, A.add, [ub + "u"], ["ru%d" % t], px=[ub])
+            if t in CFG["rua"]:
+                ac(T.ru[:, ps], pu, F.Identity, [ub + "u"], ["ru%d" % t], bias=M35, px=[ub])
+                ac(T.ru[:, ps], T.ru[:, ps], F.Identity, ["ru%d" % t], ["ru%d" % t], bias=-M35)
+            else:
+                ts(T.ru[:, ps], pu, M35, -M35, A.add, A.add, [ub + "u"], ["ru%d" % t], px=[ub])
             tt(T.uf[:, ps], pu, T.ru[:, ps], A.subtract, [ub + "u", "ru%d" % t], ["uf%d" % t], px=[ub])
             ac(T.sq[:, ps], T.uf[:, ps], F.Square, ["uf%d" % t], ["sq%d" % t], bias=2048.0 + 592)
             gt(T.tp[:, pw], T.D[:], T.DL[:, 0:wide // 16] if t == 0 else T.QL[:, 0:wide // 16], T.sq[:, pw], A.add,
@@ -492,12 +516,12 @@ def build(T, topo, core, rank):
             ho = T.h[:, W0:W0 + 12]
             ts(T.P8[:, 0:12], ho, -2048.0, None, A.add, None, ["h0"], ["P8"])
             ts(T.Ph[:, 0:12], ho, -2048.0, None, A.add, None, ["h0"], ["Ph"])
-            mm([(T.mP[:, m:192:16], T.RT[:, m], T.Ph[:, 0:12], True, True, False) for m in range(16)], ["RT%d" % m for m in range(16)] + ["Ph"], ["mPg"], ["mP"])
+            mm([(T.mP[:, m:192:16], T.RT[:, m], T.Ph[:, 0:12], True, True, False) for m in range(16)], ["RT", "Ph"], ["mPg"], ["mP"])
             cp(T.Pb[:], T.mP[:, 0:192], ["mPg"], ["Pb"], px=["mP"])
         for t, (b0, nb, xm, xu, vu) in enumerate(PCS):
             c0, cn, w = L * b0, L * nb, 12 * nb
             bs = slice(12 * b0, 12 * b0 + w)
-            Vw = T.V[:, 0:W]
+            Vw, Vt, vo = (T.V[:, 0:W], ["V", "vi%d" % t], 0.0) if s > 1 else (T.Vb[:, 0:W], ["Vb", "vi%d" % t], 32.0)
             Pu, ub = UB[t]
             gp = ub + "g"
             o = Pu[:, 2 * w:3 * w]
@@ -511,15 +535,15 @@ def build(T, topo, core, rank):
                 off = T.vi[:, 12 * u0:12 * (u0 + un)]
                 zkt, Et, At = tk("zk", u0, un), tk("E", u0, un), tk("AE", u0, un)
                 if mode in "BD":
-                    gt(T.E[:, cs], Vw, off, T.ZW[:, cs], A.subtract, ["V", "vi%d" % t] + zkt, Et)
+                    gt(T.E[:, cs], Vw, off, T.ZW[:, cs], A.subtract, Vt + zkt, Et)
                     if mode == "B":
-                        ac(T.AE[:, cs], T.E[:, cs], F.Abs, Et, At, bias=32.0, scale=0.5)
+                        ac(T.AE[:, cs], T.E[:, cs], F.Abs, Et, At, bias=vo, scale=0.5)
                     else:
-                        ts(T.AE[:, cs], T.E[:, cs], -64.0, 32.0, A.max, A.add, Et, At, 0.5)
+                        ts(T.AE[:, cs], T.E[:, cs], -2 * vo, vo, A.max, A.add, Et, At, 0.5)
                         p0 = 2 * w + 12 * (u0 - b0)
                         mm(more(sums(Pu[:, p0:p0 + 12 * un], T.GBn, T.E, L * u0, L * un)), ["GBn", gp] + Et, [ub + "f"], [ub])
                 else:
-                    ag(T.E[:, cs], Vw, off, ["V", "vi%d" % t], Et)
+                    ag(T.E[:, cs], Vw, off, Vt, Et)
                     P, p0, px = tile(L * un)
                     lst, a1 = [], L * u0
                     for a0 in range(0, L * un, 512):
@@ -527,34 +551,36 @@ def build(T, topo, core, rank):
                         lst += grp([(P[:, p0 + a0:p0 + a0 + n], T.nIb[:], T.ZW[:, a1 + a0:a1 + a0 + n], False),
                                     (P[:, p0 + a0:p0 + a0 + n], T.Ib[:], T.E[:, a1 + a0:a1 + a0 + n], False)])
                     mm(lst, ["Ib", "nIb"] + Et + zkt, px, px)
-                    ac(T.AE[:, cs], P[:, p0:p0 + L * un], F.Abs, px, At, bias=32.0, scale=0.5, px=px)
+                    ac(T.AE[:, cs], P[:, p0:p0 + L * un], F.Abs, px, At, bias=vo, scale=0.5, px=px)
             mm(more(sums(o, T.GB2, T.AE, c0, cn), True), ["GB2", gp, ub + "p"] + tk("AE", b0, nb), [ub + "f"], [ub])
-            k0 = 112 * t
-            tt(T.key[:, k0 + 12:k0 + 12 + w], o, T.K1[:, bs], A.min, [ub + "f", gp, "K1%d" % t], ["key%d" % t], px=[ub])
-            n = nb + 1
+            k0, n, rt_ = 112 * t, nb + (1, 0, 2)[t], ["key%d" % t] + (["R0"], [], ["R1", "R2"])[t]
+            tt(T.key[:, k0 + 12 * n - w:k0 + 12 * n], o, T.K1[:, bs], A.min, [ub + "f", gp, "K1%d" % t], ["key%d" % t], px=[ub])
             while n > 1:
                 hh = n // 2
                 if n > 2:
-                    dst, wt_ = T.key[:, k0:k0 + 12 * hh], ["key%d" % t, "R%d" % t]
+                    dst, wt_ = T.key[:, k0:k0 + 12 * hh], rt_
                 elif t < 2:
-                    dst, wt_ = T.key[:, k0 + 112:k0 + 124], ["R%d" % (t + 1)]
+                    dst, wt_ = T.key[:, 224 + 12 * t:236 + 12 * t], ["R%d" % (t + 1)]
                 else:
                     dst, wt_ = T.fin[:], ["fin"]
-                tt(dst, T.key[:, k0:k0 + 12 * hh], T.key[:, k0 + 12 * (n - hh):k0 + 12 * n], A.max, ["key%d" % t, "R%d" % t], wt_)
+                tt(dst, T.key[:, k0:k0 + 12 * hh], T.key[:, k0 + 12 * (n - hh):k0 + 12 * n], A.max, rt_, wt_)
                 n -= hh
         pop = T.popb[:, 0:12]
         ts(pop, T.fin[:], 32 * H1, None, A.is_lt, None, ["fin"], ["pop"])
         if not last:
             ts(T.U[:, 16 * (s + 1):16 * (s + 1) + 12], T.fin[:], 4095, None, A.bitwise_and, None, ["fin"], ["U%d" % (s + 1)])
             mm(grp([(T.mP[:, 400:413], T.ones[:], T.popb[:, 0:13], False)]), ["ones", "pop", "popc"], ["mPg"], ["mP"])
-            add("dve", lambda g: g.vector.tensor_reduce(T.xa[:, 0:1], T.mP[:, 400:413], AxisListType.X, A.add), vcost(13, 1), ["mPg"], ["xa0"], ["mP"])
+            if CFG["xa"]:
+                add("act", lambda g: g.scalar.activation(T.Es[:, 0:13], T.mP[:, 400:413], F.Copy, accum_out=T.xa[:, 0:1]), vcost(13, 1) + 20, ["mPg"], ["xa0", "Es"], ["mP"])
+            else:
+                add("dve", lambda g: g.vector.tensor_reduce(T.xa[:, 0:1], T.mP[:, 400:413], AxisListType.X, A.add), vcost(13, 1), ["mPg"], ["xa0"], ["mP"])
             ts(T.xa[:, 1:2], T.xa[:, 0:1], M28, -(M28 + 32), A.add, A.add, ["xa0"], ["xa1"])
         ts(si(1), T.fin[:], 13, 31, A.arith_shift_right, A.bitwise_and, ["fin"], ["slt"])
         tt(sm(9), si(1), T.LLd[:], A.add, ["slt", "LLd"], ["zs3"])
         ts(T.zo[:], sm(9), float(L), None, A.mult, None, ["zs3"], ["zo"])
         zr = ["zo", "flip"] + tk("zk", 0, 16) + ["z%d" % x for x in range(s)]
         if last:
-            ag(zp(RO), T.ZW[:, 0:(HIST + s) * L], T.zo[:], zr, ["zp%d" % RO], bias=-64.0)
+            ag(zp(1), T.ZW[:, 0:(HIST + s) * L], T.zo[:], zr, ["zp%d" % RO], bias=-64.0)
         else:
             ag(T.zm[:], T.ZW[:, 0:(HIST + s) * L], T.zo[:], zr, ["zm"], bias=-128.0)
         if s > 0:
@@ -569,7 +595,7 @@ def build(T, topo, core, rank):
             full = grp([(o, T.Ib[:], T.Ph[:, 0:12], False), (o, T.I8k[:], pop, False)] +
                        [(o, T.LT[:, m], T.EQ[:, :, m], False) for m in range(1, 16)] +
                        [(T.uC[:, 301:312], T.G8k[:, sl(m)], T.dupb[:, 16 + m:L:16], False) for m in range(16)])
-            later.append((full, o, zp(s), zt, zsend, s))
+            later.append((full, o, zq, zt, zsend, s))
         if last:
             writes(*later.pop())
         Hs = si(2)
@@ -585,7 +611,7 @@ def build(T, topo, core, rank):
         ac(T.Lf[:], T.mP[:, 0:L], F.Relu, ["mPg"], ["Lf"], px=["mP"])
         if not last:
             ts(T.bad1[:], T.y[:], 32 * H1, None, A.is_le, None, ["y"], ["bad1"], 0.5)
-            mm(grp([(T.mP[:, 0:L], T.Ib[:], T.P4r[:], False), (T.mP[:, 0:L], T.nIb[:], T.Lf[:], False)]), ["Ib", "nIb", "P4r", "Lf"], ["mPg"], ["mP"])
+            mm(grp([(T.mP[:, 0:L], T.nIb[:], T.P4r[:], False), (T.mP[:, 0:L], T.nIb[:], T.Lf[:], False)]), ["Ib", "nIb", "P4r", "Lf"], ["mPg"], ["mP"])
             ac(T.NR[:], T.mP[:, 0:L], F.Relu, ["mPg"], ["NR"], px=["mP"])
             least_return(T.NR, "NR")
             ts(sm(10), Hs, 31 * H1, 33 * H1, A.max, A.min, ["Hs"], ["de"])
@@ -601,20 +627,20 @@ def build(T, topo, core, rank):
             tt(T.SK[:, 1 - s % 2, 12:12 + n], SK[:, 0:n], T.Dm[:, 0:n], A.add, [Ft, St, "Dm"], [Sn])
 
     step[0] = RO
-    dma("sp", T.yv[:], T.V[:, 0:W], 1 << 20, ["V"], ())
-    dma("sp", T.yz[:], zp(RO), 49152, ["zp%d" % RO], ())
+    dma("sp", T.yv[:], T.Vb[:, 0:W], 1 << 20, ["Vb"], ())
+    dma("sp", T.yz[:], zp(1), 1 << 20, ["zp%d" % RO], ())
     gt(T.tr[:, 0:L], T.Lf[:], T.INV[:], None, None, ["Lf", "INV"], ["tr0"])
     add("dve", lambda g: g.vector.transpose(T.src4[:, 0], T.tr[:, 0:L]), vcost(L, 1), ["tr0"], ["s40"])
     mm(swap3(lambda rho: T.dA[:, 96 * rho:96 * rho + 96], lambda ga: T.src4[:, 0, :, ga, :]), ["IW0", "IW1", "s40"], ["dA0"], ["dA0"])
     for rho in range(2):
         ac(T.ol[:, :, rho, :], T.dA[:, 96 * rho:96 * rho + 96], F.Copy, ["dA0"], ["ol%d" % rho], px=["dA0"])
-    dma("act", T.yl[:], T.ol[:], 49152, ["ol0", "ol1"], ())
+    dma("act", T.yl[:], T.ol[:], 1 << 20, ["ol0", "ol1"], ())
     ts(sm(0), si(2), -1.0 / H1, 32.0, A.mult, A.add, ["Hs"], ["sm0"])
     tt(sm(1), sm(0), T.popb[:, 0:12], A.mult, ["sm0", "pop"], ["sm1"])
     gt(T.t192[:], sm(1), T.EL[:], T.DM[:], A.mult, ["sm1", "EL", "DM"], ["t192"])
     mm(grp([(T.dB[0:8, 0:L], T.B8[:], T.t192[:], True)]), ["B8", "t192"], ["dB0"], ["dB0"])
     ts(T.k37[0:8, :], T.dB[0:8, 0:L], -1.0, None, A.add, None, ["dB0"], ["k37"], px=["dB0"])
-    dma("sp", T.yp[:], T.k37[0:8, :], 6144, ["k37"], ())
+    dma("sp", T.yp[:], T.k37[0:8, :], 1 << 20, ["k37"], ())
     return ops, 2 * (RO - 1) * sum(neng)
 
 
@@ -684,15 +710,20 @@ def kinds(ops):
             nm = nm.rstrip("0123456789")
         k = (o["step"], o["eng"], nm)
         seen[k] = seen.get(k, 0) + 1
-        out.append((0 <= o["step"] < RO, o["step"] >= RO, o["eng"], nm, seen[k]))
+        out.append((1 if 0 < o["step"] < RO - 1 else o["step"], o["eng"], nm, seen[k]))
     return out
 
 
 def refine(al, place, period, lo, hi, rounds, heat, free):
     ops, kd = al[0], kinds(al[0])
     ids = [i for i, o in enumerate(ops) if lo <= o["step"] <= hi]
+    whole = lo < 0 or hi >= RO
+    if not whole:
+        f = [i for i in ids if ops[i]["name"] == "fin"]
+        ids = list(range(f[0], f[-1] + 1))
     at = {i: k for k, i in enumerate(ids)}
-    n, whole = len(ids), lo < 0 or hi >= RO
+    n = len(ids)
+    en = ["dve", "act", "pe", "pool", "sp"]
     cl, eng = [kd[i] for i in ids], [ops[i]["eng"] for i in ids]
     base = [max(ops[i]["step"], 0) * period for i in ids]
     pre = [[at[d] for d in sorted(set(ops[i]["deps"]) | set(ops[i]["soft"])) if d in at] for i in ids]
@@ -702,6 +733,7 @@ def refine(al, place, period, lo, hi, rounds, heat, free):
         sets.append(([a[i]["cost"] for i in ids], [a[i]["lat"] for i in ids],
                      [[(d, a[ids[d]]["lat"] + (0.0 if eng[k] == "pe" == eng[d] else m["HOP"])) for d in pre[k]] for k in range(n)]))
     fins = [k for k in range(n) if ops[ids[k]]["name"] == "fin"]
+    ei = [en.index(e) for e in eng]
 
     def score(place):
         key = [base[k] + place[cl[k]] for k in range(n)]
@@ -714,15 +746,19 @@ def refine(al, place, period, lo, hi, rounds, heat, free):
         order = sorted(range(n), key=lambda k: key[k])
         tot, info = 0.0, []
         for (cost, lat, pr), m in zip(sets, SETS):
-            freeat, lastop, end, why = {}, {}, [0.0] * n, [-1] * n
+            freeat, lastop, end, why = [0.0] * 5, [-1] * 5, [0.0] * n, [-1] * n
             for k in order:
-                e = eng[k]
-                t, w = freeat.get(e, 0.0), lastop.get(e, -1)
+                e = ei[k]
+                t = freeat[e]
+                w = lastop[e]
                 for d, h in pr[k]:
-                    if end[d] + h > t:
-                        t, w = end[d] + h, -2 - d
+                    x = end[d] + h
+                    if x > t:
+                        t = x
+                        w = -2 - d
                 end[k] = freeat[e] = t + cost[k]
-                why[k], lastop[e] = w, k
+                why[k] = w
+                lastop[e] = k
             tail = max(range(n), key=lambda k: end[k] + lat[k]) if whole else fins[-1]
             tot += m["WT"] * (end[tail] + lat[tail] if whole else (end[tail] - end[fins[0]]) / (len(fins) - 1))
             info.append((why, tail))
@@ -759,6 +795,21 @@ def refine(al, place, period, lo, hi, rounds, heat, free):
             continue
         new = dict(place)
         new[c] = v
+        if rnd() < PAR["PULL"]:
+            new[c] = place[c]
+            v = pick((-1, 1)) * pick((200, 600, 1500)) * rnd()
+            for x in set(cl):
+                if x[1] == c[1] and x[2].rstrip("0123456789") == c[2].rstrip("0123456789") and free(x):
+                    new[x] = place[x] + v
+        elif rnd() < PAR["PULL"]:
+            i = pick(range(n))
+            todo = [(i, cur[2][i] - pick((200, 600, 1500)) * rnd())]
+            new[c] = place[c]
+            while todo:
+                i, v = todo.pop()
+                if cur[2][i] > v and free(cl[i]) and new[cl[i]] > v - base[i]:
+                    new[cl[i]] = v - base[i]
+                    todo += [(d, v - sets[0][0][d] - h) for d, h in sets[0][2][i]]
         sc = score(new)
         if sc[0] <= cur[0] or rnd() < math.exp((cur[0] - sc[0]) / (heat * (1 - it / rounds) + 1)):
             place, cur = new, sc
@@ -769,21 +820,51 @@ def refine(al, place, period, lo, hi, rounds, heat, free):
 
 def plan(al):
     ops, kd = al[0], kinds(al[0])
-    _o, start, _e = schedule(ops)
-    f = [start[i] for i, o in enumerate(ops) if o["name"] == "fin"]
-    period, place = f[5] - f[4], {}
-    for i, o in enumerate(ops):
-        if o["step"] in (-1, 5, RO):
-            place[kd[i]] = start[i] - {-1: f[0] - period, 5: f[4], RO: f[RO - 1]}[o["step"]]
-    for i, o in enumerate(ops):
-        place.setdefault(kd[i], start[i] - f[o["step"] - 1])
-    inner = set(kd[i] for i, o in enumerate(ops) if o["step"] == 5)
-    place = refine(al, place, period, 4, 6, PAR["R1"], PAR["HEAT"], lambda c: True)[0]
-    place = refine(al, place, period, -1, 1, PAR["R2"], PAR["HEAT"], lambda c: c not in inner)[0]
-    place = refine(al, place, period, RO - 1, RO, PAR["R2"], PAR["HEAT"], lambda c: c not in inner)[0]
+    period, place = 17000.0, {}
+    last = max(i for i, o in enumerate(ops) if o["name"] == "fin")
+    for e, text in PLAN.items():
+        for x in text.split():
+            nm, v = x.split(":")
+            nm, k = (nm.split(".") + ["1"])[:2]
+            place[(1, e, nm.strip("-"), int(k))] = 10.0 * int(v)
+    inner = set(place)
+    need, way = [1e12] * len(ops), [0.0] * len(ops)
+    for i in range(len(ops) - 1, -1, -1):
+        o = ops[i]
+        late = need[i] - max(o["step"], 0) * period - o["cost"] - o["lat"] - PAR["HOP"]
+        if o["step"] in (0, RO - 1):
+            place[kd[i]] = place.get((1,) + kd[i][1:], late)
+        if o["step"] < 0:
+            place[kd[i]] = i - 1e6 if o["eng"] == "pool" else late
+        way[i] += o["cost"] + o["lat"]
+        if i > last:
+            place[kd[i]] = (RO - o["step"]) * period + 20000.0 - way[i]
+        for d in set(o["deps"]) | set(o["soft"]):
+            need[d] = min(need[d], max(o["step"], 0) * period + place[kd[i]])
+            way[d] = max(way[d], way[i] + PAR["HOP"])
+    for j, i in enumerate(i for i, o in enumerate(ops) if o["step"] < 0 and o["eng"] == "act" and o["name"][0] == "V"):
+        place[kd[i]] = period + 1500.0 * j
+    place = refine(al, place, period, -1, 2, PAR["R2"], PAR["HEAT"], lambda c: c not in inner)[0]
+    place = refine(al, place, period, RO - 2, RO, PAR["R2"], PAR["HEAT"], lambda c: c not in inner)[0]
     return refine(al, place, period, -1, RO, 0, 1.0, None)[1]
 
 
+PLAN = {
+    "dve": "nu0:44 nu1:67 t30:93 sh0:116 t31:133 xi0:146 sh1:179 xi1:228 Y12:270 Y14:305 Y13:347 Y10:383 Y11:418 sof:453 Y15:460 so:495 S10:503 S13:531 "
+           "zk10:559 zk13:588 zk4:651 zk0:661 zk2:681 ru1:720 vown:728 uf1:744 zk5:787 zk9:806 ru0:816 zk7:823 uf0:843 ru1.2:867 tp1:875 brow1:894 h1:914 "
+           "tp0:923 ru2:941 K11:948 vi1:956 h0:964 uf2:973 Ph:996 vi0:1003 E10:1015 tp2:1192 h2:1224 K10:1231 K12:1238 vi2:1247 AE10:1289 E3:1345 E8:1409 "
+           "key1:1472 fb:1480 R0:1503 key1.2:1510 P8:1518 key0:1542 key1.3:1549 key0.2:1565 Pb:1573 key0.3:1592 R2:1599 R1:1615 key2:1624 key2.2:1647 "
+           "key2.3:1670 fin:1693 pop:1716 U:1723 slt:1730 popf:1737 zs3:1762 zo:1802 xa1:1809 EQ0:1825 EQ6:1855 EQ2:1862 EQ1:1871 EQ3:1893 EQ9:1901 "
+           "EQ5:1908 EQ8:1915 EQ4:1923 EQ7:1943 EQ10:1950 Hs:1957 EQ11:1964 de:2042 y:2317 sp:2401 so_:2412 e:2437 OP:2453 F:2551 bad1:2558 Dl:2603 "
+           "Dm:2679 St:2910 bad2:2955",
+    "act": "Y2:169 Y0:235 Y4:318 Y5:355 Y7:420 S0:485 S4:523 S2:542 Y9:580 V:616 S5:694 S9:732 S7:751 sqo:788 sq1:795 D1:803 D0:810 V.2:818 sq0:895 V.3:922 "
+           "cap:999 P0:1006 dp1:1033 E2:1040 E0:1077 sq2:1149 fk:1156 brow2:1163 brow0:1171 zp:1178 AE2:1197 AE0:1230 E7:1270 z:1307 E5:1326 AE7:1391 "
+           "AE3:1424 AE5:1468 AE8:1506 flip:1543 xa0:1757 zm:1825 dupb:2001 Lf:2604 NR:2715 so_:2843 Es:2918",
+    "pe": "uCg:49 uAg:55 uBg:162 acc1:286 acc:333 dB0:382 dA0:401 dA1:438 uCg.2:476 dB1:482 dA0.2:538 uBu:632 dA1.2:687 uAu:716 uBg.2:767 uCu:858 uAg.2:907 "
+          "uAr:975 uCg.3:1024 uCr:1086 dB1.2:1135 dB0.2:1177 uBg.3:1214 uBf:1217 mPg:1273 uCg.4:1322 uBp:1325 dA1.3:1339 uBf.2:1361 dA0.3:1416 uAg.3:1453 "
+          "uAp:1456 uAf:1477 uCp:1527 uCf:1559 mPg.2:1738 dup:1896 dup.2:1945 dup.3:1973 mPg.3:2527 mPg.4:2658 mPg.5:2775 mPg.6:2866",
+    "pool": "-:518 -.2:1213",
+}
 ORDER = []
 
 

import math
from concourse.bass import DstId, RemoteDMATransfer
from concourse.mybir import AluOpType as A, AxisListType, ActivationFunctionType as F

L, W, RO = 192, 4096, 10
CFG = {
    "pieces": [(0, "R", [(2, "A"), (2, "A"), (1, "A")], [(2, "A"), (1, "A"), (2, "B")]),
               (10, "F", [(3, "D"), (3, "D")], [(6, "D")]),
               (5, "R", [(2, "A"), (2, "A"), (1, "A")], [(2, "A"), (1, "A"), (2, "B")])],
    "xs": [(0, 64), (64, 192)],
    "xa": True, "rua": (), "sca": "AAA",
    "zact": "phf",
}
f32, bf, f16, i32, u16 = "float32", "bfloat16", "float16", "int32", "uint16"
XO = 16
FLIP, HIST = 16, 17
PW = 96


def _sb(n, d):
    return ("sbuf", [128] + (list(n) if isinstance(n, tuple) else [n]), d)


SCRATCH = {
    "X": _sb(XO + W + 32, bf), "V": _sb(W + L, f32), "Vb": _sb(W + L, bf), "ZW": _sb(27 * L, bf), "zp": _sb(4 * L, bf), "zq": _sb(RO * L, f32), "zm": _sb(L, bf),
    "Y": _sb(3072, bf), "S": _sb(3072, bf), "Sh": _sb(3072, f16), "E": _sb(3072, bf), "AE": _sb(3072, bf),
    "nmi": _sb((6, 2, 16), i32), "cai": _sb((6, 2, 16), bf), "rti": _sb((6, 2, 16), bf), "wti": _sb(1, i32), "thi": _sb(1, i32),
    "src4": _sb((4, 6, 2, 16), f32), "tr": _sb(4 * L, f32),
    "nB": _sb(L, f32), "ca1": _sb(L, f32), "rtB": _sb(L, f32), "thh": _sb(L, f16), "CA": _sb(L, f32),
    "P4r": _sb(L, bf), "P4c": _sb(L, bf), "NR": _sb(L, bf), "Lf": _sb(L, bf), "Es": _sb(16, f32),
    "y": _sb(L, bf), "sp": _sb(L, bf), "so_": _sb(L, bf), "OP": _sb(L, bf),
    "k37": _sb(L, f32), "kk": _sb(L, f32), "t192": _sb(L, f32), "i192": _sb(L, i32), "j192": _sb(L, i32),
    "one": _sb(160, f32), "IW": _sb(160, f32), "IW0": _sb(160, f32), "IW1": _sb(160, f32),
    "Ib": _sb(128, bf), "nIb": _sb(128, bf), "pIb": _sb(128, bf), "NI": _sb(128, bf), "n16": _sb(128, bf), "Ph": _sb(16, f16), "I8k": _sb(128, bf),
    "BO": _sb(128, f32), "BOb": _sb(128, bf), "WB": _sb(128, f16), "B8": _sb(8, f32),
    "G": _sb(144, bf), "Gn": _sb(144, bf), "Gh": _sb(144, bf), "GB2": _sb(144, bf), "GBn": _sb(144, bf), "G8k": _sb(144, bf),
    "Wh": _sb(144, f16), "LT": _sb((16, 128), bf), "RT": _sb((16, 128), bf),
    "CI": _sb((2, PW), bf), "ones": _sb(128, bf), "N64": _sb(PW, bf),
    "DM": _sb(L, f32), "pi": _sb(1, i32), "pj": _sb(1, i32), "PM": _sb(1, f32), "hf": _sb(2, f32), "wf": _sb(4, f32), "wi": _sb(2, i32),
    "thf": _sb(1, f32), "CF": _sb(1, f32),
    "c16": _sb(12, f32), "c1": _sb(12, f32), "LL": _sb(12, f32), "DUM": _sb(12, f32), "LLd": _sb(12, f32), "KQ": _sb(12, i32), "QF": _sb(12, f32), "t12": _sb(12, f32),
    "QL": _sb(12, u16), "DL": _sb(6, u16), "EL": _sb(12, u16), "PERM": _sb(12, u16), "INV": _sb(12, u16),
    "U": _sb(16 * (RO + 1), i32), "xi": _sb(L, u16), "nu": _sb(L, f32), "t3": _sb(L, i32), "sh": _sb(L, i32),
    "ru": _sb(3 * PW, f32), "uf": _sb(3 * PW, f32), "sq": _sb(3 * PW, f32), "tp": _sb(3 * PW, i32), "h": _sb(3 * PW, i32), "vi": _sb(L, u16),
    "K1": _sb(L, f32), "key": _sb(3 * 112, f32), "brow": _sb(L, bf), "bad1": _sb(L, bf), "bad2": _sb(L, bf), "fin": _sb(12, i32),
    "SK": _sb((2, 96), f32), "Dl": _sb(64, f32), "Dm": _sb(64, f32), "D": _sb(24, f32), "e": _sb(12, f32),
    "sm": _sb(16 * 12, f32), "si": _sb(16 * 3, i32), "popb": _sb(16, bf), "xa": _sb(2, f32), "zo": _sb(12, u16),
    "P8": _sb(16, f32), "Pb": _sb(L, f16), "EQ": _sb((12, 208), bf), "dupb": _sb(L, bf),
    "so": _sb(16 * RO, u16), "rz": _sb(2 * RO * L, f32), "ro": _sb(2 * RO * 16, u16),
    "ol": _sb((6, 2, 16), bf),
    "dA": ("psum", [128, 1024], f32), "dB": ("psum", [128, 1024], f32),
    "uA": ("psum", [128, 512], f32), "uB": ("psum", [128, 512], f32), "uC": ("psum", [128, 512], f32), "mP": ("psum", [128, 512], f32),
}
NDMA = 16
SEMAPHORES = ["dve", "act", "pe", "pool", "sent"] + ["d%d" % i for i in range(NDMA)] + ["r%d_%d" % (s, j) for s in range(1, RO) for j in range(2)]

SETS = [{"FIX": 10.0, "RC": 700.0, "RL": 1500.0, "CY": 0.91, "PC": 0.46, "GA": 1.56, "SC": 3.8, "HOP": 150.0, "WT": 1.0},
        {"FIX": 10.0, "RC": 1000.0, "RL": 2500.0, "CY": 1.2, "PC": 0.6, "GA": 1.9, "SC": 5.0, "HOP": 150.0, "WT": 0.6},
        {"FIX": 10.0, "RC": 1000.0, "RL": 2000.0, "CY": 0.95, "PC": 0.48, "GA": 1.2, "SC": 2.5, "HOP": 220.0, "WT": 0.8}]
PAR = dict(SETS[0], LOOK=300.0, SLACK=40.0, ROUNDS=3, R2=20000, HEAT=100.0, PULL=0.1)


def build(T, topo, core, rank):
    ops, lastw, readers, bank, step = [], {}, {}, {}, [-1]
    FIX, RL, CY, PC, GA, SC = (PAR[k] for k in ("FIX", "RL", "CY", "PC", "GA", "SC"))

    def add(eng, fn, cost, r=(), w=(), px=(), lat=0.0, ext=(), soft=(), dma=False):
        i = len(ops)
        deps = set()
        for t in r:
            if t in lastw:
                deps.add(lastw[t])
        for t in w:
            if t in lastw:
                deps.add(lastw[t])
            deps.update(readers.get(t, ()))
        for t in r:
            readers.setdefault(t, []).append(i)
        for t in w:
            lastw[t] = i
            readers[t] = []
        for b in px:
            who, cur, prev = bank.get(b, (None, [], []))
            if who != eng:
                prev, cur = cur, []
            deps.update(prev)
            bank[b] = (eng, cur + [i], prev)
        deps.discard(i)
        if eng in ("dve", "act"):
            cost += FIX
        ops.append(dict(eng=eng, fn=fn, cost=cost, deps=deps, lat=lat, ext=list(ext), soft=list(soft), dma=dma, step=step[0], name=(list(w) + [""])[0]))
        return i

    def n_of(ap):
        n = 1
        for x in ap.shape[1:]:
            n *= x
        return n

    def vcost(n, c):
        return max(64, n * c) * CY

    def ts(out, in0, s1, s2, o0, o1, r, w, c=1.0, px=()):
        if s2 is None:
            fn = lambda g: g.vector.tensor_scalar(out, in0, s1, None, o0)
        else:
            fn = lambda g: g.vector.tensor_scalar(out, in0, s1, s2, o0, o1)
        return add("dve", fn, vcost(n_of(out), c), r, w, px)

    def tt(out, a, b, o, r, w, px=()):
        return add("dve", lambda g: g.vector.tensor_tensor(out, a, b, o), vcost(n_of(out), 1.0 if px else 2.0), r, w, px)

    def cp(out, a, r, w, c=1.0, px=()):
        return add("dve", lambda g: g.vector.tensor_copy(out, a), vcost(n_of(out), c), r, w, px)

    def gt(out, win, off, b, o, r, w):
        if b is None:
            fn = lambda g: g.vector.tensor_copy(out, win.indirect(off))
        else:
            fn = lambda g: g.vector.tensor_tensor(out, win.indirect(off), b, o)
        return add("dve", fn, (50 / 0.83 + n_of(out) * GA) * CY, r, w)

    def ag(out, win, off, r, w, bias=None):
        if bias is None:
            fn = lambda g: g.scalar.activation(out, win.indirect(off), F.Copy)
        else:
            fn = lambda g: g.scalar.activation(out, win.indirect(off), F.Identity, bias=bias)
        return add("act", fn, (65 / 0.83 + n_of(out) * GA) * CY, r, w)

    def ms(ap, val, w):
        return add("dve", lambda g: g.vector.memset(ap, val), vcost(n_of(ap), 0.5), (), w)

    def ac(out, a, func, r, w, bias=0.0, scale=1.0, px=()):
        return add("act", lambda g: g.scalar.activation(out, a, func, bias=bias, scale=scale), max(64, n_of(out)) * CY, r, w, px)

    def lin(on_act, out, a, mul, c, r, w):
        if on_act:
            return ac(out, a, F.Identity, r, w, bias=c, scale=mul)
        return ts(out, a, mul, c, A.mult, A.add, r, w, 0.5)

    def mm(lst, r, w, px):
        def fn(g):
            for (o, a, b, st, sp, sl) in lst:
                x = g.tensor.matmul(o, a, b, st, sp)
            return x
        return add("pe", fn, sum(max(64, n_of(x[2])) * (4 if x[5] else 1) for x in lst) * PC, r, w, px)

    def grp(items):
        return [(o, a, b, i == 0, i == len(items) - 1, sl) for i, (o, a, b, sl) in enumerate(items)]

    def more(items, stop=False):
        return [(x[0], x[1], x[2], False, stop and i == len(items) - 1, False) for i, x in enumerate(items)]

    def dma(q, out, a, nbytes, r, w):
        fn = (lambda g: g.sync.dma_start(out, a)) if q == "sp" else (lambda g: g.scalar.dma_start(out, a))
        return add(q, fn, 60.0, r, w, lat=2000.0 + nbytes / 200.0, dma=True)

    def io(out, pat, base, cm, w, fl=True):
        if fl:
            fn = lambda g: g.iota(out, pat, base, cm, allow_small_or_imprecise_dtypes=True)
        else:
            fn = lambda g: g.iota(out, pat, base, cm)
        return add("pool", fn, 130 + 2 * n_of(out) * CY, (), w)

    def af(out, a, pat, op, base, cm, r, w):
        return add("pool", lambda g: g.affine_select(out, a, pat, op, 0.0, base, cm), 170 + 2 * n_of(out) * CY, r, w)

    def sl(m):
        return slice(15 - m, 143 - m)

    def zs(k):
        return T.ZW[:, k * L:(k + 1) * L]

    def zp(k):
        return T.zp[:, k * L:(k + 1) * L]

    def sm(i):
        return T.sm[:, 16 * i:16 * i + 12]

    def si(i):
        return T.si[:, 16 * i:16 * i + 12]

    UB = [(T.uA, "uA"), (T.uB, "uB"), (T.uC, "uC")]
    DB = [(T.dA, ("dA0", "dA1")), (T.dB, ("dB0", "dB1"))]
    PCS = [(b0, sum(n for n, _ in xu), xm, xu, vu) for (b0, xm, xu, vu) in CFG["pieces"]]
    M23, M28, M35 = 1.5 * 2.0 ** 23, 1.5 * 2.0 ** 28, 1.5 * 2.0 ** 35
    BIG, H1, S1 = 2.0 ** 24, 2.0 ** 18, 2.0 ** 13
    W0 = 12 * PCS[0][1]

    dma("act", T.nmi[:], T.nm[:], 98304, (), ["nmi"])
    dma("sp", zp(0), T.z0[:], 49152, (), ["zp0"])
    dma("sp", T.wti[:], T.wt[:], 512, (), ["wti"])
    dma("act", T.cai[:], T.ca[:], 49152, (), ["cai"])
    dma("sp", T.rti[:], T.rt[:], 49152, (), ["rti"])
    dma("act", T.thi[:], T.th[:], 512, (), ["thi"])
    dma("sp", T.X[:, XO:XO + W], T.xt[:], 1 << 20, (), ["X0"])
    dma("act", T.X[:, XO + W:], T.xt[:, 0:32], 1 << 20, (), ["X1"])
    dma("sp", T.Vb[:, 0:W], T.vt[:], 2 << 20, (), ["Vb"])

    io(T.pi[:], [[0, 1]], 0, 1, ["pi"], fl=False)
    ms(T.one[:], 1.0, ["one"])
    af(T.IW[:], T.one[:], [[-1, 160]], A.is_equal, 16, 1, ["one"], ["IW"])
    af(T.B8[:], T.one[:, 0:8], [[-16, 8]], A.is_ge, 0, 1, ["one"], ["B8"])
    af(T.B8[:], T.B8[:], [[16, 8]], A.is_ge, 15, -1, ["B8"], ["B8"])
    io(T.c1[:], [[1, 12]], 0, 0, ["c1"])
    io(T.c16[:], [[16, 12]], 0, 0, ["c16"])
    io(T.k37[:], [[37, 16], [0, 12]], 0, 0, ["k37"])
    io(T.kk[:], [[8192, 16], [0, 12]], (63 << 18) + 2048, 0, ["kk"])
    io(T.DM[:], [[0, 12], [1, 16]], 0, 0, ["DM"])
    ts(T.pj[:], T.pi[:], 15, None, A.bitwise_and, None, ["pi"], ["pj"])
    cp(T.PM[:], T.pj[:], ["pj"], ["PM"])
    ts(T.pj[:], T.pi[:], 4, 1, A.arith_shift_right, A.bitwise_and, ["pi"], ["pj"])
    cp(T.hf[:, 1:2], T.pj[:], ["pj"], ["hf1"])
    ts(T.hf[:, 0:1], T.hf[:, 1:2], -1.0, 1.0, A.mult, A.add, ["hf1"], ["hf0"])
    ts(T.IW0[:], T.IW[:], T.hf[:, 0:1], None, A.mult, None, ["IW", "hf0"], ["IW0"])
    ts(T.IW1[:], T.IW[:], T.hf[:, 1:2], None, A.mult, None, ["IW", "hf1"], ["IW1"])
    ms(T.G[:], 0.0, ["G"])
    cp(T.G[:, 15:143:16], T.B8[:], ["B8"], ["G"])
    af(T.BO[:], T.one[:, 0:128], [[-16, 8], [0, 16]], A.is_ge, 0, 1, ["one"], ["BO"])
    af(T.BO[:], T.BO[:], [[16, 8], [0, 16]], A.is_ge, 15, -1, ["BO"], ["BO"])
    ts(T.wf[:, 0:1], T.wti[:], 2048.0, -4096.0, A.is_ge, A.mult, ["wti"], ["wf0"])
    tt(T.wf[:, 1:2], T.wf[:, 0:1], T.wti[:], A.add, ["wf0", "wti"], ["wf1"])
    ts(T.Wh[:], T.G[:], T.wf[:, 1:2], None, A.mult, None, ["G", "wf1"], ["Wh"], 0.5)
    ts(T.WB[:], T.BO[:], T.wf[:, 1:2], None, A.mult, None, ["BO", "wf1"], ["WB"])
    mm(grp([(T.uA[:, 0:12], T.Wh[:, sl(m)], T.zp[:, m:L:16], False) for m in range(16)]), ["Wh", "zp0"], ["uAg"], ["uA"])
    cp(si(0), T.uA[:, 0:12], ["uAg"], ["si0"], px=["uA"])
    ts(T.U[:, 0:12], si(0), 4095, None, A.bitwise_and, None, ["si0"], ["U0"])
    ts(T.zm[:], zp(0), -64.0, None, A.add, None, ["zp0"], ["zm"], 0.5)
    ts(T.LL[:], T.c16[:], T.PM[:], None, A.add, None, ["c16", "PM"], ["LL"])
    ts(T.KQ[:], T.LL[:], -5.5, 1.0 / 12, A.add, A.mult, ["LL"], ["KQ"])
    ts(T.t12[:], T.KQ[:], -12.0, None, A.mult, None, ["KQ"], ["t12"])
    tt(T.QF[:], T.t12[:], T.LL[:], A.add, ["t12", "LL"], ["QF"])
    cp(T.QL[:], T.QF[:], ["QF"], ["QL"])
    ts(T.t12[:], T.QF[:], 16.0, None, A.mult, None, ["QF"], ["t12"])
    tt(T.t12[:], T.t12[:], T.KQ[:], A.add, ["t12", "KQ"], ["t12"])
    cp(T.PERM[:], T.t12[:], ["t12"], ["PERM"])
    IWS = [T.IW0, T.IW1]

    def swap3(dst3, src4):
        out = []
        for rho in range(2):
            out += grp([(dst3(rho), IWS[rho][:, 16 - 16 * (ga - rho):144 - 16 * (ga - rho)], src4(ga), True) for ga in range(2)])
        return out

    srcs = [(T.nmi, "nmi", T.nB, "nB"), (T.cai, "cai", T.ca1, "ca1"), (T.rti, "rti", T.rtB, "rtB"), (None, "thf", T.thh, "thh")]
    ts(T.thf[:], T.thi[:], 0.5, None, A.add, None, ["thi"], ["thf"])
    for a, (s, sn, d, dn) in enumerate(srcs):
        s4 = T.src4[:, a]
        if a == 0:
            cp(s4, s[:], [sn], ["s4%d" % a])
        elif a == 1:
            ac(s4, s[:], F.Identity, [sn], ["s4%d" % a], bias=1.0)
        elif a == 2:
            ac(s4, s[:], F.Identity, [sn], ["s4%d" % a], bias=1.0)
        else:
            ac(s4, T.cai[:], F.Identity, [sn, "cai"], ["s4%d" % a], bias=T.thf[:], scale=0.0)
        P, bk = DB[a // 2]
        c0 = 512 * (a % 2)
        b1 = [bk[a % 2]]
        lst = swap3(lambda rho: P[:, c0 + 96 * rho:c0 + 96 * rho + 96], lambda ga: T.src4[:, a, :, ga, :])
        mm(lst, ["IW0", "IW1", "s4%d" % a], b1, b1)
        for rho in range(2):
            ac(T.src4[:, a, :, rho, :], P[:, c0 + 96 * rho:c0 + 96 * rho + 96], F.Copy, b1, ["s4%d" % a], px=b1)
        add("dve", lambda g, a=a: g.vector.transpose(T.tr[:, a * L:(a + 1) * L], T.src4[:, a]), vcost(L, 1), ["s4%d" % a], ["tr%d" % a])
        gt(d[:], T.tr[:, a * L:(a + 1) * L], T.PERM[:], None, None, ["tr%d" % a, "PERM"], [dn])
        if a == 0:
            tt(T.i192[:], T.nB[:], T.k37[:], A.add, ["nB", "k37"], ["i192"])
            ts(T.j192[:], T.i192[:], 4095, None, A.bitwise_and, None, ["i192"], ["j192"])
            ts(T.uB[:, 320:512], T.j192[:], 32.0, -131072.0, A.mult, A.add, ["j192"], ["C32"], px=["uB"])
    cp(T.Ib[:], T.IW[:, 16:144], ["IW"], ["Ib"])
    ts(T.nIb[:], T.IW[:, 16:144], -1.0, None, A.mult, None, ["IW"], ["nIb"])
    ts(T.Gn[:], T.G[:], -1.0, None, A.mult, None, ["G"], ["Gn"], 0.5)
    ts(T.Gh[:], T.G[:], 0.5, None, A.mult, None, ["G"], ["Gh"], 0.5)
    ts(sm(0), T.LL[:], float(W0), 12.0, A.is_ge, A.mult, ["LL"], ["sm0"])
    tt(sm(1), sm(0), T.QF[:], A.add, ["sm0", "QF"], ["sm1"])
    cp(T.DL[:], T.sm[:, 16:22], ["sm1"], ["DL"])
    ms(T.sq[:], 0.0, ["sq0", "sq1", "sq2", "sqo"])
    ac(T.t192[:], T.ca1[:], F.Identity, ["ca1"], ["t192"], bias=H1, scale=-H1)
    for t, (b0, nb, xm, xu, vu) in enumerate(PCS):
        bs = slice(12 * b0, 12 * (b0 + nb))
        tt(UB[t][0][:, 36 * nb:48 * nb], T.t192[:, bs], T.kk[:, bs], A.add, ["t192", "kk"], ["KS%d" % t], px=[UB[t][1]])
    ac(T.CA[:], T.ca1[:], F.Identity, ["ca1"], ["CA"], scale=H1)
    ac(T.P4r[:], T.rtB[:], F.Silu, ["rtB"], ["P4r"], scale=-2.5)
    ac(T.P4c[:], T.ca1[:], F.Silu, ["ca1"], ["P4c"], scale=-2.5)
    ac(T.pIb[:], T.IW[:, 16:144], F.Copy, ["IW"], ["pIb"], scale=-4096.0 * BIG)
    ac(T.NI[:], T.IW[:, 16:144], F.Copy, ["IW"], ["NI"], scale=-2 * BIG)
    ac(T.n16[:], T.IW[:, 16:144], F.Copy, ["IW"], ["n16"], scale=-16.0)
    ac(T.I8k[:], T.IW[:, 16:144], F.Copy, ["IW"], ["I8k"], scale=-8192.0)
    ac(T.GB2[:], T.G[:], F.Copy, ["G"], ["GB2"], scale=4 * BIG)
    ac(T.GBn[:], T.G[:], F.Copy, ["G"], ["GBn"], scale=-2 * BIG)
    ac(T.G8k[:], T.G[:], F.Copy, ["G"], ["G8k"], scale=8192.0)
    ac(T.BOb[:], T.BO[:], F.Copy, ["BO"], ["BOb"])
    ms(T.X[:, 0:XO], 0.0, ["Xpad"])
    ms(T.V[:, W:W + L], 64.0, ["Vpad"])
    ms(T.Vb[:, W:W + L], 0.0, ["Vbpad"])
    VQ = ["V%d" % c for c in range(0, W, 512)]
    for c in range(0, W, 512):
        ac(T.V[:, c:c + 512], T.Vb[:, c:c + 512], F.Identity, ["Vb"], ["V%d" % c], bias=64.0)
    ms(T.e[:], 0.0, ["e"])
    ms(T.SK[:], 0.0, ["F0", "F1", "St0", "St1"])
    ms(T.Dl[:], 0.0, ["Dl"])
    ms(T.Lf[:], 0.0, ["Lf"])
    ms(T.popb[:, 12:13], -15.75 / 128, ["popc"])
    ms(T.ones[:], 1.0, ["ones"])
    ms(T.N64[:], -64.0, ["N64"])
    ms(T.CI[:, 0], -2048.0, ["CI0"])
    ms(T.CI[:, 1], -15.0 / 64, ["CI1"])
    ts(T.DM[:], T.DM[:], T.PM[:], None, A.is_equal, None, ["DM", "PM"], ["DM"])
    io(T.RT[:], [[0, 2048]], 1, 0, ["RT"])
    af(T.RT[:], T.RT[:], [[-1, 16], [-16, 8], [0, 16]], A.is_equal, 0, 1, ["RT"], ["RT"])
    io(T.LT[:], [[0, 2048]], 8192, 0, ["LT"])
    af(T.LT[:], T.LT[:], [[-1, 16], [0, 8], [1, 16]], A.is_equal, 0, 0, ["LT"], ["LT"])
    af(T.LT[:], T.LT[:], [[0, 16], [-16, 8], [0, 16]], A.is_ge, 0, 1, ["LT"], ["LT"])
    af(T.LT[:], T.LT[:], [[1, 16], [16, 8], [0, 16]], A.is_gt, 0, -1, ["LT"], ["LT"])
    cp(T.EL[:], T.c1[:], ["c1"], ["EL"])
    ts(T.LLd[:], T.LL[:], 1.0 / L, None, A.mult, None, ["LL"], ["LLd"])
    ts(T.DUM[:], T.LL[:], W - 10240.0, None, A.add, None, ["LL"], ["DUM"])
    ts(T.t12[:, 0:1], T.PM[:], 12.0, None, A.mult, None, ["PM"], ["t12"])
    ts(T.INV[:], T.c1[:], T.t12[:, 0:1], None, A.add, None, ["c1", "t12"], ["INV"])
    cp(T.wf[:, 2:3], T.wti[:], ["wti"], ["wf2"])
    mm(grp([(T.mP[:, 400:401], T.BO[:], T.wf[:, 2:3], True)]), ["BO", "wf2"], ["mPg"], ["mP"])
    ts(T.wi[:, 0:1], T.mP[:, 400:401], 63.0, None, A.mult, None, ["mPg"], ["wi0"], px=["mP"])
    ts(T.wi[:, 1:2], T.wi[:, 0:1], 4095, None, A.bitwise_and, None, ["wi0"], ["wi1"])
    ts(T.CF[:], T.wi[:, 1:2], 32 * H1 + FLIP * S1 + 4096 + 592, None, A.add, None, ["wi1"], ["CF"])

    N = len(T.cores)
    peers = [T.cores[(rank + d) % N] for d in (1, 3)]
    halves = []
    for j, p in enumerate(peers):
        en = topo.engines(core, p)
        h = len(en) // 2
        halves.append(sum(1 << x for x in en[j * h:(j + 1) * h]))
    neng = [bin(x).count("1") for x in halves]

    def send(src, dst, s):
        def fn(g):
            trs = []
            for j, p in enumerate(peers):
                rid, pid, _se = topo.addr(p)
                trs.append(RemoteDMATransfer(dst_ids=[DstId(rid=rid, pnc=pid)], dma_engine_mask=halves[j],
                                             remote_sem=T.sem["r%d_%d" % (s, j)], src=src, dst=dst(j)))
            g.remote_dma_fused(trs, local_sem=T.sem.sent)
            return None
        return fn

    dn, later = [0], []

    def cuts(c0, n):
        out = []
        while n > 0:
            k = min(n, L - c0 % L)
            out.append((c0, k))
            c0, n = c0 + k, n - k
        return out

    def units(b0, lst):
        out = []
        for n, x in lst:
            out.append((b0, n, x))
            b0 += n
        return out

    def tk(name, b0, nb):
        return ["%s%d" % (name, x) for x in range(b0, b0 + nb)]

    def tile(un):
        k = (un + 511) // 512
        if k == 2:
            dn[0] += dn[0] % 2
        b = dn[0] % 4
        dn[0] += k
        P, names = DB[b // 2]
        return P, 512 * (b % 2), list(names[b % 2:b % 2 + k])

    def sums(o, Gm, B, c0, n):
        return [(o, Gm[:, sl(m)], B[:, c0 + m:c0 + n:16], False) for m in range(16)]

    def least_return(src, tok):
        sign = T.Ib if tok == "P4r" else T.nIb
        mm(grp([(T.mP[:, 432:480], sign[:], src[:, 48 * k:48 * k + 48], False) for k in range(4)]), ["Ib", "nIb", tok], ["mPg"], ["mP"])
        ac(T.so_[:, 0:48], T.mP[:, 432:480], F.Copy, ["mPg"], ["so_"], px=["mP"])
        mm(grp([(T.mP[:, 420:432], T.Ib[:], T.so_[:, 12 * k:12 * k + 12], False) for k in range(4)]), ["Ib", "so_"], ["mPg"], ["mP"])
        ac(T.Es[:, 0:12], T.mP[:, 420:432], F.Copy, ["mPg"], ["Es"], px=["mP"])
        gt(T.bad2[:], T.Es[:, 0:12], T.QL[:], T.P4c[:], A.is_lt, ["Es", "QL", "P4c"], ["bad2"])

    def landing(s, j):
        return zp(2 + j) if s == RO - 1 else T.rz[:, (2 * s + j) * L:(2 * s + j + 1) * L]

    def writes(full, o, z, zt, zsend, s):
        mm(full[:2], ["Ib", "I8k", "Ph", "pop"], ["uCg"], ["uC"])
        mm(full[2:17], ["EQ%d" % q for q in range(12)] + ["LT", "uCg"], ["acc1"], ["uC"])
        mm(full[17:], ["G8k", "dupb", "uCg", "acc1"], ["acc"], ["uC"])
        tt(sm(4), o, T.DUM[:], A.min, ["acc", "DUM", "uCg"], ["sof"], px=["uC"])
        so = T.so[:, 16 * s:16 * s + 12]
        ts(so, sm(4), 10240.0, None, A.add, None, ["sof"], ["so%d" % s])
        osend = add("pool", send(so, lambda j, s=s: T.ro[:, (2 * s + j) * 16:(2 * s + j) * 16 + 12], s), PAR["RC"], ["so%d" % s], (), lat=RL)
        sc = (50 / 0.83 + L * SC) * CY

        def scatter(who, off, src, r, **kw):
            if s == RO - 1:
                add("dve", lambda g: g.vector.tensor_copy(T.Vb[:].indirect(off), src), sc, r, ["Vb", "Vbpad"] + VQ, **kw)
            elif who == "A":
                add("act", lambda g: g.scalar.activation(T.V[:].indirect(off), src, F.Silu), sc + 15, r, ["V", "Vpad"] + VQ, **kw)
            else:
                add("dve", lambda g: g.vector.tensor_copy(T.V[:].indirect(off), src), sc, r, ["V", "Vpad"] + VQ, **kw)

        if s == RO - 1:
            for c in range(0, W, 512):
                ac(T.Vb[:, c:c + 512], T.V[:, c:c + 512], F.Relu, ["V", "Vb"], ["V%d" % c], bias=-64.001)
        scatter(CFG["sca"][0], so, z, ["so%d" % s, zt])
        for j in range(2):
            scatter(CFG["sca"][1 + j], T.ro[:, 16 * (2 * s + j):16 * (2 * s + j) + 12], landing(s, j), (), ext=[("r%d_%d" % (s, j), 2 * neng[j])], soft=[zsend, osend])

    least_return(T.P4r, "P4r")
    for s in range(RO):
        Uc, ut = T.U[:, 16 * s:16 * s + 12], "U%d" % s
        zt = "zp%d" % s
        last = s == RO - 1
        step[0], dn[0] = s, 0
        for i, (a, b) in enumerate(CFG["xs"]):
            gt(T.nu[:, a:b], Uc, T.QL[:, a // 16:b // 16], T.nB[:, a:b], A.mult, [ut, "QL", "nB"], ["nu%d" % i])
            tt(T.t3[:, a:b], T.nu[:, a:b], T.uB[:, 320 + a:320 + b], A.add, ["C32", "nu%d" % i], ["t3%d" % i], px=["uB"])
            ts(T.sh[:, a:b], T.t3[:, a:b], 5, 4095, A.arith_shift_right, A.bitwise_and, ["t3%d" % i], ["sh%d" % i])
            if s == 0:
                ts(T.xi[:, a:b], T.sh[:, a:b], float(XO), None, A.add, None, ["sh%d" % i], ["xi%d" % i])
            else:
                ts(T.xi[:, a:b], T.sh[:, a:b], T.xa[:, 0:1], T.xa[:, 1:2], A.add, A.subtract, ["sh%d" % i, "xa0", "xa1"], ["xi%d" % i])

        def xit(b0, nb):
            return ["xi%d" % i for i, (a, b) in enumerate(CFG["xs"]) if a < 12 * (b0 + nb) and b > 12 * b0] + ["X0", "X1", "Xpad"]

        if later:
            writes(*later.pop())
        za = CFG["zact"]
        if s > 0:
            zq = zp(0) if last else T.zq[:, s * L:(s + 1) * L]
            ac(zq, T.zm[:], F.Identity, ["zm"], [zt] + ["zp0"] * last, bias=64.0 if last else 128.0)
            zsend = add("pool", send(zq, lambda j, s=s: landing(s, j), s), PAR["RC"], [zt], (), lat=RL)
        if not last:
            lin("h" in za, zs(HIST + s), T.zm[:], 1.0, 128.0, ["zm"], ["z%d" % s])
        lin("f" in za, zs(FLIP), T.zm[:], -1.0, 63.0, ["zm"], ["flip"])
        ac(T.D[:, 0:12], T.e[:], F.Identity, ["e"], ["D0"], bias=19616.0 * (1 - 32 * s) + 1336 * 32, scale=19616.0 / H1)
        ac(T.D[:, 12:24], T.e[:], F.Identity, ["e"], ["D1"], bias=19616.0 * (-32 * s) + 1336 * 32, scale=19616.0 / H1)
        ac(sm(2), T.e[:], F.Identity, ["e"], ["dp1"], bias=1.0 - 32 * s, scale=1.0 / H1)
        ts(sm(5), Uc, 592.0, None, A.add, None, [ut], ["vown"])
        ac(T.sq[:, W0:W0 + 12], sm(5), F.Square, ["vown"], ["sqo"])
        SK, Ft, St, Sn = T.SK[:, s % 2], "F%d" % (s % 2), "St%d" % (s % 2), "St%d" % (1 - s % 2)
        if s > 0:
            ac(sm(3), T.e[:], F.Identity, ["e"], ["cap"], bias=BIG * (1 + 32 * s), scale=-64.0)
            ac(sm(6), sm(5), F.Identity, ["vown", "CF"], ["fk"], bias=T.CF[:], scale=-1.0)
            tt(sm(7), SK[:, 12:24], sm(3), A.max, [St, "cap"], ["fb"])
            tt(T.key[:, 0:12], sm(7), sm(6), A.min, ["fb", "fk"], ["R0"])
        else:
            ac(T.key[:, 0:12], sm(5), F.Identity, ["vown", "CF"], ["R0"], bias=T.CF[:], scale=-1.0)
        if not last:
            ac(sm(8), sm(5), F.Identity, ["vown"], ["P0"], bias=(HIST + s) * S1 - 32 * H1 - 592)
        for t, (b0, nb, xm, xu, vu) in enumerate(PCS):
            c0, cn, w = L * b0, L * nb, 12 * nb
            bs = slice(12 * b0, 12 * b0 + w)
            Pu, ub = UB[t]
            gp = ub + "g"
            for (u0, un, mode) in units(b0, xu):
                cs = slice(L * u0, L * (u0 + un))
                off = T.xi[:, 12 * u0:12 * (u0 + un)]
                Yt, St_, zkt = tk("Y", u0, un), tk("S", u0, un), tk("zk", u0, un)
                if xm == "F":
                    for k in range(u0, u0 + un):
                        gt(T.Y[:, L * k:L * k + L], T.X[:], T.xi[:, 12 * k:12 * k + 12], T.zm[:], A.subtract, xit(k, 1) + ["zm"], ["Y%d" % k])
                    ts(T.Sh[:, cs], T.Y[:, cs], 64.0 - 1.0 / 32, 2.0, A.max, A.mult, Yt, St_, 0.5)
                    add("dve", lambda g, cs=cs: g.vector.tensor_tensor_scan(T.ZW[:, cs], T.Sh[:, cs], T.Y[:, cs], 0.0, A.max, A.subtract),
                        vcost(L * un, 0.5), Yt + St_, zkt)
                else:
                    if mode == "A":
                        ag(T.Y[:, cs], T.X[:], off, xit(u0, un), Yt)
                    else:
                        gt(T.Y[:, cs], T.X[:], off, None, None, xit(u0, un), Yt)
                    P, p0, px = tile(L * un)
                    lst, a1 = [], L * u0
                    for a0 in range(a1, a1 + L * un, 512):
                        n = min(512, a1 + L * un - a0)
                        lst += grp([(P[:, p0 + a0 - a1:p0 + a0 - a1 + n], T.Ib[:], T.Y[:, a0:a0 + n], False)] +
                                   [(P[:, p0 + a - a1:p0 + a - a1 + k], T.nIb[:], T.zm[:, a % L:a % L + k], False) for (a, k) in cuts(a0, n)])
                    mm(lst, ["Ib", "nIb", "zm"] + Yt, px, px)
                    ac(T.S[:, cs], P[:, p0:p0 + L * un], F.Abs, px, St_, bias=-63.75, px=px)
                    ts(T.ZW[:, cs], T.S[:, cs], M23, 64.0 - M23, A.add, A.add, St_, zkt, 0.5)
            St_, zkt = tk("S", b0, nb), tk("zk", b0, nb)
            pu, pr = Pu[:, 0:w], Pu[:, w:2 * w]
            ps = slice(PW * t, PW * t + w)
            wide = (w + (12 if t == 0 else 0) + 15) // 16 * 16
            pw = slice(PW * t, PW * t + wide)
            full = grp([(pu, T.Ib[:], T.CI[:, 0, 0:w], False), (pu, T.WB[:], T.N64[:, 0:w], False)] + sums(pu, T.Wh, T.ZW, c0, cn))
            mm(full[:2], ["Ib", "WB", "N64", "CI0"], [gp, ub + "u"], [ub])
            mm(full[2:], ["Wh", gp] + zkt, [ub + "u"], [ub])
            if t in CFG["rua"]:
                ac(T.ru[:, ps], pu, F.Identity, [ub + "u"], ["ru%d" % t], bias=M35, px=[ub])
                ac(T.ru[:, ps], T.ru[:, ps], F.Identity, ["ru%d" % t], ["ru%d" % t], bias=-M35)
            else:
                ts(T.ru[:, ps], pu, M35, -M35, A.add, A.add, [ub + "u"], ["ru%d" % t], px=[ub])
            tt(T.uf[:, ps], pu, T.ru[:, ps], A.subtract, [ub + "u", "ru%d" % t], ["uf%d" % t], px=[ub])
            ac(T.sq[:, ps], T.uf[:, ps], F.Square, ["uf%d" % t], ["sq%d" % t], bias=2048.0 + 592)
            gt(T.tp[:, pw], T.D[:], T.DL[:, 0:wide // 16] if t == 0 else T.QL[:, 0:wide // 16], T.sq[:, pw], A.add,
               ["D0", "D1", "DL", "QL", "sq%d" % t] + (["sqo"] if t == 0 else []), ["tp%d" % t])
            ts(T.h[:, pw], T.tp[:, pw], 5, 4095, A.arith_shift_right, A.bitwise_and, ["tp%d" % t], ["h%d" % t])
            cp(T.vi[:, bs], T.h[:, ps], ["h%d" % t], ["vi%d" % t])
            if xm == "R":
                full = grp(sums(pr, T.G, T.S, c0, cn) + sums(pr, T.Gn, T.ZW, c0, cn))
                mm(full[:16], ["G", ub + "u"] + St_, [gp, ub + "r"], [ub])
                mm(full[16:], ["Gn", gp] + zkt, [ub + "r"], [ub])
                ac(T.brow[:, bs], pr, F.Relu, [ub + "r"], ["brow%d" % t], bias=-4096.0, scale=-4.0, px=[ub])
            else:
                mm(grp([(pr, T.Ib[:], T.CI[:, 1, 0:w], False)] + sums(pr, T.Gh, T.Sh, c0, cn)), ["Ib", "CI1", "Gh", ub + "u"] + St_, [gp, ub + "r"], [ub])
                ts(T.ru[:, ps], pr, M23, -M23, A.add, A.add, [ub + "r"], ["ru%d" % t], px=[ub])
                tt(T.brow[:, bs], pr, T.ru[:, ps], A.is_gt, [ub + "r", "ru%d" % t], ["brow%d" % t], px=[ub])
            tt(T.K1[:, bs], Pu[:, 3 * w:4 * w], T.uf[:, ps], A.add, ["KS%d" % t, "uf%d" % t], ["K1%d" % t], px=[ub])
        if s > 0:
            ho = T.h[:, W0:W0 + 12]
            ts(T.P8[:, 0:12], ho, -2048.0, None, A.add, None, ["h0"], ["P8"])
            ts(T.Ph[:, 0:12], ho, -2048.0, None, A.add, None, ["h0"], ["Ph"])
            mm([(T.mP[:, m:192:16], T.RT[:, m], T.Ph[:, 0:12], True, True, False) for m in range(16)], ["RT", "Ph"], ["mPg"], ["mP"])
            cp(T.Pb[:], T.mP[:, 0:192], ["mPg"], ["Pb"], px=["mP"])
        for t, (b0, nb, xm, xu, vu) in enumerate(PCS):
            c0, cn, w = L * b0, L * nb, 12 * nb
            bs = slice(12 * b0, 12 * b0 + w)
            Vw, Vt, vo = (T.V[:, 0:W], ["V", "vi%d" % t], 0.0) if s > 1 else (T.Vb[:, 0:W], ["Vb", "vi%d" % t], 32.0)
            Pu, ub = UB[t]
            gp = ub + "g"
            o = Pu[:, 2 * w:3 * w]
            mm([(o, T.NI[:], T.thh[:, bs], True, False, False)], ["NI", "thh", ub + "r"], [gp, ub + "f"], [ub])
            pen = [(o, T.pIb[:], T.bad2[:, bs]), (o, T.pIb[:], T.brow[:, bs])]
            if s > 0:
                pen += [(o, T.pIb[:], T.bad1[:, bs]), (o, T.pIb[:], T.Lf[:, bs])]
            mm(more(pen), ["NI", "pIb", "thh", "bad1", "bad2", "Lf", "brow%d" % t, gp], [ub + "p"], [ub])
            for (u0, un, mode) in units(b0, vu):
                cs = slice(L * u0, L * (u0 + un))
                off = T.vi[:, 12 * u0:12 * (u0 + un)]
                zkt, Et, At = tk("zk", u0, un), tk("E", u0, un), tk("AE", u0, un)
                if mode in "BD":
                    gt(T.E[:, cs], Vw, off, T.ZW[:, cs], A.subtract, Vt + zkt, Et)
                    if mode == "B":
                        ac(T.AE[:, cs], T.E[:, cs], F.Abs, Et, At, bias=vo, scale=0.5)
                    else:
                        ts(T.AE[:, cs], T.E[:, cs], -2 * vo, vo, A.max, A.add, Et, At, 0.5)
                        p0 = 2 * w + 12 * (u0 - b0)
                        mm(more(sums(Pu[:, p0:p0 + 12 * un], T.GBn, T.E, L * u0, L * un)), ["GBn", gp] + Et, [ub + "f"], [ub])
                else:
                    ag(T.E[:, cs], Vw, off, Vt, Et)
                    P, p0, px = tile(L * un)
                    lst, a1 = [], L * u0
                    for a0 in range(0, L * un, 512):
                        n = min(512, L * un - a0)
                        lst += grp([(P[:, p0 + a0:p0 + a0 + n], T.nIb[:], T.ZW[:, a1 + a0:a1 + a0 + n], False),
                                    (P[:, p0 + a0:p0 + a0 + n], T.Ib[:], T.E[:, a1 + a0:a1 + a0 + n], False)])
                    mm(lst, ["Ib", "nIb"] + Et + zkt, px, px)
                    ac(T.AE[:, cs], P[:, p0:p0 + L * un], F.Abs, px, At, bias=vo, scale=0.5, px=px)
            mm(more(sums(o, T.GB2, T.AE, c0, cn), True), ["GB2", gp, ub + "p"] + tk("AE", b0, nb), [ub + "f"], [ub])
            k0, n, rt_ = 112 * t, nb + (1, 0, 2)[t], ["key%d" % t] + (["R0"], [], ["R1", "R2"])[t]
            tt(T.key[:, k0 + 12 * n - w:k0 + 12 * n], o, T.K1[:, bs], A.min, [ub + "f", gp, "K1%d" % t], ["key%d" % t], px=[ub])
            while n > 1:
                hh = n // 2
                if n > 2:
                    dst, wt_ = T.key[:, k0:k0 + 12 * hh], rt_
                elif t < 2:
                    dst, wt_ = T.key[:, 224 + 12 * t:236 + 12 * t], ["R%d" % (t + 1)]
                else:
                    dst, wt_ = T.fin[:], ["fin"]
                tt(dst, T.key[:, k0:k0 + 12 * hh], T.key[:, k0 + 12 * (n - hh):k0 + 12 * n], A.max, rt_, wt_)
                n -= hh
        pop = T.popb[:, 0:12]
        ts(pop, T.fin[:], 32 * H1, None, A.is_lt, None, ["fin"], ["pop"])
        if not last:
            ts(T.U[:, 16 * (s + 1):16 * (s + 1) + 12], T.fin[:], 4095, None, A.bitwise_and, None, ["fin"], ["U%d" % (s + 1)])
            mm(grp([(T.mP[:, 400:413], T.ones[:], T.popb[:, 0:13], False)]), ["ones", "pop", "popc"], ["mPg"], ["mP"])
            if CFG["xa"]:
                add("act", lambda g: g.scalar.activation(T.Es[:, 0:13], T.mP[:, 400:413], F.Copy, accum_out=T.xa[:, 0:1]), vcost(13, 1) + 20, ["mPg"], ["xa0", "Es"], ["mP"])
            else:
                add("dve", lambda g: g.vector.tensor_reduce(T.xa[:, 0:1], T.mP[:, 400:413], AxisListType.X, A.add), vcost(13, 1), ["mPg"], ["xa0"], ["mP"])
            ts(T.xa[:, 1:2], T.xa[:, 0:1], M28, -(M28 + 32), A.add, A.add, ["xa0"], ["xa1"])
        ts(si(1), T.fin[:], 13, 31, A.arith_shift_right, A.bitwise_and, ["fin"], ["slt"])
        tt(sm(9), si(1), T.LLd[:], A.add, ["slt", "LLd"], ["zs3"])
        ts(T.zo[:], sm(9), float(L), None, A.mult, None, ["zs3"], ["zo"])
        zr = ["zo", "flip"] + tk("zk", 0, 16) + ["z%d" % x for x in range(s)]
        if last:
            ag(zp(1), T.ZW[:, 0:(HIST + s) * L], T.zo[:], zr, ["zp%d" % RO], bias=-64.0)
        else:
            ag(T.zm[:], T.ZW[:, 0:(HIST + s) * L], T.zo[:], zr, ["zm"], bias=-128.0)
        if s > 0:
            ts(sm(11), T.fin[:], 32 * H1, None, A.is_lt, None, ["fin"], ["popf"])
            for q in range(12):
                ts(T.EQ[:, q, 0:L - 16 * q], T.Pb[:, 16 * q:L], T.P8[:, q:q + 1], T.sm[:, 176 + q:177 + q], A.is_equal, A.mult, ["Pb", "P8", "popf"], ["EQ%d" % q], 0.5)
            full = grp([(T.mP[:, 208 + 16 * q:384], T.BOb[:], T.EQ[:, q, 16:L - 16 * q], False) for q in range(11)])
            for a, b in ((0, 3), (3, 7), (7, 11)):
                mm(full[a:b], ["BOb"] + ["EQ%d" % q for q in range(a, b)] + ["mPg"] * (a > 0), ["dup"] + ["mPg"] * (a == 0), ["mP"])
            ac(T.dupb[:, 16:L], T.mP[:, 208:384], F.Copy, ["dup", "mPg"], ["dupb"], px=["mP"])
            o = T.uC[:, 300:312]
            full = grp([(o, T.Ib[:], T.Ph[:, 0:12], False), (o, T.I8k[:], pop, False)] +
                       [(o, T.LT[:, m], T.EQ[:, :, m], False) for m in range(1, 16)] +
                       [(T.uC[:, 301:312], T.G8k[:, sl(m)], T.dupb[:, 16 + m:L:16], False) for m in range(16)])
            later.append((full, o, zq, zt, zsend, s))
        if last:
            writes(*later.pop())
        Hs = si(2)
        ts(Hs, T.fin[:], 63 << 18, None, A.bitwise_and, None, ["fin"], ["Hs"])
        gt(T.y[:], Hs, T.QL[:], T.CA[:], A.add, ["Hs", "QL", "CA"], ["y"])
        ts(T.sp[:], T.y[:], 64 * H1, 16.0, A.is_equal, A.mult, ["y"], ["sp"], 0.5)
        gt(T.OP[:], sm(2), T.QL[:], T.sp[:], A.min, ["dp1", "QL", "sp"], ["OP"])
        lst = [(T.mP[:, 0:L], T.Ib[:], T.OP[:], False)]
        if s > 0:
            ts(T.so_[:], T.y[:], 32 * H1, None, A.is_equal, None, ["y"], ["so_"], 0.5)
            lst += [(T.mP[:, 0:L], T.Ib[:], T.Lf[:], False), (T.mP[:, 0:L], T.n16[:], T.so_[:], False)]
        mm(grp(lst), ["Ib", "n16", "OP", "Lf", "so_"], ["mPg"], ["mP"])
        ac(T.Lf[:], T.mP[:, 0:L], F.Relu, ["mPg"], ["Lf"], px=["mP"])
        if not last:
            ts(T.bad1[:], T.y[:], 32 * H1, None, A.is_le, None, ["y"], ["bad1"], 0.5)
            mm(grp([(T.mP[:, 0:L], T.nIb[:], T.P4r[:], False), (T.mP[:, 0:L], T.nIb[:], T.Lf[:], False)]), ["Ib", "nIb", "P4r", "Lf"], ["mPg"], ["mP"])
            ac(T.NR[:], T.mP[:, 0:L], F.Relu, ["mPg"], ["NR"], px=["mP"])
            least_return(T.NR, "NR")
            ts(sm(10), Hs, 31 * H1, 33 * H1, A.max, A.min, ["Hs"], ["de"])
            tt(T.e[:], T.e[:], sm(10), A.add, ["e", "de"], ["e"])
            n = 12 * min(s + 1, RO - 1 - s)
            tt(SK[:, 0:12], Hs, sm(8), A.add, ["Hs", "P0"], [Ft])
            tt(T.Dl[:, 0:n], SK[:, 24:24 + n], SK[:, 0:n], A.subtract, [Ft, St], ["Dl"])
            if n == 12:
                tt(T.Dm[:, 0:n], T.Dl[:, 0:n], pop, A.mult, ["Dl", "pop"], ["Dm"])
            else:
                k = (n + 15) // 16
                gt(T.Dm[:, 0:16 * k], pop, T.QL[:, 0:k], T.Dl[:, 0:16 * k], A.mult, ["Dl", "pop", "QL"], ["Dm"])
            tt(T.SK[:, 1 - s % 2, 12:12 + n], SK[:, 0:n], T.Dm[:, 0:n], A.add, [Ft, St, "Dm"], [Sn])

    step[0] = RO
    dma("sp", T.yv[:], T.Vb[:, 0:W], 1 << 20, ["Vb"], ())
    dma("sp", T.yz[:], zp(1), 1 << 20, ["zp%d" % RO], ())
    gt(T.tr[:, 0:L], T.Lf[:], T.INV[:], None, None, ["Lf", "INV"], ["tr0"])
    add("dve", lambda g: g.vector.transpose(T.src4[:, 0], T.tr[:, 0:L]), vcost(L, 1), ["tr0"], ["s40"])
    mm(swap3(lambda rho: T.dA[:, 96 * rho:96 * rho + 96], lambda ga: T.src4[:, 0, :, ga, :]), ["IW0", "IW1", "s40"], ["dA0"], ["dA0"])
    for rho in range(2):
        ac(T.ol[:, :, rho, :], T.dA[:, 96 * rho:96 * rho + 96], F.Copy, ["dA0"], ["ol%d" % rho], px=["dA0"])
    dma("act", T.yl[:], T.ol[:], 1 << 20, ["ol0", "ol1"], ())
    ts(sm(0), si(2), -1.0 / H1, 32.0, A.mult, A.add, ["Hs"], ["sm0"])
    tt(sm(1), sm(0), T.popb[:, 0:12], A.mult, ["sm0", "pop"], ["sm1"])
    gt(T.t192[:], sm(1), T.EL[:], T.DM[:], A.mult, ["sm1", "EL", "DM"], ["t192"])
    mm(grp([(T.dB[0:8, 0:L], T.B8[:], T.t192[:], True)]), ["B8", "t192"], ["dB0"], ["dB0"])
    ts(T.k37[0:8, :], T.dB[0:8, 0:L], -1.0, None, A.add, None, ["dB0"], ["k37"], px=["dB0"])
    dma("sp", T.yp[:], T.k37[0:8, :], 1 << 20, ["k37"], ())
    return ops, 2 * (RO - 1) * sum(neng)


def schedule(ops):
    n, HOP = len(ops), PAR["HOP"]
    pre = [sorted(set(o["deps"]) | set(o["soft"])) for o in ops]
    suc = [[] for _ in range(n)]
    for i in range(n):
        for d in pre[i]:
            suc[d].append(i)

    def hop(i, j):
        return ops[i]["lat"] + (0.0 if ops[i]["eng"] == "pe" == ops[j]["eng"] else HOP)

    def run(pre, suc, pr, back):
        left = [len(p) for p in pre]
        rdy, start, order, avail, free = [0.0] * n, [0.0] * n, [], {}, {}
        for i in range(n):
            if left[i] == 0:
                avail.setdefault(ops[i]["eng"], []).append(i)
        while len(order) < n:
            best = None
            for e, lst in avail.items():
                if lst:
                    t0 = max(free.get(e, 0.0), min(rdy[i] for i in lst))
                    i = max((i for i in lst if rdy[i] <= t0 + PAR["LOOK"]), key=lambda i: (pr[i], -i))
                    if rdy[i] > t0:
                        fill = [j for j in lst if max(t0, rdy[j]) + ops[j]["cost"] <= rdy[i] + PAR["SLACK"] and j != i and rdy[j] < rdy[i]]
                        if fill:
                            i = max(fill, key=lambda j: (pr[j], -j))
                    t = max(t0, rdy[i])
                    if best is None or t < best[0]:
                        best = (t, i, e)
            t, i, e = best
            avail[e].remove(i)
            order.append(i)
            start[i] = t
            free[e] = t + ops[i]["cost"]
            for j in suc[i]:
                rdy[j] = max(rdy[j], free[e] + (hop(j, i) if back else hop(i, j)))
                left[j] -= 1
                if left[j] == 0:
                    avail.setdefault(ops[j]["eng"], []).append(j)
        return order, start, max(start[i] + ops[i]["cost"] + (0.0 if back else ops[i]["lat"]) for i in range(n))

    pr = [0.0] * n
    for i in range(n - 1, -1, -1):
        pr[i] = ops[i]["cost"] + max([pr[j] + hop(i, j) for j in suc[i]] + [ops[i]["lat"]])
    best = None
    for _ in range(PAR["ROUNDS"]):
        for i in range(n):
            if ops[i]["dma"] and not pre[i]:
                pr[i] = 1e9 - i
        order, start, end = run(pre, suc, pr, False)
        if best is None or end < best[2]:
            best = (order, start, end)
        _o, rev, _e = run(suc, pre, [start[i] + ops[i]["cost"] for i in range(n)], True)
        pr = [rev[i] + ops[i]["cost"] for i in range(n)]
    return best


def kinds(ops):
    seen, out = {}, []
    for o in ops:
        nm = o["name"]
        if nm.rstrip("0123456789") in ("U", "zp", "z", "so", "F", "St"):
            nm = nm.rstrip("0123456789")
        k = (o["step"], o["eng"], nm)
        seen[k] = seen.get(k, 0) + 1
        out.append((1 if 0 < o["step"] < RO - 1 else o["step"], o["eng"], nm, seen[k]))
    return out


def refine(al, place, period, lo, hi, rounds, heat, free):
    ops, kd = al[0], kinds(al[0])
    ids = [i for i, o in enumerate(ops) if lo <= o["step"] <= hi]
    whole = lo < 0 or hi >= RO
    if not whole:
        f = [i for i in ids if ops[i]["name"] == "fin"]
        ids = list(range(f[0], f[-1] + 1))
    at = {i: k for k, i in enumerate(ids)}
    n = len(ids)
    en = ["dve", "act", "pe", "pool", "sp"]
    cl, eng = [kd[i] for i in ids], [ops[i]["eng"] for i in ids]
    base = [max(ops[i]["step"], 0) * period for i in ids]
    pre = [[at[d] for d in sorted(set(ops[i]["deps"]) | set(ops[i]["soft"])) if d in at] for i in ids]
    first = [k for k, i in enumerate(ids) if ops[i]["dma"] and not ops[i]["deps"]]
    sets = []
    for a, m in zip(al, SETS):
        sets.append(([a[i]["cost"] for i in ids], [a[i]["lat"] for i in ids],
                     [[(d, a[ids[d]]["lat"] + (0.0 if eng[k] == "pe" == eng[d] else m["HOP"])) for d in pre[k]] for k in range(n)]))
    fins = [k for k in range(n) if ops[ids[k]]["name"] == "fin"]
    ei = [en.index(e) for e in eng]

    def score(place):
        key = [base[k] + place[cl[k]] for k in range(n)]
        for k in first:
            key[k] = -1e9 + k
        for k in range(n):
            for d in pre[k]:
                if key[d] >= key[k]:
                    key[k] = key[d] + 1e-3
        order = sorted(range(n), key=lambda k: key[k])
        tot, info = 0.0, []
        for (cost, lat, pr), m in zip(sets, SETS):
            freeat, lastop, end, why = [0.0] * 5, [-1] * 5, [0.0] * n, [-1] * n
            for k in order:
                e = ei[k]
                t = freeat[e]
                w = lastop[e]
                for d, h in pr[k]:
                    x = end[d] + h
                    if x > t:
                        t = x
                        w = -2 - d
                end[k] = freeat[e] = t + cost[k]
                why[k] = w
                lastop[e] = k
            tail = max(range(n), key=lambda k: end[k] + lat[k]) if whole else fins[-1]
            tot += m["WT"] * (end[tail] + lat[tail] if whole else (end[tail] - end[fins[0]]) / (len(fins) - 1))
            info.append((why, tail))
        return tot, info, key, order

    seed = [12345]

    def rnd():
        seed[0] = (seed[0] * 1103515245 + 12345) % 2147483648
        return seed[0] / 2147483648.0

    def pick(x):
        return x[int(rnd() * len(x))]

    cur = best = score(place)
    keep = place
    for it in range(rounds):
        why, k = pick(cur[1])
        arcs = []
        while why[k] != -1:
            if why[k] >= 0:
                arcs.append((why[k], k))
            k = why[k] if why[k] >= 0 else -2 - why[k]
        if arcs and rnd() < 0.7:
            j, i = pick(arcs)
            if rnd() < 0.5:
                c, v = cl[i], cur[2][j] - base[i] - pick((1, 1, 100, 400)) * rnd()
            else:
                c, v = cl[j], cur[2][i] - base[j] + pick((1, 100, 400, 1500)) * rnd()
        else:
            c = pick(cl)
            v = place[c] + pick((-1, 1)) * pick((50, 200, 800)) * rnd()
        if not free(c):
            continue
        new = dict(place)
        new[c] = v
        if rnd() < PAR["PULL"]:
            new[c] = place[c]
            v = pick((-1, 1)) * pick((200, 600, 1500)) * rnd()
            for x in set(cl):
                if x[1] == c[1] and x[2].rstrip("0123456789") == c[2].rstrip("0123456789") and free(x):
                    new[x] = place[x] + v
        elif rnd() < PAR["PULL"]:
            i = pick(range(n))
            todo = [(i, cur[2][i] - pick((200, 600, 1500)) * rnd())]
            new[c] = place[c]
            while todo:
                i, v = todo.pop()
                if cur[2][i] > v and free(cl[i]) and new[cl[i]] > v - base[i]:
                    new[cl[i]] = v - base[i]
                    todo += [(d, v - sets[0][0][d] - h) for d, h in sets[0][2][i]]
        sc = score(new)
        if sc[0] <= cur[0] or rnd() < math.exp((cur[0] - sc[0]) / (heat * (1 - it / rounds) + 1)):
            place, cur = new, sc
            if sc[0] < best[0]:
                best, keep = sc, new
    return keep, [ids[k] for k in best[3]], best[0]


def plan(al):
    ops, kd = al[0], kinds(al[0])
    period, place = 17000.0, {}
    last = max(i for i, o in enumerate(ops) if o["name"] == "fin")
    for e, text in PLAN.items():
        for x in text.split():
            nm, v = x.split(":")
            nm, k = (nm.split(".") + ["1"])[:2]
            place[(1, e, nm.strip("-"), int(k))] = 10.0 * int(v)
    inner = set(place)
    need, way = [1e12] * len(ops), [0.0] * len(ops)
    for i in range(len(ops) - 1, -1, -1):
        o = ops[i]
        late = need[i] - max(o["step"], 0) * period - o["cost"] - o["lat"] - PAR["HOP"]
        if o["step"] in (0, RO - 1):
            place[kd[i]] = place.get((1,) + kd[i][1:], late)
        if o["step"] < 0:
            place[kd[i]] = i - 1e6 if o["eng"] == "pool" else late
        way[i] += o["cost"] + o["lat"]
        if i > last:
            place[kd[i]] = (RO - o["step"]) * period + 20000.0 - way[i]
        for d in set(o["deps"]) | set(o["soft"]):
            need[d] = min(need[d], max(o["step"], 0) * period + place[kd[i]])
            way[d] = max(way[d], way[i] + PAR["HOP"])
    for j, i in enumerate(i for i, o in enumerate(ops) if o["step"] < 0 and o["eng"] == "act" and o["name"][0] == "V"):
        place[kd[i]] = period + 1500.0 * j
    place = refine(al, place, period, -1, 2, PAR["R2"], PAR["HEAT"], lambda c: c not in inner)[0]
    place = refine(al, place, period, RO - 2, RO, PAR["R2"], PAR["HEAT"], lambda c: c not in inner)[0]
    return refine(al, place, period, -1, RO, 0, 1.0, None)[1]


PLAN = {
    "dve": "nu0:44 nu1:67 t30:93 sh0:116 t31:133 xi0:146 sh1:179 xi1:228 Y12:270 Y14:305 Y13:347 Y10:383 Y11:418 sof:453 Y15:460 so:495 S10:503 S13:531 "
           "zk10:559 zk13:588 zk4:651 zk0:661 zk2:681 ru1:720 vown:728 uf1:744 zk5:787 zk9:806 ru0:816 zk7:823 uf0:843 ru1.2:867 tp1:875 brow1:894 h1:914 "
           "tp0:923 ru2:941 K11:948 vi1:956 h0:964 uf2:973 Ph:996 vi0:1003 E10:1015 tp2:1192 h2:1224 K10:1231 K12:1238 vi2:1247 AE10:1289 E3:1345 E8:1409 "
           "key1:1472 fb:1480 R0:1503 key1.2:1510 P8:1518 key0:1542 key1.3:1549 key0.2:1565 Pb:1573 key0.3:1592 R2:1599 R1:1615 key2:1624 key2.2:1647 "
           "key2.3:1670 fin:1693 pop:1716 U:1723 slt:1730 popf:1737 zs3:1762 zo:1802 xa1:1809 EQ0:1825 EQ6:1855 EQ2:1862 EQ1:1871 EQ3:1893 EQ9:1901 "
           "EQ5:1908 EQ8:1915 EQ4:1923 EQ7:1943 EQ10:1950 Hs:1957 EQ11:1964 de:2042 y:2317 sp:2401 so_:2412 e:2437 OP:2453 F:2551 bad1:2558 Dl:2603 "
           "Dm:2679 St:2910 bad2:2955",
    "act": "Y2:169 Y0:235 Y4:318 Y5:355 Y7:420 S0:485 S4:523 S2:542 Y9:580 V:616 S5:694 S9:732 S7:751 sqo:788 sq1:795 D1:803 D0:810 V.2:818 sq0:895 V.3:922 "
           "cap:999 P0:1006 dp1:1033 E2:1040 E0:1077 sq2:1149 fk:1156 brow2:1163 brow0:1171 zp:1178 AE2:1197 AE0:1230 E7:1270 z:1307 E5:1326 AE7:1391 "
           "AE3:1424 AE5:1468 AE8:1506 flip:1543 xa0:1757 zm:1825 dupb:2001 Lf:2604 NR:2715 so_:2843 Es:2918",
    "pe": "uCg:49 uAg:55 uBg:162 acc1:286 acc:333 dB0:382 dA0:401 dA1:438 uCg.2:476 dB1:482 dA0.2:538 uBu:632 dA1.2:687 uAu:716 uBg.2:767 uCu:858 uAg.2:907 "
          "uAr:975 uCg.3:1024 uCr:1086 dB1.2:1135 dB0.2:1177 uBg.3:1214 uBf:1217 mPg:1273 uCg.4:1322 uBp:1325 dA1.3:1339 uBf.2:1361 dA0.3:1416 uAg.3:1453 "
          "uAp:1456 uAf:1477 uCp:1527 uCf:1559 mPg.2:1738 dup:1896 dup.2:1945 dup.3:1973 mPg.3:2527 mPg.4:2658 mPg.5:2775 mPg.6:2866",
    "pool": "-:518 -.2:1213",
}
ORDER = []


def rank_program(g, core, T, topo):
    rank = T.rank_of(core)
    if rank is None:
        return
    if not ORDER:
        al = []
        for m in SETS[::-1]:
            PAR.update(m)
            al.insert(0, build(T, topo, core, rank)[0])
        ORDER.append(plan(al))
    ops, nsent = build(T, topo, core, rank)
    queue = {"dve": g.vector, "act": g.scalar, "pe": g.tensor, "pool": g, "sp": g.sync}
    known = {e: {} for e in queue}
    mark, count, nd = {}, {}, 0
    for i in ORDER[0]:
        o = ops[i]
        kn = known[o["eng"]]
        need = {}
        for d in o["deps"]:
            if mark[d] is not None and not (o["eng"] == "pe" == ops[d]["eng"]):
                need[mark[d][0]] = max(need.get(mark[d][0], (0, None)), (mark[d][1], d))
        for sem, (val, d) in sorted(need.items(), key=lambda x: -x[1][1]):
            if kn.get(sem, 0) < val:
                queue[o["eng"]].wait_ge(T.sem[sem], val)
                for a, b in mark[d][2].items():
                    kn[a] = max(kn.get(a, 0), b)
        for sem, val in o["ext"]:
            queue[o["eng"]].wait_ge(T.sem[sem], val)
        x = o["fn"](g)
        if x is None:
            mark[i] = None
            continue
        if o["dma"]:
            sem, inc = "d%d" % nd, 16
            nd += 1
        else:
            sem, inc = o["eng"], 1
        x.then_inc(T.sem[sem], inc)
        count[sem] = count.get(sem, 0) + inc
        clock = dict(kn)
        clock[sem] = count[sem]
        mark[i] = (sem, count[sem], clock)
    for sem, val in sorted(count.items()):
        g.wait_ge(T.sem[sem], val)
    g.wait_ge(T.sem.sent, nsent)
